import numpy as np
import ml_dtypes


def mxq(x, axis, fmt="e4m3"):
    dtype, down = {"e4m3": (ml_dtypes.float8_e4m3fn, 7), "e5m2": (ml_dtypes.float8_e5m2, 14)}[fmt]
    v = np.moveaxis(np.asarray(x, np.float32).astype(ml_dtypes.bfloat16).astype(np.float64), axis, -1)
    blocks = v.reshape(v.shape[:-1] + (-1, 32))
    amax = np.abs(blocks).max(-1, keepdims=True)
    byte = np.maximum(np.where(amax > 0, np.frexp(amax)[1] - 1 + 127, 0) - down, 1)
    scale = np.exp2(byte - 127.0)
    codes = (blocks / scale).astype(np.float32).astype(dtype).astype(np.float64)
    return np.moveaxis((codes * scale).reshape(v.shape), -1, axis)


WIDE = False


def mx_kscale(k):
    if not WIDE:
        return np.ones(k)
    levels = np.array([10, -10, 5, -5, 0])
    if k % 512:
        return np.exp2(np.random.permutation(np.resize(levels, k // 32))).repeat(32)
    a = np.empty((k // 512, 16))
    for p in range(k // 512):
        a[p, :8] = np.random.permutation(np.resize(levels, 8))
        for g in range(8):
            far = levels[np.abs(levels - a[p, g]) >= 10]
            a[p, g + 8] = far[np.random.randint(len(far))]
    return np.exp2(a.ravel()).repeat(32)


def f64(x):
    return np.asarray(x).astype(np.float64)


def striped(idx):
    return np.tile(idx.reshape(-1, 16).T, (8, 1)).astype(np.uint16)


def unstriped(offs):
    return offs[:16].T.reshape(-1).astype(np.int64)


E2M1 = np.array([0.0, 0.5, 1.0, 1.5, 2.0, 3.0, 4.0, 6.0, -0.0, -0.5, -1.0, -1.5, -2.0, -3.0, -4.0, -6.0])


def pack_weight(w, fmt):
    k, n = w.shape
    w = f64(np.asarray(w, np.float32).astype(ml_dtypes.bfloat16)).reshape(k // 32, 32, n)
    amax = np.abs(w).max(1)
    if fmt == "e4m3":
        byte = np.frexp(amax)[1] - 1 + 127 - 7
    else:
        mant, ex = np.frexp(amax / 6.0)
        byte = np.where(mant > 0.5, ex, ex - 1) + 127
    byte = np.clip(np.where(amax > 0, byte, 1), 1, 254)
    scaled = (w * np.exp2(127.0 - byte)[:, None, :]).reshape(k, n).astype(np.float32)
    by_word = np.ascontiguousarray(scaled.reshape(k // 512, 128, 4, n).transpose(0, 1, 3, 2))
    if fmt == "e4m3":
        words = by_word.astype(ml_dtypes.float8_e4m3fn).view(np.uint8)
    else:
        c = by_word.astype(ml_dtypes.float4_e2m1fn).view(np.uint8) & 0xF
        words = (c[..., 0::2] | (c[..., 1::2] << 4)).reshape(k // 512, 128, 2 * n)
    return np.ascontiguousarray(words), np.ascontiguousarray(byte.astype(np.uint8).reshape(k // 512, 16, n))


def unpack_weight(words, scales, fmt):
    g, _, n = scales.shape
    words = np.ascontiguousarray(words).reshape(g, 128, n, -1)
    if fmt == "e4m3":
        vals = words.view(ml_dtypes.float8_e4m3fn).astype(np.float64)
    else:
        nib = np.empty((g, 128, n, 4), np.uint8)
        nib[..., 0::2] = words & 0xF
        nib[..., 1::2] = words >> 4
        vals = E2M1[nib]
    vals = vals * np.repeat(np.exp2(scales.astype(np.float64) - 127.0), 8, axis=1)[..., None]
    return vals.transpose(0, 1, 3, 2).reshape(g * 512, n)


def gelu(v):
    return 0.5 * v * (1.0 + np.tanh(np.sqrt(2.0 / np.pi) * (v + 0.044715 * v**3)))


K, H, N, T, S = 1024, 512, 768, 4096, 1024

def setup_inputs():
    n = np.random.standard_normal
    s = mx_kscale(K)[:, None]
    u = mx_kscale(H)[:, None]
    tab_words, tab_scales = pack_weight(n((K, T)) * s, "e4m3")
    w2_words, w2_scales = pack_weight(n((H, H)) / np.sqrt(H) / u, "e2m1")
    return {
        "tab_words": tab_words, "tab_scales": tab_scales,
        "offs": striped(np.random.permutation(T)[:S]),
        "w1": (n((K, H)) / np.sqrt(K) / s).astype(np.float32),
        "w2_words": w2_words, "w2_scales": w2_scales,
        "step": (np.exp(0.3 * n(H)) * u[:, 0]).astype(np.float32),
        "w3": (n((H, N)) / np.sqrt(H) / u).astype(np.float32),
        "offs2": striped(np.random.permutation(S)),
        "wgo": np.exp(0.3 * n((128, S))).astype(np.float32),
        "x0": n((N, S)).astype(np.float32),
    }

def reference(tab_words, tab_scales, offs, w1, w2_words, w2_scales, step, w3, offs2, wgo, x0):
    v = unpack_weight(tab_words, tab_scales, "e4m3")[:, unstriped(offs)]
    w2 = unpack_weight(w2_words, w2_scales, "e2m1")
    d = f64(step)[:, None]
    a = mxq(f64(w1), 0, "e4m3").T @ v
    f1 = d * np.tanh(a)
    b = a + w2.T @ mxq(f1, 0, "e4m3")
    h = f1 + d * np.tanh(b)
    y = mxq(f64(w3), 0, "e4m3").T @ mxq(h, 0, "e4m3")
    page = np.zeros((N, S))
    page[:, unstriped(offs2)] = np.tile(f64(wgo), (N // 128, 1)) * y
    return page + f64(x0)

@@ -1,0 +1,371 @@
+from contextlib import ExitStack
+
+import concourse.mybir as mybir
+from concourse.masks import make_identity
+
+K, H, N, T, S = 1024, 512, 768, 4096, 1024
+FLOPS = 2 * S * (K * H + H * H + H * N)
+
+F32 = mybir.dt.float32
+BF16 = mybir.dt.bfloat16
+I32 = mybir.dt.int32
+U32 = mybir.dt.uint32
+U16 = mybir.dt.uint16
+U8 = mybir.dt.uint8
+FP8X4 = mybir.dt.float8_e4m3fn_x4
+FP4X4 = mybir.dt.float4_e2m1fn_x4
+ALU = mybir.AluOpType
+ACT = mybir.ActivationFunctionType
+
+P = 128
+PACK = 4
+BANK = 512
+CHUNKS = [(0, 128), (128, 128), (256, 256), (512, 256), (768, 256)]
+N_TILES = N // P
+W3_PIECE = 256
+
+
+def tile_list_core_age_slopes_kernel(tc, tab_words, tab_scales, offs, w1, w2_words, w2_scales, step, w3, offs2, wgo, x0, out):
+    nc = tc.nc
+    with ExitStack() as ctx:
+        keep = ctx.enter_context(tc.tile_pool(name="keep", bufs=1))
+        ring = ctx.enter_context(tc.tile_pool(name="ring", bufs=3))
+        psum = ctx.enter_context(tc.psum_pool(name="psum", bufs=1))
+
+        def held(shape, dtype, name):
+            return keep.tile(shape, dtype, name=name, tag=name, align_bytes=64)
+
+        def bank(tag, bufs):
+            return psum.tile([P, BANK], F32, name=tag, tag=tag, bufs=bufs)
+
+        picks = held([P, S // 16], U16, "picks")
+        places = held([P, S // 16], U16, "places")
+        steps = held([P, PACK], F32, "steps")
+        w2_raw = held([P, 2 * H], U8, "w2_raw")
+        w2_scale_raw = held([P, H], U8, "w2_scale_raw")
+        tab_scale = held([P, T], U8, "tab_scale")
+        tab = [held([P, T], I32, f"tab{a}") for a in range(2)]
+        w1_raw = [[held([P, PACK, H // 2], F32, f"w1_raw{a}_{i}") for i in range(2)] for a in range(2)]
+        w3_raw = [held([P, PACK, W3_PIECE], F32, f"w3_raw{i}") for i in range(N // W3_PIECE)]
+        gains = held([P, S], F32, "gains")
+        rows = [held([P, S], F32, f"rows{n}") for n in range(N_TILES)]
+        ident = held([P, P], F32, "ident")
+        warm = held([P, 2], F32, "warm")
+
+        nc.vector.memset(tab_scale[:].bitcast(I32), 0)
+        nc.vector.memset(w2_scale_raw[:].bitcast(I32), 0)
+        nc.gpsimd.memset(warm[:, 0:1], 0.0)
+        nc.scalar.activation(warm[:, 1:2], warm[:, 0:1], ACT.Tanh)
+
+        nc.sync.dma_start(picks[:], offs)
+        nc.sync.dma_start(places[:], offs2)
+        nc.sync.dma_start(steps[:], step.rearrange("(p t) -> p t", t=PACK))
+        nc.sync.dma_start(w2_raw[:].bitcast(I32), w2_words[0].bitcast(I32))
+        tab_rows = [tab_words[a].rearrange("p t i -> p (t i)").bitcast(I32) for a in range(2)]
+        w1_rows = [w1[a * 512 : (a + 1) * 512, :].rearrange("(p j) c -> p j c", j=PACK) for a in range(2)]
+        for i in range(4):
+            cols = slice(i * T // 4, (i + 1) * T // 4)
+            nc.sync.dma_start(tab[0][:, cols], tab_rows[0][:, cols])
+        for q in range(4):
+            nc.sync.dma_start(tab_scale[32 * q : 32 * q + 8, :].bitcast(I32), tab_scales[:, 4 * q : 4 * q + 4, :].bitcast(I32))
+        nc.sync.dma_start(tab[1][:], tab_rows[1])
+        for q in range(4):
+            nc.sync.dma_start(w2_scale_raw[32 * q : 32 * q + 4, :].bitcast(I32), w2_scales[0, 4 * q : 4 * q + 4, :].bitcast(I32))
+        for a in range(2):
+            for i in range(2):
+                nc.sync.dma_start(w1_raw[a][i][:], w1_rows[a][:, :, i * H // 2 : (i + 1) * H // 2])
+
+        def load_w3(i):
+            nc.sync.dma_start(w3_raw[i][:], w3[:, i * W3_PIECE : (i + 1) * W3_PIECE].rearrange("(p j) c -> p j c", j=PACK))
+
+        load_w3(0)
+        nc.sync.dma_start(gains[:], wgo)
+        load_w3(1)
+        load_w3(2)
+        for n in range(N_TILES):
+            nc.sync.dma_start(rows[n][:], x0[n * P : (n + 1) * P, :])
+        make_identity(nc, ident[:])
+
+        w2_codes = held([P, 2 * H], U8, "w2_codes")
+        w2_scale = held([P, H], U8, "w2_scale")
+        nc.vector.tensor_copy(
+            w2_codes[:].rearrange("p (t m b) -> p t m b", t=PACK, b=2),
+            w2_raw[:].rearrange("p (m t b) -> p t m b", t=PACK, b=2),
+        )
+
+        w1_codes = [held([P, H], U32, f"w1_codes{a}") for a in range(2)]
+        w1_scale = [held([P, H], U8, f"w1_scale{a}") for a in range(2)]
+        w1_grouped = [held([P, PACK * H], BF16, f"w1_grouped{a}") for a in range(2)]
+        v_scale = held([P, S], U8, "v_scale")
+        v_codes = [held([P, S], U32, f"v_codes{a}") for a in range(2)]
+
+        def cast_w1(engine_copy, a, raw, m0):
+            source = raw.rearrange("p j (m t) -> p m j t", t=PACK)
+            count = raw.shape[2] // PACK
+            engine_copy(w1_grouped[a][:].rearrange("p (t m j) -> p m j t", t=PACK, j=PACK)[:, m0 : m0 + count], source)
+
+        def quantize_w1(a):
+            nc.vector.quantize_mx(out=w1_codes[a][:].bitcast(FP8X4), scales=w1_scale[a][:], in_=w1_grouped[a][:])
+
+        nc.vector.tensor_copy(v_codes[0][:], tab[0][:].bitcast(U32).indirect(picks[:]))
+        nc.vector.tensor_copy(v_scale[:], tab_scale[:].indirect(picks[:]))
+        nc.vector.tensor_copy(v_codes[1][:], tab[1][:].bitcast(U32).indirect(picks[:]))
+        nc.vector.tensor_copy(
+            w2_scale[:].rearrange("p (t m) -> p t m", t=PACK),
+            w2_scale_raw[:].rearrange("p (m t) -> p t m", t=PACK),
+        )
+        for a in range(2):
+            cast_w1(nc.scalar.copy, a, w1_raw[a][0][:], 0)
+            cast_w1(nc.vector.tensor_copy, a, w1_raw[a][1][:], P // 2)
+            quantize_w1(a)
+
+        def interleave(engine_copy, grouped, planes):
+            engine_copy(
+                grouped.rearrange("p (c i t) -> p c t i", i=4, t=PACK),
+                planes.rearrange("p (t c i) -> p c t i", i=4, t=PACK),
+            )
+
+        w3_codes = [held([P, W3_PIECE], U32, f"w3_codes{i}") for i in range(N // W3_PIECE)]
+        w3_scale = [held([P, W3_PIECE], U8, f"w3_scale{i}") for i in range(N // W3_PIECE)]
+        w3_grouped = [held([P, PACK * W3_PIECE], BF16, f"w3_grouped{i}") for i in range(N // W3_PIECE)]
+
+        def cast_w3(i, engine_copy):
+            interleave(engine_copy, w3_grouped[i][:], w3_raw[i][:].rearrange("p j c -> p (j c)"))
+
+        def quantize_w3(i):
+            nc.vector.quantize_mx(out=w3_codes[i][:].bitcast(FP8X4), scales=w3_scale[i][:], in_=w3_grouped[i][:])
+
+        f1, arg, f1_grouped, f1_codes, f1_scale, h_grouped, h_codes, h_scale = ([] for i in range(8))
+        h_planes = {}
+        for c, (j0, w) in enumerate(CHUNKS):
+            f1.append(held([P, PACK * w], F32, f"f1_{c}"))
+            arg.append(held([P, PACK * w], F32, f"arg{c}"))
+            f1_grouped.append(held([P, PACK * w], BF16, f"f1_grouped{c}"))
+            f1_codes.append(held([P, w], U32, f"f1_codes{c}"))
+            f1_scale.append(held([P, w], U8, f"f1_scale{c}"))
+            h_grouped.append(held([P, PACK * w], BF16, f"h_grouped{c}"))
+            h_codes.append(held([P, w], U32, f"h_codes{c}"))
+            h_scale.append(held([P, w], U8, f"h_scale{c}"))
+        pages = [held([P, S], F32, f"page{n}") for n in range(N_TILES)]
+
+        def first_product(c, b):
+            j0, w = CHUNKS[c]
+            per_bank = BANK // w
+            cols = slice(j0, j0 + w)
+            acc = bank("a_bank", 3)
+            for a in range(2):
+                for u in range(per_bank):
+                    t = b * per_bank + u
+                    nc.tensor.matmul_mx(
+                        out=acc[:, u * w : (u + 1) * w],
+                        lhsT=w1_codes[a][:, t * P : (t + 1) * P].bitcast(FP8X4),
+                        lhsT_scale=w1_scale[a][:, t * P : (t + 1) * P],
+                        rhs=v_codes[a][:, cols].bitcast(FP8X4),
+                        rhs_scale=v_scale[4 * a : P, cols],
+                        start=(a == 0 and u == 0),
+                        stop=(a == 1 and u == per_bank - 1),
+                    )
+            return acc
+
+        def woven(ap, w):
+            return ap.rearrange("p (t j) -> p j t", t=PACK)
+
+        def by_column(ap):
+            return ap.rearrange("p (j t) -> p j t", t=PACK)
+
+        def step_rows(w):
+            return steps[:].unsqueeze(1).to_broadcast([P, w, PACK])
+
+        def short_first_slope(c):
+            w = CHUNKS[c][1]
+            acc = first_product(c, 0)
+            nc.scalar.activation(by_column(f1[c][:]), woven(acc[:], w), ACT.Tanh)
+            nc.vector.tensor_tensor(by_column(f1_grouped[c][:]), by_column(f1[c][:]), step_rows(w), ALU.mult)
+            nc.vector.quantize_mx(out=f1_codes[c][:].bitcast(FP8X4), scales=f1_scale[c][:], in_=f1_grouped[c][:])
+            nc.scalar.copy(by_column(arg[c][:]), woven(acc[:], w))
+
+        def short_second_slope(c):
+            w = CHUNKS[c][1]
+            nc.scalar.activation(arg[c][:], arg[c][:], ACT.Tanh)
+            nc.vector.tensor_tensor(arg[c][:], arg[c][:], f1[c][:], ALU.add)
+            nc.vector.tensor_tensor(by_column(h_grouped[c][:]), by_column(arg[c][:]), step_rows(w), ALU.mult)
+            nc.vector.quantize_mx(out=h_codes[c][:].bitcast(FP8X4), scales=h_scale[c][:], in_=h_grouped[c][:])
+
+        def first_slope(c, b):
+            w = CHUNKS[c][1]
+            per_bank = BANK // w
+            acc = first_product(c, b)
+            nc.scalar.activation(f1[c][:, b * BANK : (b + 1) * BANK], acc[:], ACT.Tanh)
+            for u in range(per_bank):
+                t = b * per_bank + u
+                plane = f1[c][:, t * w : (t + 1) * w]
+                nc.scalar.activation(plane, plane, ACT.Copy, scale=steps[:, t : t + 1])
+            return acc
+
+        def keep_argument(c, b, acc):
+            nc.scalar.copy(arg[c][:, b * BANK : (b + 1) * BANK], acc[:])
+
+        def quantize_f1(c):
+            interleave(nc.scalar.copy, f1_grouped[c][:], f1[c][:])
+            nc.vector.quantize_mx(out=f1_codes[c][:].bitcast(FP8X4), scales=f1_scale[c][:], in_=f1_grouped[c][:])
+
+        def second_argument(c, short=False):
+            j0, w = CHUNKS[c]
+            per_bank = BANK // w
+            for b in range(PACK // per_bank):
+                acc = bank("p_bank", 2)
+                span = slice(b * BANK, (b + 1) * BANK)
+                for u in range(per_bank):
+                    t = b * per_bank + u
+                    nc.tensor.matmul_mx(
+                        out=acc[:, u * w : (u + 1) * w],
+                        lhsT=w2_codes[:, 2 * t * P : 2 * (t + 1) * P].bitcast(FP4X4),
+                        lhsT_scale=w2_scale[:, t * P : (t + 1) * P],
+                        rhs=f1_codes[c][:].bitcast(FP8X4),
+                        rhs_scale=f1_scale[c][:],
+                        start=True,
+                        stop=True,
+                    )
+                if short:
+                    nc.vector.tensor_tensor(by_column(arg[c][:]), woven(acc[:], w), by_column(arg[c][:]), ALU.add)
+                else:
+                    nc.vector.tensor_tensor(arg[c][:, span], acc[:], arg[c][:, span], ALU.add)
+
+        def second_slope(c):
+            j0, w = CHUNKS[c]
+            h_planes[c] = held([P, PACK * w], BF16, f"h_planes{c}")
+            per_bank = BANK // w
+            for b in range(PACK // per_bank):
+                span = slice(b * BANK, (b + 1) * BANK)
+                nc.scalar.activation(arg[c][:, span], arg[c][:, span], ACT.Tanh)
+                for u in range(per_bank):
+                    t = b * per_bank + u
+                    plane = slice(t * w, (t + 1) * w)
+                    nc.vector.scalar_tensor_tensor(h_planes[c][:, plane], arg[c][:, plane], steps[:, t : t + 1], f1[c][:, plane], ALU.mult, ALU.add)
+
+        def quantize_h(c):
+            interleave(nc.scalar.copy, h_grouped[c][:], h_planes[c][:])
+            nc.vector.quantize_mx(out=h_codes[c][:].bitcast(FP8X4), scales=h_scale[c][:], in_=h_grouped[c][:])
+
+        def place(chunks, tiles, y_tag=None, in_p_bank=False):
+            j0 = CHUNKS[chunks[0]][0]
+            w = sum(CHUNKS[c][1] for c in chunks)
+            acc = bank("p_bank", 2) if in_p_bank else bank("y_bank", 3)
+            if y_tag is None:
+                y = ring.tile([P, BANK], F32, name="y")
+            else:
+                y = keep.tile([P, BANK], F32, name="y", tag=y_tag, align_bytes=64)
+            for u, n in enumerate(tiles):
+                i, n0 = divmod(n * P, W3_PIECE)
+                for c in chunks:
+                    first = u * w + CHUNKS[c][0] - j0
+                    nc.tensor.matmul_mx(
+                        out=acc[:, first : first + CHUNKS[c][1]],
+                        lhsT=w3_codes[i][:, n0 : n0 + P].bitcast(FP8X4),
+                        lhsT_scale=w3_scale[i][:, n0 : n0 + P],
+                        rhs=h_codes[c][:].bitcast(FP8X4),
+                        rhs_scale=h_scale[c][:],
+                        start=True,
+                        stop=True,
+                    )
+            nc.scalar.copy(y[:, 0 : len(tiles) * w], acc[:, 0 : len(tiles) * w])
+            for u, n in enumerate(tiles):
+                nc.vector.tensor_tensor(
+                    pages[n][:].indirect(places[:, j0 // 16 : (j0 + w) // 16]),
+                    y[:, u * w : (u + 1) * w],
+                    gains[:, j0 : j0 + w],
+                    ALU.mult,
+                )
+
+        def add_on_tensor(n):
+            blocks = BANK // P
+            for half in range(S // BANK):
+                turned_acc = bank("a_bank", 3)
+                turned = ring.tile([P, BANK], F32, name="turned", tag="turned", bufs=2)
+                for first, source in ((True, rows[n]), (False, pages[n])):
+                    for u in range(blocks):
+                        nc.tensor.matmul(
+                            turned_acc[:, u * P : (u + 1) * P],
+                            source[:, half * BANK + u * P : half * BANK + (u + 1) * P],
+                            ident[:],
+                            is_transpose=True,
+                            start=(first and u == 0),
+                            stop=(not first and u == blocks - 1),
+                        )
+                nc.scalar.copy(turned[:], turned_acc[:])
+                back_acc = bank("p_bank", 2)
+                for u in range(blocks):
+                    nc.tensor.transpose(back_acc[:, u * P : (u + 1) * P], turned[:, u * P : (u + 1) * P], ident[:])
+                cols = slice(half * BANK, (half + 1) * BANK)
+                nc.scalar.copy(rows[n][:, cols], back_acc[:])
+                nc.sync.dma_start(out[n * P : (n + 1) * P, cols], rows[n][:, cols])
+
+        def add_on_vector(n):
+            for half in range(S // BANK):
+                cols = slice(half * BANK, (half + 1) * BANK)
+                total = ring.tile([P, BANK], F32, name="total", tag="turned", bufs=2)
+                nc.vector.tensor_tensor(total[:], pages[n][:, cols], rows[n][:, cols], ALU.add)
+                nc.sync.dma_start(out[n * P : (n + 1) * P, cols], total[:])
+
+        short_first_slope(0)
+        second_argument(0, short=True)
+        cast_w3(0, nc.vector.tensor_copy)
+        short_first_slope(1)
+        short_second_slope(0)
+        quantize_w3(0)
+        second_argument(1, short=True)
+        cast_w3(1, nc.vector.tensor_copy)
+        quantize_w3(1)
+        acc20 = first_slope(2, 0)
+        place((0,), (0, 1,))
+        short_second_slope(1)
+        acc21 = first_slope(2, 1)
+        keep_argument(2, 0, acc20)
+        place((0,), (2, 3,))
+        cast_w3(2, nc.scalar.copy)
+        quantize_w3(2)
+        quantize_f1(2)
+        keep_argument(2, 1, acc21)
+        place((0,), (4, 5,))
+        second_argument(2)
+        place((1,), (0, 1,), y_tag="f1_grouped2")
+        acc30 = first_slope(3, 0)
+        second_slope(2)
+        place((1,), (2, 3,), in_p_bank=True)
+        quantize_h(2)
+        place((1,), (4, 5,), y_tag="arg2")
+        keep_argument(3, 0, acc30)
+        acc31 = first_slope(3, 1)
+        quantize_f1(3)
+        keep_argument(3, 1, acc31)
+        place((2,), (0,))
+        second_argument(3)
+        place((2,), (1,), y_tag="f1_grouped3")
+        acc40 = first_slope(4, 0)
+        second_slope(3)
+        place((2,), (2,), in_p_bank=True)
+        quantize_h(3)
+        place((2,), (3,), y_tag="arg3")
+        keep_argument(4, 0, acc40)
+        acc41 = first_slope(4, 1)
+        quantize_f1(4)
+        keep_argument(4, 1, acc41)
+        place((2,), (4,))
+        second_argument(4)
+        place((2,), (5,), y_tag="f1_grouped4")
+        second_slope(4)
+        place((3,), (0,), in_p_bank=True)
+        quantize_h(4)
+        place((3,), (1,), y_tag="arg4")
+        place((4,), (0,))
+        place((4,), (1,))
+        place((3, 4,), (2,))
+        place((3, 4,), (3,))
+        add_on_tensor(0)
+        add_on_tensor(1)
+        place((3, 4,), (4,), in_p_bank=True)
+        add_on_tensor(2)
+        place((3, 4,), (5,), in_p_bank=True)
+        add_on_tensor(3)
+        add_on_tensor(4)
+        add_on_vector(5)

@@ -45,8 +45,8 @@ def tile_list_core_age_slopes_kernel(tc, tab_words, tab_scales, offs, w1, w2_wor
         w2_scale_raw = held([P, H], U8, "w2_scale_raw")
         tab_scale = held([P, T], U8, "tab_scale")
         tab = [held([P, T], I32, f"tab{a}") for a in range(2)]
-        w1_raw = [[held([P, PACK, H // 2], F32, f"w1_raw{a}_{i}") for i in range(2)] for a in range(2)]
-        w3_raw = [held([P, PACK, W3_PIECE], F32, f"w3_raw{i}") for i in range(N // W3_PIECE)]
+        w1_raw = [held([P, PACK, H], F32, f"w1_raw{a}") for a in range(2)]
+        w3_raw = held([P, PACK, N], F32, "w3_raw")
         gains = held([P, S], F32, "gains")
         rows = [held([P, S], F32, f"rows{n}") for n in range(N_TILES)]
         ident = held([P, P], F32, "ident")
@@ -63,25 +63,17 @@ def tile_list_core_age_slopes_kernel(tc, tab_words, tab_scales, offs, w1, w2_wor
         nc.sync.dma_start(w2_raw[:].bitcast(I32), w2_words[0].bitcast(I32))
         tab_rows = [tab_words[a].rearrange("p t i -> p (t i)").bitcast(I32) for a in range(2)]
         w1_rows = [w1[a * 512 : (a + 1) * 512, :].rearrange("(p j) c -> p j c", j=PACK) for a in range(2)]
-        for i in range(4):
-            cols = slice(i * T // 4, (i + 1) * T // 4)
-            nc.sync.dma_start(tab[0][:, cols], tab_rows[0][:, cols])
+        for a in range(2):
+            for j in range(0, PACK, 2):
+                nc.sync.dma_start(w1_raw[a][:, j : j + 2, :], w1_rows[a][:, j : j + 2, :])
         for q in range(4):
             nc.sync.dma_start(tab_scale[32 * q : 32 * q + 8, :].bitcast(I32), tab_scales[:, 4 * q : 4 * q + 4, :].bitcast(I32))
-        nc.sync.dma_start(tab[1][:], tab_rows[1])
+        nc.sync.dma_start(tab[0][:], tab_rows[0])
         for q in range(4):
             nc.sync.dma_start(w2_scale_raw[32 * q : 32 * q + 4, :].bitcast(I32), w2_scales[0, 4 * q : 4 * q + 4, :].bitcast(I32))
-        for a in range(2):
-            for i in range(2):
-                nc.sync.dma_start(w1_raw[a][i][:], w1_rows[a][:, :, i * H // 2 : (i + 1) * H // 2])
-
-        def load_w3(i):
-            nc.sync.dma_start(w3_raw[i][:], w3[:, i * W3_PIECE : (i + 1) * W3_PIECE].rearrange("(p j) c -> p j c", j=PACK))
-
-        load_w3(0)
+        nc.sync.dma_start(tab[1][:], tab_rows[1])
+        nc.sync.dma_start(w3_raw[:], w3.rearrange("(p j) c -> p j c", j=PACK))
         nc.sync.dma_start(gains[:], wgo)
-        load_w3(1)
-        load_w3(2)
         for n in range(N_TILES):
             nc.sync.dma_start(rows[n][:], x0[n * P : (n + 1) * P, :])
         make_identity(nc, ident[:])
@@ -97,32 +89,35 @@ def tile_list_core_age_slopes_kernel(tc, tab_words, tab_scales, offs, w1, w2_wor
         w1_scale = [held([P, H], U8, f"w1_scale{a}") for a in range(2)]
         w1_grouped = [held([P, PACK * H], BF16, f"w1_grouped{a}") for a in range(2)]
         v_scale = held([P, S], U8, "v_scale")
-        v_codes = [held([P, S], U32, f"v_codes{a}") for a in range(2)]
+        v_codes0 = held([P, S], U32, "v_codes0")
+        v_codes1 = [held([P, S // 2], U32, f"v_codes1_{i}") for i in range(2)]
 
-        def cast_w1(engine_copy, a, raw, m0):
-            source = raw.rearrange("p j (m t) -> p m j t", t=PACK)
-            count = raw.shape[2] // PACK
-            engine_copy(w1_grouped[a][:].rearrange("p (t m j) -> p m j t", t=PACK, j=PACK)[:, m0 : m0 + count], source)
+        def cast_w1(a):
+            nc.vector.tensor_copy(
+                w1_grouped[a][:].rearrange("p (t m j) -> p m j t", t=PACK, j=PACK),
+                w1_raw[a][:].rearrange("p j (m t) -> p m j t", t=PACK),
+            )
 
         def quantize_w1(a):
             nc.vector.quantize_mx(out=w1_codes[a][:].bitcast(FP8X4), scales=w1_scale[a][:], in_=w1_grouped[a][:])
 
-        nc.vector.tensor_copy(v_codes[0][:], tab[0][:].bitcast(U32).indirect(picks[:]))
+        cast_w1(0)
+        cast_w1(1)
+        quantize_w1(0)
+        quantize_w1(1)
         nc.vector.tensor_copy(v_scale[:], tab_scale[:].indirect(picks[:]))
-        nc.vector.tensor_copy(v_codes[1][:], tab[1][:].bitcast(U32).indirect(picks[:]))
+        nc.vector.tensor_copy(v_codes0[:], tab[0][:].bitcast(U32).indirect(picks[:]))
         nc.vector.tensor_copy(
             w2_scale[:].rearrange("p (t m) -> p t m", t=PACK),
             w2_scale_raw[:].rearrange("p (m t) -> p t m", t=PACK),
         )
-        for a in range(2):
-            cast_w1(nc.scalar.copy, a, w1_raw[a][0][:], 0)
-            cast_w1(nc.vector.tensor_copy, a, w1_raw[a][1][:], P // 2)
-            quantize_w1(a)
+        for i in range(2):
+            nc.vector.tensor_copy(v_codes1[i][:], tab[1][:].bitcast(U32).indirect(picks[:, 32 * i : 32 * (i + 1)]))
 
         def interleave(engine_copy, grouped, planes):
             engine_copy(
                 grouped.rearrange("p (c i t) -> p c t i", i=4, t=PACK),
-                planes.rearrange("p (t c i) -> p c t i", i=4, t=PACK),
+                planes.rearrange("p t (c i) -> p c t i", i=4),
             )
 
         w3_codes = [held([P, W3_PIECE], U32, f"w3_codes{i}") for i in range(N // W3_PIECE)]
@@ -130,7 +125,7 @@ def tile_list_core_age_slopes_kernel(tc, tab_words, tab_scales, offs, w1, w2_wor
         w3_grouped = [held([P, PACK * W3_PIECE], BF16, f"w3_grouped{i}") for i in range(N // W3_PIECE)]
 
         def cast_w3(i, engine_copy):
-            interleave(engine_copy, w3_grouped[i][:], w3_raw[i][:].rearrange("p j c -> p (j c)"))
+            interleave(engine_copy, w3_grouped[i][:], w3_raw[:, :, i * W3_PIECE : (i + 1) * W3_PIECE])
 
         def quantize_w3(i):
             nc.vector.quantize_mx(out=w3_codes[i][:].bitcast(FP8X4), scales=w3_scale[i][:], in_=w3_grouped[i][:])
@@ -152,6 +147,8 @@ def tile_list_core_age_slopes_kernel(tc, tab_words, tab_scales, offs, w1, w2_wor
             j0, w = CHUNKS[c]
             per_bank = BANK // w
             cols = slice(j0, j0 + w)
+            half, h0 = divmod(j0, S // 2)
+            moving = [v_codes0[:, cols], v_codes1[half][:, h0 : h0 + w]]
             acc = bank("a_bank", 3)
             for a in range(2):
                 for u in range(per_bank):
@@ -160,7 +157,7 @@ def tile_list_core_age_slopes_kernel(tc, tab_words, tab_scales, offs, w1, w2_wor
                         out=acc[:, u * w : (u + 1) * w],
                         lhsT=w1_codes[a][:, t * P : (t + 1) * P].bitcast(FP8X4),
                         lhsT_scale=w1_scale[a][:, t * P : (t + 1) * P],
-                        rhs=v_codes[a][:, cols].bitcast(FP8X4),
+                        rhs=moving[a].bitcast(FP8X4),
                         rhs_scale=v_scale[4 * a : P, cols],
                         start=(a == 0 and u == 0),
                         stop=(a == 1 and u == per_bank - 1),
@@ -206,7 +203,7 @@ def tile_list_core_age_slopes_kernel(tc, tab_words, tab_scales, offs, w1, w2_wor
             nc.scalar.copy(arg[c][:, b * BANK : (b + 1) * BANK], acc[:])
 
         def quantize_f1(c):
-            interleave(nc.scalar.copy, f1_grouped[c][:], f1[c][:])
+            interleave(nc.scalar.copy, f1_grouped[c][:], f1[c][:].rearrange("p (t j) -> p t j", t=PACK))
             nc.vector.quantize_mx(out=f1_codes[c][:].bitcast(FP8X4), scales=f1_scale[c][:], in_=f1_grouped[c][:])
 
         def second_argument(c, short=False):
@@ -244,7 +241,7 @@ def tile_list_core_age_slopes_kernel(tc, tab_words, tab_scales, offs, w1, w2_wor
                     nc.vector.scalar_tensor_tensor(h_planes[c][:, plane], arg[c][:, plane], steps[:, t : t + 1], f1[c][:, plane], ALU.mult, ALU.add)
 
         def quantize_h(c):
-            interleave(nc.scalar.copy, h_grouped[c][:], h_planes[c][:])
+            interleave(nc.scalar.copy, h_grouped[c][:], h_planes[c][:].rearrange("p (t j) -> p t j", t=PACK))
             nc.vector.quantize_mx(out=h_codes[c][:].bitcast(FP8X4), scales=h_scale[c][:], in_=h_grouped[c][:])
 
         def place(chunks, tiles, y_tag=None, in_p_bank=False):

@@ -52,26 +52,48 @@ def tile_list_core_age_slopes_kernel(tc, tab_words, tab_scales, offs, w1, w2_wor
         ident = held([P, P], F32, "ident")
         warm = held([P, 2], F32, "warm")
 
-        nc.vector.memset(tab_scale[:].bitcast(I32), 0)
-        nc.vector.memset(w2_scale_raw[:].bitcast(I32), 0)
+        nc.vector.memset(tab_scale[32:64, :].bitcast(I32), 0)
+        nc.vector.memset(tab_scale[64:P, :].bitcast(I32), 0)
+        v_scale = held([P, S], U8, "v_scale")
+        nc.vector.memset(v_scale[:].bitcast(I32), 0)
+        nc.gpsimd.memset(w2_scale_raw[:].bitcast(I32), 0)
         nc.gpsimd.memset(warm[:, 0:1], 0.0)
         nc.scalar.activation(warm[:, 1:2], warm[:, 0:1], ACT.Tanh)
 
         nc.sync.dma_start(picks[:], offs)
+        nc.sync.dma_start(tab_scale[0:32, :].bitcast(I32), tab_scales.rearrange("a q t -> (a q) t").bitcast(I32))
         nc.sync.dma_start(places[:], offs2)
         nc.sync.dma_start(steps[:], step.rearrange("(p t) -> p t", t=PACK))
-        nc.sync.dma_start(w2_raw[:].bitcast(I32), w2_words[0].bitcast(I32))
         tab_rows = [tab_words[a].rearrange("p t i -> p (t i)").bitcast(I32) for a in range(2)]
         w1_rows = [w1[a * 512 : (a + 1) * 512, :].rearrange("(p j) c -> p j c", j=PACK) for a in range(2)]
         for a in range(2):
             for j in range(0, PACK, 2):
                 nc.sync.dma_start(w1_raw[a][:, j : j + 2, :], w1_rows[a][:, j : j + 2, :])
-        for q in range(4):
-            nc.sync.dma_start(tab_scale[32 * q : 32 * q + 8, :].bitcast(I32), tab_scales[:, 4 * q : 4 * q + 4, :].bitcast(I32))
-        nc.sync.dma_start(tab[0][:], tab_rows[0])
-        for q in range(4):
+        nc.sync.dma_start(w2_raw[:].bitcast(I32), w2_words[0].bitcast(I32))
+
+        def load_w2_scales(q):
             nc.sync.dma_start(w2_scale_raw[32 * q : 32 * q + 4, :].bitcast(I32), w2_scales[0, 4 * q : 4 * q + 4, :].bitcast(I32))
+
+        picked_scale = held([P, S], U8, "picked_scale")
+        nc.vector.tensor_copy(picked_scale[:], tab_scale[:].indirect(picks[:]))
+
+        def move_scales(a, q):
+            nc.sync.dma_start(
+                v_scale[32 * q + 4 * a : 32 * q + 4 * a + 4, :].bitcast(I32),
+                picked_scale[16 * a + 4 * q : 16 * a + 4 * q + 4, :].bitcast(I32),
+            )
+
+        for q in range(3):
+            load_w2_scales(q)
+        nc.sync.dma_start(tab[0][:], tab_rows[0])
+        load_w2_scales(3)
+        for q in range(2):
+            move_scales(0, q)
         nc.sync.dma_start(tab[1][:], tab_rows[1])
+        for q in range(2, 4):
+            move_scales(0, q)
+        for q in range(4):
+            move_scales(1, q)
         nc.sync.dma_start(w3_raw[:], w3.rearrange("(p j) c -> p j c", j=PACK))
         nc.sync.dma_start(gains[:], wgo)
         for n in range(N_TILES):
@@ -88,7 +110,6 @@ def tile_list_core_age_slopes_kernel(tc, tab_words, tab_scales, offs, w1, w2_wor
         w1_codes = [held([P, H], U32, f"w1_codes{a}") for a in range(2)]
         w1_scale = [held([P, H], U8, f"w1_scale{a}") for a in range(2)]
         w1_grouped = [held([P, PACK * H], BF16, f"w1_grouped{a}") for a in range(2)]
-        v_scale = held([P, S], U8, "v_scale")
         v_codes0 = held([P, S], U32, "v_codes0")
         v_codes1 = [held([P, S // 2], U32, f"v_codes1_{i}") for i in range(2)]
 
@@ -105,7 +126,6 @@ def tile_list_core_age_slopes_kernel(tc, tab_words, tab_scales, offs, w1, w2_wor
         cast_w1(1)
         quantize_w1(0)
         quantize_w1(1)
-        nc.vector.tensor_copy(v_scale[:], tab_scale[:].indirect(picks[:]))
         nc.vector.tensor_copy(v_codes0[:], tab[0][:].bitcast(U32).indirect(picks[:]))
         nc.vector.tensor_copy(
             w2_scale[:].rearrange("p (t m) -> p t m", t=PACK),
@@ -149,7 +169,7 @@ def tile_list_core_age_slopes_kernel(tc, tab_words, tab_scales, offs, w1, w2_wor
             cols = slice(j0, j0 + w)
             half, h0 = divmod(j0, S // 2)
             moving = [v_codes0[:, cols], v_codes1[half][:, h0 : h0 + w]]
-            acc = bank("a_bank", 3)
+            acc = bank("a_bank", 2)
             for a in range(2):
                 for u in range(per_bank):
                     t = b * per_bank + u
@@ -249,7 +269,7 @@ def tile_list_core_age_slopes_kernel(tc, tab_words, tab_scales, offs, w1, w2_wor
             w = sum(CHUNKS[c][1] for c in chunks)
             acc = bank("p_bank", 2) if in_p_bank else bank("y_bank", 3)
             if y_tag is None:
-                y = ring.tile([P, BANK], F32, name="y")
+                y = ring.tile([P, BANK], F32, name="y", tag="y", bufs=8)
             else:
                 y = keep.tile([P, BANK], F32, name="y", tag=y_tag, align_bytes=64)
             for u, n in enumerate(tiles):
@@ -277,7 +297,7 @@ def tile_list_core_age_slopes_kernel(tc, tab_words, tab_scales, offs, w1, w2_wor
         def add_on_tensor(n):
             blocks = BANK // P
             for half in range(S // BANK):
-                turned_acc = bank("a_bank", 3)
+                turned_acc = bank("a_bank", 2)
                 turned = ring.tile([P, BANK], F32, name="turned", tag="turned", bufs=2)
                 for first, source in ((True, rows[n]), (False, pages[n])):
                     for u in range(blocks):
@@ -295,14 +315,13 @@ def tile_list_core_age_slopes_kernel(tc, tab_words, tab_scales, offs, w1, w2_wor
                     nc.tensor.transpose(back_acc[:, u * P : (u + 1) * P], turned[:, u * P : (u + 1) * P], ident[:])
                 cols = slice(half * BANK, (half + 1) * BANK)
                 nc.scalar.copy(rows[n][:, cols], back_acc[:])
-                nc.sync.dma_start(out[n * P : (n + 1) * P, cols], rows[n][:, cols])
+            nc.scalar.dma_start(out[n * P : (n + 1) * P, :], rows[n][:])
 
         def add_on_vector(n):
             for half in range(S // BANK):
                 cols = slice(half * BANK, (half + 1) * BANK)
-                total = ring.tile([P, BANK], F32, name="total", tag="turned", bufs=2)
-                nc.vector.tensor_tensor(total[:], pages[n][:, cols], rows[n][:, cols], ALU.add)
-                nc.sync.dma_start(out[n * P : (n + 1) * P, cols], total[:])
+                nc.vector.tensor_tensor(rows[n][:, cols], pages[n][:, cols], rows[n][:, cols], ALU.add)
+                nc.sync.dma_start(out[n * P : (n + 1) * P, cols], rows[n][:, cols])
 
         short_first_slope(0)
         second_argument(0, short=True)
@@ -318,51 +337,49 @@ def tile_list_core_age_slopes_kernel(tc, tab_words, tab_scales, offs, w1, w2_wor
         short_second_slope(1)
         acc21 = first_slope(2, 1)
         keep_argument(2, 0, acc20)
-        place((0,), (2, 3,))
         cast_w3(2, nc.scalar.copy)
         quantize_w3(2)
         quantize_f1(2)
         keep_argument(2, 1, acc21)
-        place((0,), (4, 5,))
+        place((0,), (2, 3,))
         second_argument(2)
-        place((1,), (0, 1,), y_tag="f1_grouped2")
         acc30 = first_slope(3, 0)
-        second_slope(2)
-        place((1,), (2, 3,), in_p_bank=True)
-        quantize_h(2)
-        place((1,), (4, 5,), y_tag="arg2")
         keep_argument(3, 0, acc30)
+        place((0,), (4, 5,), y_tag="f1_grouped2")
         acc31 = first_slope(3, 1)
-        quantize_f1(3)
+        second_slope(2)
         keep_argument(3, 1, acc31)
-        place((2,), (0,))
+        place((1,), (0, 1,), in_p_bank=True)
+        quantize_f1(3)
+        quantize_h(2)
+        place((1,), (2, 3,), y_tag="arg2")
         second_argument(3)
-        place((2,), (1,), y_tag="f1_grouped3")
         acc40 = first_slope(4, 0)
-        second_slope(3)
-        place((2,), (2,), in_p_bank=True)
-        quantize_h(3)
-        place((2,), (3,), y_tag="arg3")
         keep_argument(4, 0, acc40)
+        place((1,), (4, 5,), y_tag="f1_grouped3")
         acc41 = first_slope(4, 1)
-        quantize_f1(4)
+        second_slope(3)
         keep_argument(4, 1, acc41)
-        place((2,), (4,))
+        place((2,), (0,), in_p_bank=True)
+        quantize_f1(4)
+        quantize_h(3)
+        place((2,), (1,), y_tag="arg3")
         second_argument(4)
-        place((2,), (5,), y_tag="f1_grouped4")
+        place((2,), (2,), y_tag="f1_grouped4")
         second_slope(4)
-        place((3,), (0,), in_p_bank=True)
+        place((2,), (3,), in_p_bank=True)
         quantize_h(4)
-        place((3,), (1,), y_tag="arg4")
-        place((4,), (0,))
-        place((4,), (1,))
+        place((2,), (4,), y_tag="arg4")
+        place((3, 4,), (0,))
+        place((3, 4,), (1,))
         place((3, 4,), (2,))
         place((3, 4,), (3,))
+        place((3, 4,), (4,))
+        place((2,), (5,))
+        add_on_vector(4)
+        place((3, 4,), (5,))
         add_on_tensor(0)
         add_on_tensor(1)
-        place((3, 4,), (4,), in_p_bank=True)
         add_on_tensor(2)
-        place((3, 4,), (5,), in_p_bank=True)
         add_on_tensor(3)
-        add_on_tensor(4)
         add_on_vector(5)

@@ -19,27 +19,43 @@ ACT = mybir.ActivationFunctionType
 
 P = 128
 PACK = 4
+K_PASS = P * PACK
+QUADRANT = 32
 BANK = 512
-CHUNKS = [(0, 128), (128, 128), (256, 256), (512, 256), (768, 256)]
-N_TILES = N // P
+LIST_COLUMN = 16
+ROW_TILES = N // P
 W3_PIECE = 256
+
+CHUNKS = [(0, 128), (128, 128), (256, 256), (512, 256), (768, 256)]
+TENSOR_ADDS = 4
+A_BANKS, B_BANKS, Y_BANKS = 2, 2, 3
+Y_TILES = 8
 
 
 def tile_list_core_age_slopes_kernel(tc, tab_words, tab_scales, offs, w1, w2_words, w2_scales, step, w3, offs2, wgo, x0, out):
     nc = tc.nc
     with ExitStack() as ctx:
         keep = ctx.enter_context(tc.tile_pool(name="keep", bufs=1))
-        ring = ctx.enter_context(tc.tile_pool(name="ring", bufs=3))
+        ring = ctx.enter_context(tc.tile_pool(name="ring", bufs=1))
         psum = ctx.enter_context(tc.psum_pool(name="psum", bufs=1))
 
         def held(shape, dtype, name):
             return keep.tile(shape, dtype, name=name, tag=name, align_bytes=64)
 
-        def bank(tag, bufs):
-            return psum.tile([P, BANK], F32, name=tag, tag=tag, bufs=bufs)
+        def a_bank():
+            return psum.tile([P, BANK], F32, name="a_bank", tag="a_bank", bufs=A_BANKS)
 
-        picks = held([P, S // 16], U16, "picks")
-        places = held([P, S // 16], U16, "places")
+        def b_bank():
+            return psum.tile([P, BANK], F32, name="b_bank", tag="b_bank", bufs=B_BANKS)
+
+        def y_bank():
+            return psum.tile([P, BANK], F32, name="y_bank", tag="y_bank", bufs=Y_BANKS)
+
+        def quantize(codes, scale, grouped):
+            nc.vector.quantize_mx(out=codes[:].bitcast(FP8X4), scales=scale[:], in_=grouped[:])
+
+        picks = held([P, S // LIST_COLUMN], U16, "picks")
+        places = held([P, S // LIST_COLUMN], U16, "places")
         steps = held([P, PACK], F32, "steps")
         w2_raw = held([P, 2 * H], U8, "w2_raw")
         w2_scale_raw = held([P, H], U8, "w2_scale_raw")
@@ -48,55 +64,57 @@ def tile_list_core_age_slopes_kernel(tc, tab_words, tab_scales, offs, w1, w2_wor
         w1_raw = [held([P, PACK, H], F32, f"w1_raw{a}") for a in range(2)]
         w3_raw = held([P, PACK, N], F32, "w3_raw")
         gains = held([P, S], F32, "gains")
-        rows = [held([P, S], F32, f"rows{n}") for n in range(N_TILES)]
+        rows = [held([P, S], F32, f"rows{n}") for n in range(ROW_TILES)]
         ident = held([P, P], F32, "ident")
-        warm = held([P, 2], F32, "warm")
-
-        nc.vector.memset(tab_scale[32:64, :].bitcast(I32), 0)
-        nc.vector.memset(tab_scale[64:P, :].bitcast(I32), 0)
         v_scale = held([P, S], U8, "v_scale")
+        picked_scale = held([P, S], U8, "picked_scale")
+
+        nc.vector.memset(tab_scale[QUADRANT : 2 * QUADRANT, :].bitcast(I32), 0)
+        nc.vector.memset(tab_scale[2 * QUADRANT : P, :].bitcast(I32), 0)
         nc.vector.memset(v_scale[:].bitcast(I32), 0)
         nc.gpsimd.memset(w2_scale_raw[:].bitcast(I32), 0)
-        nc.gpsimd.memset(warm[:, 0:1], 0.0)
-        nc.scalar.activation(warm[:, 1:2], warm[:, 0:1], ACT.Tanh)
 
         nc.sync.dma_start(picks[:], offs)
-        nc.sync.dma_start(tab_scale[0:32, :].bitcast(I32), tab_scales.rearrange("a q t -> (a q) t").bitcast(I32))
+        nc.sync.dma_start(tab_scale[0:QUADRANT, :].bitcast(I32), tab_scales.rearrange("a q t -> (a q) t").bitcast(I32))
         nc.sync.dma_start(places[:], offs2)
         nc.sync.dma_start(steps[:], step.rearrange("(p t) -> p t", t=PACK))
-        tab_rows = [tab_words[a].rearrange("p t i -> p (t i)").bitcast(I32) for a in range(2)]
-        w1_rows = [w1[a * 512 : (a + 1) * 512, :].rearrange("(p j) c -> p j c", j=PACK) for a in range(2)]
         for a in range(2):
+            w1_rows = w1[a * K_PASS : (a + 1) * K_PASS, :].rearrange("(p j) c -> p j c", j=PACK)
             for j in range(0, PACK, 2):
-                nc.sync.dma_start(w1_raw[a][:, j : j + 2, :], w1_rows[a][:, j : j + 2, :])
+                nc.sync.dma_start(w1_raw[a][:, j : j + 2, :], w1_rows[:, j : j + 2, :])
         nc.sync.dma_start(w2_raw[:].bitcast(I32), w2_words[0].bitcast(I32))
-
-        def load_w2_scales(q):
-            nc.sync.dma_start(w2_scale_raw[32 * q : 32 * q + 4, :].bitcast(I32), w2_scales[0, 4 * q : 4 * q + 4, :].bitcast(I32))
-
-        picked_scale = held([P, S], U8, "picked_scale")
         nc.vector.tensor_copy(picked_scale[:], tab_scale[:].indirect(picks[:]))
 
-        def move_scales(a, q):
+        def load_table(a):
+            nc.sync.dma_start(tab[a][:], tab_words[a].rearrange("p t i -> p (t i)").bitcast(I32))
+
+        def load_w2_scales(quadrant):
             nc.sync.dma_start(
-                v_scale[32 * q + 4 * a : 32 * q + 4 * a + 4, :].bitcast(I32),
-                picked_scale[16 * a + 4 * q : 16 * a + 4 * q + 4, :].bitcast(I32),
+                w2_scale_raw[QUADRANT * quadrant : QUADRANT * quadrant + 4, :].bitcast(I32),
+                w2_scales[0, 4 * quadrant : 4 * quadrant + 4, :].bitcast(I32),
             )
 
-        for q in range(3):
-            load_w2_scales(q)
-        nc.sync.dma_start(tab[0][:], tab_rows[0])
+        def move_scales(a, quadrant):
+            first = QUADRANT * quadrant + 4 * a
+            nc.sync.dma_start(
+                v_scale[first : first + 4, :].bitcast(I32),
+                picked_scale[16 * a + 4 * quadrant : 16 * a + 4 * quadrant + 4, :].bitcast(I32),
+            )
+
+        for quadrant in range(3):
+            load_w2_scales(quadrant)
+        load_table(0)
         load_w2_scales(3)
-        for q in range(2):
-            move_scales(0, q)
-        nc.sync.dma_start(tab[1][:], tab_rows[1])
-        for q in range(2, 4):
-            move_scales(0, q)
-        for q in range(4):
-            move_scales(1, q)
+        for quadrant in range(2):
+            move_scales(0, quadrant)
+        load_table(1)
+        for quadrant in range(2, 4):
+            move_scales(0, quadrant)
+        for quadrant in range(4):
+            move_scales(1, quadrant)
         nc.sync.dma_start(w3_raw[:], w3.rearrange("(p j) c -> p j c", j=PACK))
         nc.sync.dma_start(gains[:], wgo)
-        for n in range(N_TILES):
+        for n in range(ROW_TILES):
             nc.sync.dma_start(rows[n][:], x0[n * P : (n + 1) * P, :])
         make_identity(nc, ident[:])
 
@@ -110,276 +128,287 @@ def tile_list_core_age_slopes_kernel(tc, tab_words, tab_scales, offs, w1, w2_wor
         w1_codes = [held([P, H], U32, f"w1_codes{a}") for a in range(2)]
         w1_scale = [held([P, H], U8, f"w1_scale{a}") for a in range(2)]
         w1_grouped = [held([P, PACK * H], BF16, f"w1_grouped{a}") for a in range(2)]
-        v_codes0 = held([P, S], U32, "v_codes0")
-        v_codes1 = [held([P, S // 2], U32, f"v_codes1_{i}") for i in range(2)]
-
-        def cast_w1(a):
+        for a in range(2):
             nc.vector.tensor_copy(
                 w1_grouped[a][:].rearrange("p (t m j) -> p m j t", t=PACK, j=PACK),
                 w1_raw[a][:].rearrange("p j (m t) -> p m j t", t=PACK),
             )
+        for a in range(2):
+            quantize(w1_codes[a], w1_scale[a], w1_grouped[a])
 
-        def quantize_w1(a):
-            nc.vector.quantize_mx(out=w1_codes[a][:].bitcast(FP8X4), scales=w1_scale[a][:], in_=w1_grouped[a][:])
-
-        cast_w1(0)
-        cast_w1(1)
-        quantize_w1(0)
-        quantize_w1(1)
+        v_codes0 = held([P, S], U32, "v_codes0")
+        v_codes1 = [held([P, S // 2], U32, f"v_codes1_{half}") for half in range(2)]
         nc.vector.tensor_copy(v_codes0[:], tab[0][:].bitcast(U32).indirect(picks[:]))
         nc.vector.tensor_copy(
             w2_scale[:].rearrange("p (t m) -> p t m", t=PACK),
             w2_scale_raw[:].rearrange("p (m t) -> p t m", t=PACK),
         )
-        for i in range(2):
-            nc.vector.tensor_copy(v_codes1[i][:], tab[1][:].bitcast(U32).indirect(picks[:, 32 * i : 32 * (i + 1)]))
+        half_list = S // 2 // LIST_COLUMN
+        for half in range(2):
+            nc.vector.tensor_copy(v_codes1[half][:], tab[1][:].bitcast(U32).indirect(picks[:, half_list * half : half_list * (half + 1)]))
 
-        def interleave(engine_copy, grouped, planes):
+        def group(engine_copy, grouped, planes):
             engine_copy(
                 grouped.rearrange("p (c i t) -> p c t i", i=4, t=PACK),
                 planes.rearrange("p t (c i) -> p c t i", i=4),
             )
 
-        w3_codes = [held([P, W3_PIECE], U32, f"w3_codes{i}") for i in range(N // W3_PIECE)]
-        w3_scale = [held([P, W3_PIECE], U8, f"w3_scale{i}") for i in range(N // W3_PIECE)]
-        w3_grouped = [held([P, PACK * W3_PIECE], BF16, f"w3_grouped{i}") for i in range(N // W3_PIECE)]
+        def as_planes(tile):
+            return tile[:].rearrange("p (t j) -> p t j", t=PACK)
+
+        def planes_by_sample(tile):
+            return tile[:].rearrange("p (t j) -> p j t", t=PACK)
+
+        def as_grouped(tile):
+            return tile[:].rearrange("p (j t) -> p j t", t=PACK)
+
+        w3_pieces = range(N // W3_PIECE)
+        w3_codes = [held([P, W3_PIECE], U32, f"w3_codes{i}") for i in w3_pieces]
+        w3_scale = [held([P, W3_PIECE], U8, f"w3_scale{i}") for i in w3_pieces]
+        w3_grouped = [held([P, PACK * W3_PIECE], BF16, f"w3_grouped{i}") for i in w3_pieces]
 
         def cast_w3(i, engine_copy):
-            interleave(engine_copy, w3_grouped[i][:], w3_raw[:, :, i * W3_PIECE : (i + 1) * W3_PIECE])
+            group(engine_copy, w3_grouped[i][:], w3_raw[:, :, i * W3_PIECE : (i + 1) * W3_PIECE])
 
         def quantize_w3(i):
-            nc.vector.quantize_mx(out=w3_codes[i][:].bitcast(FP8X4), scales=w3_scale[i][:], in_=w3_grouped[i][:])
+            quantize(w3_codes[i], w3_scale[i], w3_grouped[i])
 
-        f1, arg, f1_grouped, f1_codes, f1_scale, h_grouped, h_codes, h_scale = ([] for i in range(8))
-        h_planes = {}
-        for c, (j0, w) in enumerate(CHUNKS):
-            f1.append(held([P, PACK * w], F32, f"f1_{c}"))
-            arg.append(held([P, PACK * w], F32, f"arg{c}"))
-            f1_grouped.append(held([P, PACK * w], BF16, f"f1_grouped{c}"))
-            f1_codes.append(held([P, w], U32, f"f1_codes{c}"))
-            f1_scale.append(held([P, w], U8, f"f1_scale{c}"))
-            h_grouped.append(held([P, PACK * w], BF16, f"h_grouped{c}"))
-            h_codes.append(held([P, w], U32, f"h_codes{c}"))
-            h_scale.append(held([P, w], U8, f"h_scale{c}"))
-        pages = [held([P, S], F32, f"page{n}") for n in range(N_TILES)]
+        def chunk_tiles(dtype, pack, name):
+            return [held([P, pack * width], dtype, f"{name}{c}") for c, (first, width) in enumerate(CHUNKS)]
 
-        def first_product(c, b):
-            j0, w = CHUNKS[c]
-            per_bank = BANK // w
-            cols = slice(j0, j0 + w)
-            half, h0 = divmod(j0, S // 2)
-            moving = [v_codes0[:, cols], v_codes1[half][:, h0 : h0 + w]]
-            acc = bank("a_bank", 2)
+        slope = chunk_tiles(F32, PACK, "slope")
+        arg = chunk_tiles(F32, PACK, "arg")
+        f1_grouped = chunk_tiles(BF16, PACK, "f1_grouped")
+        f1_codes = chunk_tiles(U32, 1, "f1_codes")
+        f1_scale = chunk_tiles(U8, 1, "f1_scale")
+        h_grouped = chunk_tiles(BF16, PACK, "h_grouped")
+        h_codes = chunk_tiles(U32, 1, "h_codes")
+        h_scale = chunk_tiles(U8, 1, "h_scale")
+        pages = [held([P, S], F32, f"page{n}") for n in range(ROW_TILES)]
+
+        def bank_planes(c, b):
+            width = CHUNKS[c][1]
+            count = BANK // width
+            return [(b * count + u, slice(u * width, (u + 1) * width)) for u in range(count)]
+
+        def bank_span(b):
+            return slice(b * BANK, (b + 1) * BANK)
+
+        def w1_product(acc, c, b, close):
+            first, width = CHUNKS[c]
+            samples = slice(first, first + width)
+            half, in_half = divmod(first, S // 2)
+            moving = [v_codes0[:, samples], v_codes1[half][:, in_half : in_half + width]]
+            planes = bank_planes(c, b)
             for a in range(2):
-                for u in range(per_bank):
-                    t = b * per_bank + u
+                for u, (t, cols) in enumerate(planes):
                     nc.tensor.matmul_mx(
-                        out=acc[:, u * w : (u + 1) * w],
+                        out=acc[:, cols],
                         lhsT=w1_codes[a][:, t * P : (t + 1) * P].bitcast(FP8X4),
                         lhsT_scale=w1_scale[a][:, t * P : (t + 1) * P],
                         rhs=moving[a].bitcast(FP8X4),
-                        rhs_scale=v_scale[4 * a : P, cols],
+                        rhs_scale=v_scale[4 * a : P, samples],
                         start=(a == 0 and u == 0),
-                        stop=(a == 1 and u == per_bank - 1),
+                        stop=(close and a == 1 and u == len(planes) - 1),
                     )
+
+        def w2_product(acc, c, b, onto_a):
+            planes = bank_planes(c, b)
+            for u, (t, cols) in enumerate(planes):
+                nc.tensor.matmul_mx(
+                    out=acc[:, cols],
+                    lhsT=w2_codes[:, 2 * t * P : 2 * (t + 1) * P].bitcast(FP4X4),
+                    lhsT_scale=w2_scale[:, t * P : (t + 1) * P],
+                    rhs=f1_codes[c][:].bitcast(FP8X4),
+                    rhs_scale=f1_scale[c][:],
+                    start=not onto_a,
+                    stop=(not onto_a or u == len(planes) - 1),
+                )
+
+        def times_step(grouped, values, c):
+            repeated = steps[:].unsqueeze(1).to_broadcast([P, CHUNKS[c][1], PACK])
+            nc.vector.tensor_tensor(as_grouped(grouped), as_grouped(values), repeated, ALU.mult)
+
+        def narrow_f1(c):
+            acc = a_bank()
+            w1_product(acc, c, 0, close=True)
+            nc.scalar.activation(as_grouped(slope[c]), planes_by_sample(acc), ACT.Tanh)
+            times_step(f1_grouped[c], slope[c], c)
+            quantize(f1_codes[c], f1_scale[c], f1_grouped[c])
             return acc
 
-        def woven(ap, w):
-            return ap.rearrange("p (t j) -> p j t", t=PACK)
+        def narrow_h(c):
+            nc.vector.tensor_tensor(arg[c][:], arg[c][:], slope[c][:], ALU.add)
+            times_step(h_grouped[c], arg[c], c)
+            quantize(h_codes[c], h_scale[c], h_grouped[c])
 
-        def by_column(ap):
-            return ap.rearrange("p (j t) -> p j t", t=PACK)
-
-        def step_rows(w):
-            return steps[:].unsqueeze(1).to_broadcast([P, w, PACK])
-
-        def short_first_slope(c):
-            w = CHUNKS[c][1]
-            acc = first_product(c, 0)
-            nc.scalar.activation(by_column(f1[c][:]), woven(acc[:], w), ACT.Tanh)
-            nc.vector.tensor_tensor(by_column(f1_grouped[c][:]), by_column(f1[c][:]), step_rows(w), ALU.mult)
-            nc.vector.quantize_mx(out=f1_codes[c][:].bitcast(FP8X4), scales=f1_scale[c][:], in_=f1_grouped[c][:])
-            nc.scalar.copy(by_column(arg[c][:]), woven(acc[:], w))
-
-        def short_second_slope(c):
-            w = CHUNKS[c][1]
-            nc.scalar.activation(arg[c][:], arg[c][:], ACT.Tanh)
-            nc.vector.tensor_tensor(arg[c][:], arg[c][:], f1[c][:], ALU.add)
-            nc.vector.tensor_tensor(by_column(h_grouped[c][:]), by_column(arg[c][:]), step_rows(w), ALU.mult)
-            nc.vector.quantize_mx(out=h_codes[c][:].bitcast(FP8X4), scales=h_scale[c][:], in_=h_grouped[c][:])
-
-        def first_slope(c, b):
-            w = CHUNKS[c][1]
-            per_bank = BANK // w
-            acc = first_product(c, b)
-            nc.scalar.activation(f1[c][:, b * BANK : (b + 1) * BANK], acc[:], ACT.Tanh)
-            for u in range(per_bank):
-                t = b * per_bank + u
-                plane = f1[c][:, t * w : (t + 1) * w]
+        def wide_f1(c, b):
+            acc = a_bank()
+            w1_product(acc, c, b, close=True)
+            nc.scalar.activation(slope[c][:, bank_span(b)], acc[:], ACT.Tanh)
+            for t, cols in bank_planes(c, b):
+                plane = as_planes(slope[c])[:, t, :]
                 nc.scalar.activation(plane, plane, ACT.Copy, scale=steps[:, t : t + 1])
             return acc
 
-        def keep_argument(c, b, acc):
-            nc.scalar.copy(arg[c][:, b * BANK : (b + 1) * BANK], acc[:])
+        def keep_a(c, b, acc):
+            nc.scalar.copy(arg[c][:, bank_span(b)], acc[:])
 
-        def quantize_f1(c):
-            interleave(nc.scalar.copy, f1_grouped[c][:], f1[c][:].rearrange("p (t j) -> p t j", t=PACK))
-            nc.vector.quantize_mx(out=f1_codes[c][:].bitcast(FP8X4), scales=f1_scale[c][:], in_=f1_grouped[c][:])
+        def wide_quantize_f1(c):
+            group(nc.scalar.copy, f1_grouped[c][:], as_planes(slope[c]))
+            quantize(f1_codes[c], f1_scale[c], f1_grouped[c])
 
-        def second_argument(c, short=False):
-            j0, w = CHUNKS[c]
-            per_bank = BANK // w
-            for b in range(PACK // per_bank):
-                acc = bank("p_bank", 2)
-                span = slice(b * BANK, (b + 1) * BANK)
-                for u in range(per_bank):
-                    t = b * per_bank + u
-                    nc.tensor.matmul_mx(
-                        out=acc[:, u * w : (u + 1) * w],
-                        lhsT=w2_codes[:, 2 * t * P : 2 * (t + 1) * P].bitcast(FP4X4),
-                        lhsT_scale=w2_scale[:, t * P : (t + 1) * P],
-                        rhs=f1_codes[c][:].bitcast(FP8X4),
-                        rhs_scale=f1_scale[c][:],
-                        start=True,
-                        stop=True,
+        def wide_b(c):
+            for b in range(2):
+                acc = b_bank()
+                w2_product(acc, c, b, onto_a=False)
+                nc.vector.tensor_tensor(arg[c][:, bank_span(b)], acc[:], arg[c][:, bank_span(b)], ALU.add)
+
+        def wide_h(c):
+            h_planes = held([P, PACK * CHUNKS[c][1]], BF16, f"h_planes{c}")
+            for b in range(2):
+                nc.scalar.activation(arg[c][:, bank_span(b)], arg[c][:, bank_span(b)], ACT.Tanh)
+                for t, cols in bank_planes(c, b):
+                    nc.vector.scalar_tensor_tensor(
+                        as_planes(h_planes)[:, t, :],
+                        as_planes(arg[c])[:, t, :],
+                        steps[:, t : t + 1],
+                        as_planes(slope[c])[:, t, :],
+                        ALU.mult,
+                        ALU.add,
                     )
-                if short:
-                    nc.vector.tensor_tensor(by_column(arg[c][:]), woven(acc[:], w), by_column(arg[c][:]), ALU.add)
-                else:
-                    nc.vector.tensor_tensor(arg[c][:, span], acc[:], arg[c][:, span], ALU.add)
+            return h_planes
 
-        def second_slope(c):
-            j0, w = CHUNKS[c]
-            h_planes[c] = held([P, PACK * w], BF16, f"h_planes{c}")
-            per_bank = BANK // w
-            for b in range(PACK // per_bank):
-                span = slice(b * BANK, (b + 1) * BANK)
-                nc.scalar.activation(arg[c][:, span], arg[c][:, span], ACT.Tanh)
-                for u in range(per_bank):
-                    t = b * per_bank + u
-                    plane = slice(t * w, (t + 1) * w)
-                    nc.vector.scalar_tensor_tensor(h_planes[c][:, plane], arg[c][:, plane], steps[:, t : t + 1], f1[c][:, plane], ALU.mult, ALU.add)
+        def wide_quantize_h(c, h_planes):
+            group(nc.scalar.copy, h_grouped[c][:], as_planes(h_planes))
+            quantize(h_codes[c], h_scale[c], h_grouped[c])
 
-        def quantize_h(c):
-            interleave(nc.scalar.copy, h_grouped[c][:], h_planes[c][:].rearrange("p (t j) -> p t j", t=PACK))
-            nc.vector.quantize_mx(out=h_codes[c][:].bitcast(FP8X4), scales=h_scale[c][:], in_=h_grouped[c][:])
-
-        def place(chunks, tiles, y_tag=None, in_p_bank=False):
-            j0 = CHUNKS[chunks[0]][0]
-            w = sum(CHUNKS[c][1] for c in chunks)
-            acc = bank("p_bank", 2) if in_p_bank else bank("y_bank", 3)
-            if y_tag is None:
-                y = ring.tile([P, BANK], F32, name="y", tag="y", bufs=8)
-            else:
-                y = keep.tile([P, BANK], F32, name="y", tag=y_tag, align_bytes=64)
+        def unit(chunks, tiles, acc, y):
+            first = CHUNKS[chunks[0]][0]
+            width = sum(CHUNKS[c][1] for c in chunks)
             for u, n in enumerate(tiles):
-                i, n0 = divmod(n * P, W3_PIECE)
+                i, in_piece = divmod(n * P, W3_PIECE)
                 for c in chunks:
-                    first = u * w + CHUNKS[c][0] - j0
+                    column = u * width + CHUNKS[c][0] - first
                     nc.tensor.matmul_mx(
-                        out=acc[:, first : first + CHUNKS[c][1]],
-                        lhsT=w3_codes[i][:, n0 : n0 + P].bitcast(FP8X4),
-                        lhsT_scale=w3_scale[i][:, n0 : n0 + P],
+                        out=acc[:, column : column + CHUNKS[c][1]],
+                        lhsT=w3_codes[i][:, in_piece : in_piece + P].bitcast(FP8X4),
+                        lhsT_scale=w3_scale[i][:, in_piece : in_piece + P],
                         rhs=h_codes[c][:].bitcast(FP8X4),
                         rhs_scale=h_scale[c][:],
                         start=True,
                         stop=True,
                     )
-            nc.scalar.copy(y[:, 0 : len(tiles) * w], acc[:, 0 : len(tiles) * w])
+            nc.scalar.copy(y[:, 0 : len(tiles) * width], acc[:, 0 : len(tiles) * width])
             for u, n in enumerate(tiles):
                 nc.vector.tensor_tensor(
-                    pages[n][:].indirect(places[:, j0 // 16 : (j0 + w) // 16]),
-                    y[:, u * w : (u + 1) * w],
-                    gains[:, j0 : j0 + w],
+                    pages[n][:].indirect(places[:, first // LIST_COLUMN : (first + width) // LIST_COLUMN]),
+                    y[:, u * width : (u + 1) * width],
+                    gains[:, first : first + width],
                     ALU.mult,
                 )
+
+        def y_tile():
+            return ring.tile([P, BANK], F32, name="y", tag="y", bufs=Y_TILES)
+
+        def free_unit(chunks, tiles):
+            unit(chunks, tiles, y_bank(), y_tile())
+
+        def unit_staged_in(name, chunks, tiles):
+            unit(chunks, tiles, y_bank(), held([P, BANK], F32, name))
+
+        def unit_in_b_bank(chunks, tiles):
+            unit(chunks, tiles, b_bank(), y_tile())
 
         def add_on_tensor(n):
             blocks = BANK // P
             for half in range(S // BANK):
-                turned_acc = bank("a_bank", 2)
+                turned_acc = a_bank()
                 turned = ring.tile([P, BANK], F32, name="turned", tag="turned", bufs=2)
-                for first, source in ((True, rows[n]), (False, pages[n])):
+                for opens, source in ((True, rows[n]), (False, pages[n])):
                     for u in range(blocks):
                         nc.tensor.matmul(
                             turned_acc[:, u * P : (u + 1) * P],
                             source[:, half * BANK + u * P : half * BANK + (u + 1) * P],
                             ident[:],
                             is_transpose=True,
-                            start=(first and u == 0),
-                            stop=(not first and u == blocks - 1),
+                            start=(opens and u == 0),
+                            stop=(not opens and u == blocks - 1),
                         )
                 nc.scalar.copy(turned[:], turned_acc[:])
-                back_acc = bank("p_bank", 2)
+                back_acc = b_bank()
                 for u in range(blocks):
                     nc.tensor.transpose(back_acc[:, u * P : (u + 1) * P], turned[:, u * P : (u + 1) * P], ident[:])
-                cols = slice(half * BANK, (half + 1) * BANK)
-                nc.scalar.copy(rows[n][:, cols], back_acc[:])
+                nc.scalar.copy(rows[n][:, bank_span(half)], back_acc[:])
             nc.scalar.dma_start(out[n * P : (n + 1) * P, :], rows[n][:])
 
         def add_on_vector(n):
             for half in range(S // BANK):
-                cols = slice(half * BANK, (half + 1) * BANK)
+                cols = bank_span(half)
                 nc.vector.tensor_tensor(rows[n][:, cols], pages[n][:, cols], rows[n][:, cols], ALU.add)
                 nc.sync.dma_start(out[n * P : (n + 1) * P, cols], rows[n][:, cols])
 
-        short_first_slope(0)
-        second_argument(0, short=True)
+        early = [((c,), (n, n + 1)) for c in (0, 1) for n in range(0, ROW_TILES, 2)]
+        early = early + [((2,), (n,)) for n in range(ROW_TILES)]
+
+        narrow_f1(0)
+        acc = b_bank()
+        w1_product(acc, 0, 0, close=False)
+        w2_product(acc, 0, 0, onto_a=True)
         cast_w3(0, nc.vector.tensor_copy)
-        short_first_slope(1)
-        short_second_slope(0)
+        nc.scalar.activation(as_grouped(arg[0]), planes_by_sample(acc), ACT.Tanh)
+        narrow_h(0)
         quantize_w3(0)
-        second_argument(1, short=True)
+        free_unit(*early[0])
+
+        acc = narrow_f1(1)
+        nc.scalar.copy(as_grouped(arg[1]), planes_by_sample(acc))
+        acc = b_bank()
+        w2_product(acc, 1, 0, onto_a=False)
+        nc.vector.tensor_tensor(as_grouped(arg[1]), planes_by_sample(acc), as_grouped(arg[1]), ALU.add)
         cast_w3(1, nc.vector.tensor_copy)
         quantize_w3(1)
-        acc20 = first_slope(2, 0)
-        place((0,), (0, 1,))
-        short_second_slope(1)
-        acc21 = first_slope(2, 1)
-        keep_argument(2, 0, acc20)
+        nc.scalar.activation(arg[1][:], arg[1][:], ACT.Tanh)
+        narrow_h(1)
+
+        acc0 = wide_f1(2, 0)
+        acc1 = wide_f1(2, 1)
+        keep_a(2, 0, acc0)
         cast_w3(2, nc.scalar.copy)
         quantize_w3(2)
-        quantize_f1(2)
-        keep_argument(2, 1, acc21)
-        place((0,), (2, 3,))
-        second_argument(2)
-        acc30 = first_slope(3, 0)
-        keep_argument(3, 0, acc30)
-        place((0,), (4, 5,), y_tag="f1_grouped2")
-        acc31 = first_slope(3, 1)
-        second_slope(2)
-        keep_argument(3, 1, acc31)
-        place((1,), (0, 1,), in_p_bank=True)
-        quantize_f1(3)
-        quantize_h(2)
-        place((1,), (2, 3,), y_tag="arg2")
-        second_argument(3)
-        acc40 = first_slope(4, 0)
-        keep_argument(4, 0, acc40)
-        place((1,), (4, 5,), y_tag="f1_grouped3")
-        acc41 = first_slope(4, 1)
-        second_slope(3)
-        keep_argument(4, 1, acc41)
-        place((2,), (0,), in_p_bank=True)
-        quantize_f1(4)
-        quantize_h(3)
-        place((2,), (1,), y_tag="arg3")
-        second_argument(4)
-        place((2,), (2,), y_tag="f1_grouped4")
-        second_slope(4)
-        place((2,), (3,), in_p_bank=True)
-        quantize_h(4)
-        place((2,), (4,), y_tag="arg4")
-        place((3, 4,), (0,))
-        place((3, 4,), (1,))
-        place((3, 4,), (2,))
-        place((3, 4,), (3,))
-        place((3, 4,), (4,))
-        place((2,), (5,))
-        add_on_vector(4)
-        place((3, 4,), (5,))
+        wide_quantize_f1(2)
+        keep_a(2, 1, acc1)
+        free_unit(*early[1])
+        wide_b(2)
+
+        last = len(CHUNKS) - 1
+        at = 2
+        for c in range(2, last):
+            keep_a(c + 1, 0, wide_f1(c + 1, 0))
+            unit_staged_in(f"f1_grouped{c}", *early[at])
+            acc1 = wide_f1(c + 1, 1)
+            h_planes = wide_h(c)
+            keep_a(c + 1, 1, acc1)
+            unit_in_b_bank(*early[at + 1])
+            wide_quantize_f1(c + 1)
+            unit_staged_in(f"arg{c}", *early[at + 2])
+            wide_b(c + 1)
+            wide_quantize_h(c, h_planes)
+            at = at + 3
+        unit_staged_in(f"f1_grouped{last}", *early[at])
+        h_planes = wide_h(last)
+        unit_in_b_bank(*early[at + 1])
+        wide_quantize_h(last, h_planes)
+        unit_staged_in(f"arg{last}", *early[at + 2])
+
+        late_chunks = (last - 1, last)
+        for n in range(ROW_TILES - 1):
+            free_unit(late_chunks, (n,))
+        free_unit(*early[at + 3])
         add_on_tensor(0)
-        add_on_tensor(1)
-        add_on_tensor(2)
-        add_on_tensor(3)
-        add_on_vector(5)
+        for n in range(TENSOR_ADDS, ROW_TILES - 1):
+            add_on_vector(n)
+        free_unit(late_chunks, (ROW_TILES - 1,))
+        for n in range(1, TENSOR_ADDS):
+            add_on_tensor(n)
+        add_on_vector(ROW_TILES - 1)

@@ -300,12 +300,13 @@ def tile_list_core_age_slopes_kernel(tc, tab_words, tab_scales, offs, w1, w2_wor
                         stop=True,
                     )
             nc.scalar.copy(y[:, 0 : len(tiles) * width], acc[:, 0 : len(tiles) * width])
+            staged = y[:, 0 : len(tiles) * width].rearrange("p (u j) -> p u j", j=width)
+            factors = gains[:, first : first + width].unsqueeze(1).to_broadcast([P, len(tiles), width])
+            nc.gpsimd.tensor_tensor(staged, staged, factors, ALU.mult)
             for u, n in enumerate(tiles):
-                nc.vector.tensor_tensor(
+                nc.vector.tensor_copy(
                     pages[n][:].indirect(places[:, first // LIST_COLUMN : (first + width) // LIST_COLUMN]),
                     y[:, u * width : (u + 1) * width],
-                    gains[:, first : first + width],
-                    ALU.mult,
                 )
 
         def y_tile():

@@ -25,11 +25,11 @@ BANK = 512
 LIST_COLUMN = 16
 ROW_TILES = N // P
 W3_PIECE = 256
-
+HALF = H // 2
 CHUNKS = [(0, 128), (128, 128), (256, 256), (512, 256), (768, 256)]
-TENSOR_ADDS = 4
-A_BANKS, B_BANKS, Y_BANKS = 2, 2, 3
+A_BANKS, B_BANKS, Y_BANKS = 3, 2, 3
 Y_TILES = 8
+VECTOR_SHARE = 84
 
 
 def tile_list_core_age_slopes_kernel(tc, tab_words, tab_scales, offs, w1, w2_words, w2_scales, step, w3, offs2, wgo, x0, out):
@@ -42,8 +42,8 @@ def tile_list_core_age_slopes_kernel(tc, tab_words, tab_scales, offs, w1, w2_wor
         def held(shape, dtype, name):
             return keep.tile(shape, dtype, name=name, tag=name, align_bytes=64)
 
-        def a_bank():
-            return psum.tile([P, BANK], F32, name="a_bank", tag="a_bank", bufs=A_BANKS)
+        def a_bank(i):
+            return psum.tile([P, BANK], F32, name=f"a_bank{i}", tag=f"a_bank{i}", bufs=1)
 
         def b_bank():
             return psum.tile([P, BANK], F32, name="b_bank", tag="b_bank", bufs=B_BANKS)
@@ -52,7 +52,7 @@ def tile_list_core_age_slopes_kernel(tc, tab_words, tab_scales, offs, w1, w2_wor
             return psum.tile([P, BANK], F32, name="y_bank", tag="y_bank", bufs=Y_BANKS)
 
         def quantize(codes, scale, grouped):
-            nc.vector.quantize_mx(out=codes[:].bitcast(FP8X4), scales=scale[:], in_=grouped[:])
+            nc.vector.quantize_mx(out=codes.bitcast(FP8X4), scales=scale, in_=grouped)
 
         picks = held([P, S // LIST_COLUMN], U16, "picks")
         places = held([P, S // LIST_COLUMN], U16, "places")
@@ -62,28 +62,18 @@ def tile_list_core_age_slopes_kernel(tc, tab_words, tab_scales, offs, w1, w2_wor
         tab_scale = held([P, T], U8, "tab_scale")
         tab = [held([P, T], I32, f"tab{a}") for a in range(2)]
         w1_raw = [held([P, PACK, H], F32, f"w1_raw{a}") for a in range(2)]
-        w3_raw = held([P, PACK, N], F32, "w3_raw")
+        w3_pieces = range(N // W3_PIECE)
+        w3_raw = [held([P, PACK, W3_PIECE], F32, f"w3_raw{i}") for i in w3_pieces]
         gains = held([P, S], F32, "gains")
-        rows = [held([P, S], F32, f"rows{n}") for n in range(ROW_TILES)]
         ident = held([P, P], F32, "ident")
-        v_scale = held([P, S], U8, "v_scale")
+        v_scale = [held([P, S], U8, f"v_scale{a}") for a in range(2)]
         picked_scale = held([P, S], U8, "picked_scale")
 
         nc.vector.memset(tab_scale[QUADRANT : 2 * QUADRANT, :].bitcast(I32), 0)
         nc.vector.memset(tab_scale[2 * QUADRANT : P, :].bitcast(I32), 0)
-        nc.vector.memset(v_scale[:].bitcast(I32), 0)
-        nc.gpsimd.memset(w2_scale_raw[:].bitcast(I32), 0)
-
-        nc.sync.dma_start(picks[:], offs)
-        nc.sync.dma_start(tab_scale[0:QUADRANT, :].bitcast(I32), tab_scales.rearrange("a q t -> (a q) t").bitcast(I32))
-        nc.sync.dma_start(places[:], offs2)
-        nc.sync.dma_start(steps[:], step.rearrange("(p t) -> p t", t=PACK))
         for a in range(2):
-            w1_rows = w1[a * K_PASS : (a + 1) * K_PASS, :].rearrange("(p j) c -> p j c", j=PACK)
-            for j in range(0, PACK, 2):
-                nc.sync.dma_start(w1_raw[a][:, j : j + 2, :], w1_rows[:, j : j + 2, :])
-        nc.sync.dma_start(w2_raw[:].bitcast(I32), w2_words[0].bitcast(I32))
-        nc.vector.tensor_copy(picked_scale[:], tab_scale[:].indirect(picks[:]))
+            nc.vector.memset(v_scale[a][:].bitcast(I32), 0)
+        nc.gpsimd.memset(w2_scale_raw[:].bitcast(I32), 0)
 
         def load_table(a):
             nc.sync.dma_start(tab[a][:], tab_words[a].rearrange("p t i -> p (t i)").bitcast(I32))
@@ -95,63 +85,80 @@ def tile_list_core_age_slopes_kernel(tc, tab_words, tab_scales, offs, w1, w2_wor
             )
 
         def move_scales(a, quadrant):
-            first = QUADRANT * quadrant + 4 * a
+            first = QUADRANT * quadrant
             nc.sync.dma_start(
-                v_scale[first : first + 4, :].bitcast(I32),
+                v_scale[a][first : first + 4, :].bitcast(I32),
                 picked_scale[16 * a + 4 * quadrant : 16 * a + 4 * quadrant + 4, :].bitcast(I32),
             )
 
+        w1_rows = [w1[a * K_PASS : (a + 1) * K_PASS, :].rearrange("(p j) c -> p j c", j=PACK) for a in range(2)]
+        w3_rows = w3.rearrange("(p j) c -> p j c", j=PACK)
+
+        nc.sync.dma_start(picks[:], offs)
+        nc.sync.dma_start(tab_scale[0:QUADRANT, :].bitcast(I32), tab_scales.rearrange("a q t -> (a q) t").bitcast(I32))
+        nc.vector.tensor_copy(picked_scale[:], tab_scale[:].indirect(picks[:]))
+        load_table(0)
+        nc.sync.dma_start(steps[:], step.rearrange("(p t) -> p t", t=PACK))
+        nc.sync.dma_start(w2_raw[:].bitcast(I32), w2_words[0].bitcast(I32))
         for quadrant in range(3):
             load_w2_scales(quadrant)
-        load_table(0)
-        load_w2_scales(3)
-        for quadrant in range(2):
-            move_scales(0, quadrant)
         load_table(1)
-        for quadrant in range(2, 4):
+        load_w2_scales(3)
+        nc.sync.dma_start(w1_raw[0][:], w1_rows[0])
+        for quadrant in range(4):
             move_scales(0, quadrant)
+        nc.sync.dma_start(w1_raw[1][:], w1_rows[1])
         for quadrant in range(4):
             move_scales(1, quadrant)
-        nc.sync.dma_start(w3_raw[:], w3.rearrange("(p j) c -> p j c", j=PACK))
+        for i in range(2):
+            nc.sync.dma_start(w3_raw[i][:], w3_rows[:, :, i * W3_PIECE : (i + 1) * W3_PIECE])
+        nc.sync.dma_start(places[:], offs2)
         nc.sync.dma_start(gains[:], wgo)
-        for n in range(ROW_TILES):
-            nc.sync.dma_start(rows[n][:], x0[n * P : (n + 1) * P, :])
+        nc.sync.dma_start(w3_raw[2][:], w3_rows[:, :, 2 * W3_PIECE : 3 * W3_PIECE])
         make_identity(nc, ident[:])
 
+        v_codes = [held([P, S], U32, f"v_codes{a}") for a in range(2)]
+        nc.vector.tensor_copy(v_codes[0][:], tab[0][:].bitcast(U32).indirect(picks[:]))
         w2_codes = held([P, 2 * H], U8, "w2_codes")
         w2_scale = held([P, H], U8, "w2_scale")
         nc.vector.tensor_copy(
             w2_codes[:].rearrange("p (t m b) -> p t m b", t=PACK, b=2),
             w2_raw[:].rearrange("p (m t b) -> p t m b", t=PACK, b=2),
         )
-
-        w1_codes = [held([P, H], U32, f"w1_codes{a}") for a in range(2)]
-        w1_scale = [held([P, H], U8, f"w1_scale{a}") for a in range(2)]
-        w1_grouped = [held([P, PACK * H], BF16, f"w1_grouped{a}") for a in range(2)]
-        for a in range(2):
-            nc.vector.tensor_copy(
-                w1_grouped[a][:].rearrange("p (t m j) -> p m j t", t=PACK, j=PACK),
-                w1_raw[a][:].rearrange("p j (m t) -> p m j t", t=PACK),
-            )
-        for a in range(2):
-            quantize(w1_codes[a], w1_scale[a], w1_grouped[a])
-
-        v_codes0 = held([P, S], U32, "v_codes0")
-        v_codes1 = [held([P, S // 2], U32, f"v_codes1_{half}") for half in range(2)]
-        nc.vector.tensor_copy(v_codes0[:], tab[0][:].bitcast(U32).indirect(picks[:]))
+        step_row = held([P, P, PACK], F32, "step_row")
+        nc.vector.tensor_copy(step_row[:], steps[:].unsqueeze(1).to_broadcast([P, P, PACK]))
+        nc.vector.tensor_copy(v_codes[1][:], tab[1][:].bitcast(U32).indirect(picks[:]))
         nc.vector.tensor_copy(
             w2_scale[:].rearrange("p (t m) -> p t m", t=PACK),
             w2_scale_raw[:].rearrange("p (m t) -> p t m", t=PACK),
         )
-        half_list = S // 2 // LIST_COLUMN
-        for half in range(2):
-            nc.vector.tensor_copy(v_codes1[half][:], tab[1][:].bitcast(U32).indirect(picks[:, half_list * half : half_list * (half + 1)]))
 
-        def group(engine_copy, grouped, planes):
-            engine_copy(
-                grouped.rearrange("p (c i t) -> p c t i", i=4, t=PACK),
-                planes.rearrange("p t (c i) -> p c t i", i=4),
-            )
+        rows_low = held([P, 4, S], F32, "tab0")
+        rows_high = held([P, 2, S], F32, "tab1")
+        rows = [rows_low[:, n, :] for n in range(4)] + [rows_high[:, n, :] for n in range(2)]
+        for n in range(ROW_TILES):
+            nc.sync.dma_start(rows[n], x0[n * P : (n + 1) * P, :])
+
+        w1_codes = [held([P, H], U32, f"w1_codes{a}") for a in range(2)]
+        w1_scale = [held([P, H], U8, f"w1_scale{a}") for a in range(2)]
+        w1_grouped = [held([P, PACK * H], BF16, f"w1_grouped{a}") for a in range(2)]
+
+        for a in range(2):
+            grouped = w1_grouped[a][:].rearrange("p (t m j) -> p m j t", t=PACK, j=PACK)
+            source = w1_raw[a][:].rearrange("p j (m t) -> p m j t", t=PACK)
+            for pair in range(2):
+                ts = slice(2 * pair, 2 * pair + 2)
+                nc.vector.tensor_copy(grouped[:, 0:VECTOR_SHARE, :, ts], source[:, 0:VECTOR_SHARE, :, ts])
+                nc.scalar.copy(grouped[:, VECTOR_SHARE:P, :, ts], source[:, VECTOR_SHARE:P, :, ts])
+            for pair in range(2):
+                cols = slice(pair * HALF, (pair + 1) * HALF)
+                quantize(w1_codes[a][:, cols], w1_scale[a][:, cols], w1_grouped[a][:, PACK * cols.start : PACK * cols.stop])
+
+        def woven(grouped):
+            return grouped.rearrange("p (c i t) -> p c t i", i=4, t=PACK)
+
+        def by_fours(planes):
+            return planes.rearrange("p t (c i) -> p c t i", i=4)
 
         def as_planes(tile):
             return tile[:].rearrange("p (t j) -> p t j", t=PACK)
@@ -162,28 +169,47 @@ def tile_list_core_age_slopes_kernel(tc, tab_words, tab_scales, offs, w1, w2_wor
         def as_grouped(tile):
             return tile[:].rearrange("p (j t) -> p j t", t=PACK)
 
-        w3_pieces = range(N // W3_PIECE)
         w3_codes = [held([P, W3_PIECE], U32, f"w3_codes{i}") for i in w3_pieces]
         w3_scale = [held([P, W3_PIECE], U8, f"w3_scale{i}") for i in w3_pieces]
         w3_grouped = [held([P, PACK * W3_PIECE], BF16, f"w3_grouped{i}") for i in w3_pieces]
 
+        def gpsimd_copy(dst, src):
+            nc.gpsimd.tensor_scalar(dst, src, 1.0, 0.0, ALU.mult, ALU.add)
+
         def cast_w3(i, engine_copy):
-            group(engine_copy, w3_grouped[i][:], w3_raw[:, :, i * W3_PIECE : (i + 1) * W3_PIECE])
+            engine_copy(woven(w3_grouped[i][:]), by_fours(w3_raw[i][:]))
 
         def quantize_w3(i):
-            quantize(w3_codes[i], w3_scale[i], w3_grouped[i])
+            quantize(w3_codes[i][:], w3_scale[i][:], w3_grouped[i][:])
 
         def chunk_tiles(dtype, pack, name):
             return [held([P, pack * width], dtype, f"{name}{c}") for c, (first, width) in enumerate(CHUNKS)]
 
         slope = chunk_tiles(F32, PACK, "slope")
         arg = chunk_tiles(F32, PACK, "arg")
-        f1_grouped = chunk_tiles(BF16, PACK, "f1_grouped")
-        f1_codes = chunk_tiles(U32, 1, "f1_codes")
-        f1_scale = chunk_tiles(U8, 1, "f1_scale")
-        h_grouped = chunk_tiles(BF16, PACK, "h_grouped")
-        h_codes = chunk_tiles(U32, 1, "h_codes")
-        h_scale = chunk_tiles(U8, 1, "h_scale")
+        f1_grouped, f1_codes, f1_scale, h_grouped, h_codes, h_scale = {}, {}, {}, {}, {}, {}
+        batches = {}
+
+        def batch(name, members, tag=None, grouped=None):
+            width = sum(CHUNKS[c][1] for kind, c in members)
+            if grouped is None:
+                grouped = held([P, PACK * width], BF16, tag or f"{name}_grouped")[:]
+            codes = held([P, width], U32, f"{name}_codes")
+            scale = held([P, width], U8, f"{name}_scale")
+            at = 0
+            for kind, c in members:
+                cols = slice(at, at + CHUNKS[c][1])
+                views = (f1_grouped, f1_codes, f1_scale) if kind == "f1" else (h_grouped, h_codes, h_scale)
+                views[0][c] = grouped[:, PACK * cols.start : PACK * cols.stop]
+                views[1][c] = codes[:, cols]
+                views[2][c] = scale[:, cols]
+                at = cols.stop
+            batches[name] = (codes, scale, grouped)
+
+        def quantize_batch(name):
+            codes, scale, grouped = batches[name]
+            quantize(codes[:], scale[:], grouped)
+
         pages = [held([P, S], F32, f"page{n}") for n in range(ROW_TILES)]
 
         def bank_planes(c, b):
@@ -197,8 +223,6 @@ def tile_list_core_age_slopes_kernel(tc, tab_words, tab_scales, offs, w1, w2_wor
         def w1_product(acc, c, b, close):
             first, width = CHUNKS[c]
             samples = slice(first, first + width)
-            half, in_half = divmod(first, S // 2)
-            moving = [v_codes0[:, samples], v_codes1[half][:, in_half : in_half + width]]
             planes = bank_planes(c, b)
             for a in range(2):
                 for u, (t, cols) in enumerate(planes):
@@ -206,8 +230,8 @@ def tile_list_core_age_slopes_kernel(tc, tab_words, tab_scales, offs, w1, w2_wor
                         out=acc[:, cols],
                         lhsT=w1_codes[a][:, t * P : (t + 1) * P].bitcast(FP8X4),
                         lhsT_scale=w1_scale[a][:, t * P : (t + 1) * P],
-                        rhs=moving[a].bitcast(FP8X4),
-                        rhs_scale=v_scale[4 * a : P, samples],
+                        rhs=v_codes[a][:, samples].bitcast(FP8X4),
+                        rhs_scale=v_scale[a][:, samples],
                         start=(a == 0 and u == 0),
                         stop=(close and a == 1 and u == len(planes) - 1),
                     )
@@ -219,73 +243,70 @@ def tile_list_core_age_slopes_kernel(tc, tab_words, tab_scales, offs, w1, w2_wor
                     out=acc[:, cols],
                     lhsT=w2_codes[:, 2 * t * P : 2 * (t + 1) * P].bitcast(FP4X4),
                     lhsT_scale=w2_scale[:, t * P : (t + 1) * P],
-                    rhs=f1_codes[c][:].bitcast(FP8X4),
-                    rhs_scale=f1_scale[c][:],
+                    rhs=f1_codes[c].bitcast(FP8X4),
+                    rhs_scale=f1_scale[c],
                     start=not onto_a,
                     stop=(not onto_a or u == len(planes) - 1),
                 )
 
-        def times_step(grouped, values, c):
-            repeated = steps[:].unsqueeze(1).to_broadcast([P, CHUNKS[c][1], PACK])
-            nc.vector.tensor_tensor(as_grouped(grouped), as_grouped(values), repeated, ALU.mult)
+        def times_step(engine, grouped, values):
+            engine.tensor_tensor(grouped, values, step_row[:].rearrange("p j t -> p (j t)")[:, 0 : values.shape[1]], ALU.mult)
 
-        def narrow_f1(c):
-            acc = a_bank()
-            w1_product(acc, c, 0, close=True)
-            nc.scalar.activation(as_grouped(slope[c]), planes_by_sample(acc), ACT.Tanh)
-            times_step(f1_grouped[c], slope[c], c)
-            quantize(f1_codes[c], f1_scale[c], f1_grouped[c])
-            return acc
+        def tanh_in_halves(target, acc):
+            for half in range(2):
+                samples = slice(half * P // 2, (half + 1) * P // 2)
+                nc.scalar.activation(as_grouped(target)[:, samples], planes_by_sample(acc)[:, samples], ACT.Tanh)
 
-        def narrow_h(c):
-            nc.vector.tensor_tensor(arg[c][:], arg[c][:], slope[c][:], ALU.add)
-            times_step(h_grouped[c], arg[c], c)
-            quantize(h_codes[c], h_scale[c], h_grouped[c])
+        halves = [slice(0, BANK // 2), slice(BANK // 2, BANK)]
 
-        def wide_f1(c, b):
-            acc = a_bank()
-            w1_product(acc, c, b, close=True)
-            nc.scalar.activation(slope[c][:, bank_span(b)], acc[:], ACT.Tanh)
+        def banks(c):
+            return range(PACK * CHUNKS[c][1] // BANK)
+
+        def scale_planes(tile, c, b):
             for t, cols in bank_planes(c, b):
-                plane = as_planes(slope[c])[:, t, :]
+                plane = as_planes(tile)[:, t, :]
                 nc.scalar.activation(plane, plane, ACT.Copy, scale=steps[:, t : t + 1])
-            return acc
 
-        def keep_a(c, b, acc):
-            nc.scalar.copy(arg[c][:, bank_span(b)], acc[:])
+        def first_slope(c, names):
+            accs = []
+            for b in banks(c):
+                acc = a_bank(names[b])
+                w1_product(acc, c, b, close=True)
+                nc.scalar.activation(slope[c][:, bank_span(b)], acc[:], ACT.Tanh)
+                scale_planes(slope[c], c, b)
+                accs.append(acc)
+            nc.scalar.copy(woven(f1_grouped[c]), by_fours(as_planes(slope[c])))
+            return accs
 
-        def wide_quantize_f1(c):
-            group(nc.scalar.copy, f1_grouped[c][:], as_planes(slope[c]))
-            quantize(f1_codes[c], f1_scale[c], f1_grouped[c])
+        def keep_a(c, accs):
+            for b in banks(c):
+                nc.scalar.copy(arg[c][:, bank_span(b)], accs[b][:])
 
-        def wide_b(c):
-            for b in range(2):
-                acc = b_bank()
+        def slope_product(c):
+            accs = [b_bank() for b in banks(c)]
+            for b, acc in enumerate(accs):
                 w2_product(acc, c, b, onto_a=False)
-                nc.vector.tensor_tensor(arg[c][:, bank_span(b)], acc[:], arg[c][:, bank_span(b)], ALU.add)
+            return accs
 
-        def wide_h(c):
-            h_planes = held([P, PACK * CHUNKS[c][1]], BF16, f"h_planes{c}")
-            for b in range(2):
-                nc.scalar.activation(arg[c][:, bank_span(b)], arg[c][:, bank_span(b)], ACT.Tanh)
-                for t, cols in bank_planes(c, b):
-                    nc.vector.scalar_tensor_tensor(
-                        as_planes(h_planes)[:, t, :],
-                        as_planes(arg[c])[:, t, :],
-                        steps[:, t : t + 1],
-                        as_planes(slope[c])[:, t, :],
-                        ALU.mult,
-                        ALU.add,
-                    )
-            return h_planes
+        def second_argument(c, b, acc, target):
+            nc.vector.tensor_tensor(target[:, bank_span(b)], acc[:], arg[c][:, bank_span(b)], ALU.add)
 
-        def wide_quantize_h(c, h_planes):
-            group(nc.scalar.copy, h_grouped[c][:], as_planes(h_planes))
-            quantize(h_codes[c], h_scale[c], h_grouped[c])
+        def second_slope(c, target):
+            for b in banks(c):
+                nc.scalar.activation(target[:, bank_span(b)], target[:, bank_span(b)], ACT.Tanh)
+                scale_planes(target, c, b)
+            nc.gpsimd.tensor_tensor(woven(h_grouped[c]), by_fours(as_planes(target)), by_fours(as_planes(slope[c])), ALU.add)
 
-        def unit(chunks, tiles, acc, y):
+        def y_tile():
+            return ring.tile([P, BANK], F32, name="y", tag="y", bufs=Y_TILES)
+
+        def pieces(ap, count, width):
+            return ap[:, 0 : count * width].rearrange("p (u j) -> p u j", j=width)
+
+        def product(chunks, tiles, on_vector=False, into=None, y=None, acc=None):
             first = CHUNKS[chunks[0]][0]
             width = sum(CHUNKS[c][1] for c in chunks)
+            acc = acc if acc is not None else y_bank()
             for u, n in enumerate(tiles):
                 i, in_piece = divmod(n * P, W3_PIECE)
                 for c in chunks:
@@ -294,122 +315,145 @@ def tile_list_core_age_slopes_kernel(tc, tab_words, tab_scales, offs, w1, w2_wor
                         out=acc[:, column : column + CHUNKS[c][1]],
                         lhsT=w3_codes[i][:, in_piece : in_piece + P].bitcast(FP8X4),
                         lhsT_scale=w3_scale[i][:, in_piece : in_piece + P],
-                        rhs=h_codes[c][:].bitcast(FP8X4),
-                        rhs_scale=h_scale[c][:],
+                        rhs=h_codes[c].bitcast(FP8X4),
+                        rhs_scale=h_scale[c],
                         start=True,
                         stop=True,
                     )
-            nc.scalar.copy(y[:, 0 : len(tiles) * width], acc[:, 0 : len(tiles) * width])
-            staged = y[:, 0 : len(tiles) * width].rearrange("p (u j) -> p u j", j=width)
             factors = gains[:, first : first + width].unsqueeze(1).to_broadcast([P, len(tiles), width])
-            nc.gpsimd.tensor_tensor(staged, staged, factors, ALU.mult)
+            if on_vector:
+                nc.vector.tensor_tensor(into, pieces(acc[:], len(tiles), width), factors, ALU.mult)
+                return first, width, tiles, into
+            y = y if y is not None else y_tile()[:]
+            nc.scalar.copy(y[:, 0 : len(tiles) * width], acc[:, 0 : len(tiles) * width])
+            plain = pieces(y, len(tiles), width)
+            into = into if into is not None else plain
+            nc.gpsimd.tensor_tensor(into, plain, factors, ALU.mult)
+            return first, width, tiles, into
+
+        def scatter(first, width, tiles, staged):
             for u, n in enumerate(tiles):
                 nc.vector.tensor_copy(
                     pages[n][:].indirect(places[:, first // LIST_COLUMN : (first + width) // LIST_COLUMN]),
-                    y[:, u * width : (u + 1) * width],
+                    staged[:, u, :],
                 )
 
-        def y_tile():
-            return ring.tile([P, BANK], F32, name="y", tag="y", bufs=Y_TILES)
+        def unit(chunks, tiles, **where):
+            scatter(*product(chunks, tiles, **where))
 
-        def free_unit(chunks, tiles):
-            unit(chunks, tiles, y_bank(), y_tile())
+        def add_on_gpsimd(n, cols, target):
+            nc.gpsimd.tensor_tensor(target[:, cols], pages[n][:, cols], rows[n][:, cols], ALU.add)
+            nc.sync.dma_start(out[n * P : (n + 1) * P, cols], target[:, cols])
 
-        def unit_staged_in(name, chunks, tiles):
-            unit(chunks, tiles, y_bank(), held([P, BANK], F32, name))
-
-        def unit_in_b_bank(chunks, tiles):
-            unit(chunks, tiles, b_bank(), y_tile())
-
-        def add_on_tensor(n):
-            blocks = BANK // P
-            for half in range(S // BANK):
-                turned_acc = a_bank()
-                turned = ring.tile([P, BANK], F32, name="turned", tag="turned", bufs=2)
-                for opens, source in ((True, rows[n]), (False, pages[n])):
-                    for u in range(blocks):
-                        nc.tensor.matmul(
-                            turned_acc[:, u * P : (u + 1) * P],
-                            source[:, half * BANK + u * P : half * BANK + (u + 1) * P],
-                            ident[:],
-                            is_transpose=True,
-                            start=(opens and u == 0),
-                            stop=(not opens and u == blocks - 1),
-                        )
-                nc.scalar.copy(turned[:], turned_acc[:])
-                back_acc = b_bank()
+        def add_on_tensor(n, first, blocks, turned_acc):
+            span = slice(0, blocks * P)
+            cols = slice(first, first + blocks * P)
+            turned = ring.tile([P, BANK], F32, name="turned", tag="turned", bufs=2)
+            for opens, source in ((True, rows[n]), (False, pages[n][:])):
                 for u in range(blocks):
-                    nc.tensor.transpose(back_acc[:, u * P : (u + 1) * P], turned[:, u * P : (u + 1) * P], ident[:])
-                nc.scalar.copy(rows[n][:, bank_span(half)], back_acc[:])
-            nc.scalar.dma_start(out[n * P : (n + 1) * P, :], rows[n][:])
+                    nc.tensor.matmul(
+                        turned_acc[:, u * P : (u + 1) * P],
+                        source[:, first + u * P : first + (u + 1) * P],
+                        ident[:],
+                        is_transpose=True,
+                        start=(opens and u == 0),
+                        stop=(not opens and u == blocks - 1),
+                    )
+            nc.scalar.copy(turned[:, span], turned_acc[:, span])
+            back_acc = b_bank()
+            for u in range(blocks):
+                nc.tensor.transpose(back_acc[:, u * P : (u + 1) * P], turned[:, u * P : (u + 1) * P], ident[:])
+            nc.scalar.copy(rows[n][:, cols], back_acc[:, span])
+            nc.scalar.dma_start(out[n * P : (n + 1) * P, cols], rows[n][:, cols])
 
-        def add_on_vector(n):
+        def add_on_vector(n, target):
             for half in range(S // BANK):
                 cols = bank_span(half)
-                nc.vector.tensor_tensor(rows[n][:, cols], pages[n][:, cols], rows[n][:, cols], ALU.add)
-                nc.sync.dma_start(out[n * P : (n + 1) * P, cols], rows[n][:, cols])
+                nc.vector.tensor_tensor(target[:, cols], pages[n][:, cols], rows[n][:, cols], ALU.add)
+                nc.sync.dma_start(out[n * P : (n + 1) * P, cols], target[:, cols])
 
-        early = [((c,), (n, n + 1)) for c in (0, 1) for n in range(0, ROW_TILES, 2)]
-        early = early + [((2,), (n,)) for n in range(ROW_TILES)]
-
-        narrow_f1(0)
+        batch("f0", [("f1", 0)])
+        batch("h0", [("h", 0)])
+        batch("f1", [("f1", 1)])
+        batch("h1f2", [("h", 1), ("f1", 2)])
+        batch("h2f3", [("h", 2), ("f1", 3)])
+        batch("h3f4", [("h", 3), ("f1", 4)])
+        batch("h4", [("h", 4)])
+        acc = a_bank(0)
+        w1_product(acc, 0, 0, close=True)
+        nc.scalar.activation(as_grouped(slope[0]), planes_by_sample(acc), ACT.Tanh)
+        times_step(nc.vector, f1_grouped[0], slope[0][:])
+        quantize_batch("f0")
         acc = b_bank()
         w1_product(acc, 0, 0, close=False)
         w2_product(acc, 0, 0, onto_a=True)
-        cast_w3(0, nc.vector.tensor_copy)
         nc.scalar.activation(as_grouped(arg[0]), planes_by_sample(acc), ACT.Tanh)
-        narrow_h(0)
+        nc.vector.tensor_tensor(arg[0][:], arg[0][:], slope[0][:], ALU.add)
+        times_step(nc.vector, h_grouped[0], arg[0][:])
+        quantize_batch("h0")
+        cast_w3(0, nc.vector.tensor_copy)
         quantize_w3(0)
-        free_unit(*early[0])
-
-        acc = narrow_f1(1)
+        wide = held([P, 2 * BANK + P], F32, "wide")
+        arg[1] = wide[:, 0:BANK]
+        acc = a_bank(1)
+        w1_product(acc, 1, 0, close=True)
+        nc.scalar.activation(as_grouped(slope[1]), planes_by_sample(acc), ACT.Tanh)
+        times_step(nc.vector, f1_grouped[1], slope[1][:])
+        quantize_batch("f1")
         nc.scalar.copy(as_grouped(arg[1]), planes_by_sample(acc))
         acc = b_bank()
         w2_product(acc, 1, 0, onto_a=False)
         nc.vector.tensor_tensor(as_grouped(arg[1]), planes_by_sample(acc), as_grouped(arg[1]), ALU.add)
+        nc.scalar.activation(arg[1][:], arg[1][:], ACT.Tanh)
+        nc.vector.tensor_tensor(arg[1][:], arg[1][:], slope[1][:], ALU.add)
+        times_step(nc.vector, h_grouped[1], arg[1][:])
+        w3_grouped[1] = held([P, PACK * W3_PIECE], BF16, "f0_grouped")
         cast_w3(1, nc.vector.tensor_copy)
         quantize_w3(1)
-        nc.scalar.activation(arg[1][:], arg[1][:], ACT.Tanh)
-        narrow_h(1)
-
-        acc0 = wide_f1(2, 0)
-        acc1 = wide_f1(2, 1)
-        keep_a(2, 0, acc0)
-        cast_w3(2, nc.scalar.copy)
+        accs = first_slope(2, (2, 0))
+        quantize_batch("h1f2")
+        unit((0,), (0, 1), on_vector=True, into=wide[:].rearrange("p (u j) -> p u j", j=P)[:, 0:9:8, :])
+        keep_a(2, accs)
+        cast_w3(2, nc.vector.tensor_copy)
         quantize_w3(2)
-        wide_quantize_f1(2)
-        keep_a(2, 1, acc1)
-        free_unit(*early[1])
-        wide_b(2)
-
-        last = len(CHUNKS) - 1
-        at = 2
-        for c in range(2, last):
-            keep_a(c + 1, 0, wide_f1(c + 1, 0))
-            unit_staged_in(f"f1_grouped{c}", *early[at])
-            acc1 = wide_f1(c + 1, 1)
-            h_planes = wide_h(c)
-            keep_a(c + 1, 1, acc1)
-            unit_in_b_bank(*early[at + 1])
-            wide_quantize_f1(c + 1)
-            unit_staged_in(f"arg{c}", *early[at + 2])
-            wide_b(c + 1)
-            wide_quantize_h(c, h_planes)
-            at = at + 3
-        unit_staged_in(f"f1_grouped{last}", *early[at])
-        h_planes = wide_h(last)
-        unit_in_b_bank(*early[at + 1])
-        wide_quantize_h(last, h_planes)
-        unit_staged_in(f"arg{last}", *early[at + 2])
-
-        late_chunks = (last - 1, last)
-        for n in range(ROW_TILES - 1):
-            free_unit(late_chunks, (n,))
-        free_unit(*early[at + 3])
-        add_on_tensor(0)
-        for n in range(TENSOR_ADDS, ROW_TILES - 1):
-            add_on_vector(n)
-        free_unit(late_chunks, (ROW_TILES - 1,))
-        for n in range(1, TENSOR_ADDS):
-            add_on_tensor(n)
-        add_on_vector(ROW_TILES - 1)
+        accs = slope_product(2)
+        second_argument(2, 0, accs[0], wide)
+        late = product((0,), (2,), on_vector=True, into=wide[:, 2 * BANK : 2 * BANK + P].unsqueeze(1))
+        second_argument(2, 1, accs[1], wide)
+        scatter(*late)
+        unit((0,), (3, 4, 5), into=pieces(arg[2][:, 0:BANK], 3, P), acc=a_bank(1))
+        unit((1,), (0, 1), y=f1_grouped[3].bitcast(F32), into=pieces(y_tile()[:], 2, P))
+        unit((1,), (2, 3), y=h_grouped[2].bitcast(F32), into=pieces(y_tile()[:], 2, P))
+        second_slope(2, wide[:, 0 : 2 * BANK])
+        keep_a(3, first_slope(3, (2, 0)))
+        unit((1,), (4, 5), into=pieces(slope[2][:], 2, BANK)[:, :, 0:P], acc=a_bank(0))
+        quantize_batch("h2f3")
+        unit((2,), (0,))
+        for b, acc in enumerate(slope_product(3)):
+            second_argument(3, b, acc, slope[2])
+        unit((2,), (1,))
+        unit((2,), (2, 3))
+        second_slope(3, slope[2][:])
+        keep_a(4, first_slope(4, (1, 2)))
+        unit((2,), (4,), into=pieces(slope[3][:], 1, 2 * P), acc=a_bank(2))
+        quantize_batch("h3f4")
+        unit((3,), (0,))
+        for b, acc in enumerate(slope_product(4)):
+            second_argument(4, b, acc, slope[3])
+        unit((3,), (1, 2))
+        second_slope(4, slope[3][:])
+        unit((2,), (5,), into=pieces(arg[4][:], 1, 2 * P))
+        unit((3,), (3,), into=pieces(slope[4][:], 1, 2 * P))
+        quantize_batch("h4")
+        unit((3,), (4,), into=pieces(held([P, BANK], F32, "h4_grouped")[:], 1, 2 * P))
+        unit((4,), (0, 1))
+        unit((4,), (2, 3))
+        unit((4,), (4,))
+        unit((3, 4), (5,))
+        for half in range(2):
+            add_on_tensor(0, half * BANK, 4, a_bank(half))
+        for n, acc in ((1, a_bank(2)), (2, y_bank()), (3, y_bank())):
+            add_on_gpsimd(n, slice(0, 5 * P), rows[n])
+            add_on_tensor(n, 5 * P, 3, acc)
+        add_on_gpsimd(4, slice(0, S), held([P, S], F32, "sum4")[:])
+        add_on_vector(5, rows[4])

@@ -42,14 +42,8 @@ def tile_list_core_age_slopes_kernel(tc, tab_words, tab_scales, offs, w1, w2_wor
         def held(shape, dtype, name):
             return keep.tile(shape, dtype, name=name, tag=name, align_bytes=64)
 
-        def a_bank(i):
-            return psum.tile([P, BANK], F32, name=f"a_bank{i}", tag=f"a_bank{i}", bufs=1)
-
-        def b_bank():
-            return psum.tile([P, BANK], F32, name="b_bank", tag="b_bank", bufs=B_BANKS)
-
-        def y_bank():
-            return psum.tile([P, BANK], F32, name="y_bank", tag="y_bank", bufs=Y_BANKS)
+        def bank(i):
+            return psum.tile([P, BANK], F32, name=f"bank{i}", tag=f"bank{i}", bufs=1)
 
         def quantize(codes, scale, grouped):
             nc.vector.quantize_mx(out=codes.bitcast(FP8X4), scales=scale, in_=grouped)
@@ -270,20 +264,22 @@ def tile_list_core_age_slopes_kernel(tc, tab_words, tab_scales, offs, w1, w2_wor
         def first_slope(c, names):
             accs = []
             for b in banks(c):
-                acc = a_bank(names[b])
+                acc = bank(names[b])
                 w1_product(acc, c, b, close=True)
                 nc.scalar.activation(slope[c][:, bank_span(b)], acc[:], ACT.Tanh)
                 scale_planes(slope[c], c, b)
                 accs.append(acc)
-            nc.scalar.copy(woven(f1_grouped[c]), by_fours(as_planes(slope[c])))
             return accs
+
+        def group_f1(c):
+            nc.scalar.copy(woven(f1_grouped[c]), by_fours(as_planes(slope[c])))
 
         def keep_a(c, accs):
             for b in banks(c):
                 nc.scalar.copy(arg[c][:, bank_span(b)], accs[b][:])
 
         def slope_product(c):
-            accs = [b_bank() for b in banks(c)]
+            accs = [bank(3 + b) for b in banks(c)]
             for b, acc in enumerate(accs):
                 w2_product(acc, c, b, onto_a=False)
             return accs
@@ -303,10 +299,9 @@ def tile_list_core_age_slopes_kernel(tc, tab_words, tab_scales, offs, w1, w2_wor
         def pieces(ap, count, width):
             return ap[:, 0 : count * width].rearrange("p (u j) -> p u j", j=width)
 
-        def product(chunks, tiles, on_vector=False, into=None, y=None, acc=None):
+        def stage(chunks, tiles, acc, into=None):
             first = CHUNKS[chunks[0]][0]
             width = sum(CHUNKS[c][1] for c in chunks)
-            acc = acc if acc is not None else y_bank()
             for u, n in enumerate(tiles):
                 i, in_piece = divmod(n * P, W3_PIECE)
                 for c in chunks:
@@ -320,35 +315,32 @@ def tile_list_core_age_slopes_kernel(tc, tab_words, tab_scales, offs, w1, w2_wor
                         start=True,
                         stop=True,
                     )
-            factors = gains[:, first : first + width].unsqueeze(1).to_broadcast([P, len(tiles), width])
-            if on_vector:
-                nc.vector.tensor_tensor(into, pieces(acc[:], len(tiles), width), factors, ALU.mult)
-                return first, width, tiles, into
-            y = y if y is not None else y_tile()[:]
-            nc.scalar.copy(y[:, 0 : len(tiles) * width], acc[:, 0 : len(tiles) * width])
-            plain = pieces(y, len(tiles), width)
-            into = into if into is not None else plain
-            nc.gpsimd.tensor_tensor(into, plain, factors, ALU.mult)
-            return first, width, tiles, into
+            staged = into if into is not None else pieces(y_tile()[:], len(tiles), width)
+            nc.scalar.copy(staged, pieces(acc[:], len(tiles), width))
+            return first, width, tiles, staged
 
-        def scatter(first, width, tiles, staged):
+        def window(n, first, width):
+            return pages[n][:].indirect(places[:, first // LIST_COLUMN : (first + width) // LIST_COLUMN])
+
+        def place_fused(first, width, tiles, staged):
             for u, n in enumerate(tiles):
-                nc.vector.tensor_copy(
-                    pages[n][:].indirect(places[:, first // LIST_COLUMN : (first + width) // LIST_COLUMN]),
-                    staged[:, u, :],
-                )
+                nc.vector.tensor_tensor(window(n, first, width), staged[:, u, :], gains[:, first : first + width], ALU.mult)
 
-        def unit(chunks, tiles, **where):
-            scatter(*product(chunks, tiles, **where))
+        def place(first, width, tiles, staged, into=None):
+            factors = gains[:, first : first + width].unsqueeze(1).to_broadcast([P, len(tiles), width])
+            into = into if into is not None else staged
+            nc.gpsimd.tensor_tensor(into, staged, factors, ALU.mult)
+            for u, n in enumerate(tiles):
+                nc.vector.tensor_copy(window(n, first, width), into[:, u, :])
 
         def add_on_gpsimd(n, cols, target):
             nc.gpsimd.tensor_tensor(target[:, cols], pages[n][:, cols], rows[n][:, cols], ALU.add)
             nc.sync.dma_start(out[n * P : (n + 1) * P, cols], target[:, cols])
 
-        def add_on_tensor(n, first, blocks, turned_acc):
+        def add_on_tensor(n, first, blocks, turned_acc, back_acc, target):
             span = slice(0, blocks * P)
             cols = slice(first, first + blocks * P)
-            turned = ring.tile([P, BANK], F32, name="turned", tag="turned", bufs=2)
+            turned = ring.tile([P, BANK], F32, name="turned", tag="turned", bufs=3)
             for opens, source in ((True, rows[n]), (False, pages[n][:])):
                 for u in range(blocks):
                     nc.tensor.matmul(
@@ -360,11 +352,10 @@ def tile_list_core_age_slopes_kernel(tc, tab_words, tab_scales, offs, w1, w2_wor
                         stop=(not opens and u == blocks - 1),
                     )
             nc.scalar.copy(turned[:, span], turned_acc[:, span])
-            back_acc = b_bank()
             for u in range(blocks):
                 nc.tensor.transpose(back_acc[:, u * P : (u + 1) * P], turned[:, u * P : (u + 1) * P], ident[:])
-            nc.scalar.copy(rows[n][:, cols], back_acc[:, span])
-            nc.scalar.dma_start(out[n * P : (n + 1) * P, cols], rows[n][:, cols])
+            nc.scalar.copy(target[:, cols], back_acc[:, span])
+            nc.scalar.dma_start(out[n * P : (n + 1) * P, cols], target[:, cols])
 
         def add_on_vector(n, target):
             for half in range(S // BANK):
@@ -373,87 +364,98 @@ def tile_list_core_age_slopes_kernel(tc, tab_words, tab_scales, offs, w1, w2_wor
                 nc.sync.dma_start(out[n * P : (n + 1) * P, cols], target[:, cols])
 
         batch("f0", [("f1", 0)])
-        batch("h0", [("h", 0)])
         batch("f1", [("f1", 1)])
-        batch("h1f2", [("h", 1), ("f1", 2)])
+        batch("h1", [("h", 1)])
+        batch("h0f2", [("h", 0), ("f1", 2)])
         batch("h2f3", [("h", 2), ("f1", 3)])
         batch("h3f4", [("h", 3), ("f1", 4)])
         batch("h4", [("h", 4)])
-        acc = a_bank(0)
-        w1_product(acc, 0, 0, close=True)
-        nc.scalar.activation(as_grouped(slope[0]), planes_by_sample(acc), ACT.Tanh)
+        arg[0] = arg[2][:, 0:BANK]
+        arg[1] = arg[2][:, BANK : 2 * BANK]
+        kept = bank(0)
+        w1_product(kept, 0, 0, close=True)
+        nc.scalar.activation(as_grouped(slope[0]), planes_by_sample(kept), ACT.Tanh)
         times_step(nc.vector, f1_grouped[0], slope[0][:])
         quantize_batch("f0")
-        acc = b_bank()
-        w1_product(acc, 0, 0, close=False)
-        w2_product(acc, 0, 0, onto_a=True)
-        nc.scalar.activation(as_grouped(arg[0]), planes_by_sample(acc), ACT.Tanh)
-        nc.vector.tensor_tensor(arg[0][:], arg[0][:], slope[0][:], ALU.add)
-        times_step(nc.vector, h_grouped[0], arg[0][:])
-        quantize_batch("h0")
-        cast_w3(0, nc.vector.tensor_copy)
-        quantize_w3(0)
-        wide = held([P, 2 * BANK + P], F32, "wide")
-        arg[1] = wide[:, 0:BANK]
-        acc = a_bank(1)
+        acc = bank(1)
         w1_product(acc, 1, 0, close=True)
         nc.scalar.activation(as_grouped(slope[1]), planes_by_sample(acc), ACT.Tanh)
+        nc.scalar.copy(as_grouped(arg[0]), planes_by_sample(kept))
+        acc = bank(4)
+        w2_product(acc, 0, 0, onto_a=False)
+        nc.vector.tensor_tensor(as_grouped(arg[0]), planes_by_sample(acc), as_grouped(arg[0]), ALU.add)
+        nc.scalar.activation(arg[0][:], arg[0][:], ACT.Tanh)
         times_step(nc.vector, f1_grouped[1], slope[1][:])
         quantize_batch("f1")
-        nc.scalar.copy(as_grouped(arg[1]), planes_by_sample(acc))
-        acc = b_bank()
-        w2_product(acc, 1, 0, onto_a=False)
-        nc.vector.tensor_tensor(as_grouped(arg[1]), planes_by_sample(acc), as_grouped(arg[1]), ALU.add)
-        nc.scalar.activation(arg[1][:], arg[1][:], ACT.Tanh)
+        acc = bank(3)
+        w1_product(acc, 1, 0, close=False)
+        w2_product(acc, 1, 0, onto_a=True)
+        nc.scalar.activation(as_grouped(arg[1]), planes_by_sample(acc), ACT.Tanh)
         nc.vector.tensor_tensor(arg[1][:], arg[1][:], slope[1][:], ALU.add)
         times_step(nc.vector, h_grouped[1], arg[1][:])
+        quantize_batch("h1")
+        cast_w3(2, nc.vector.tensor_copy)
+        quantize_w3(2)
+        nc.vector.tensor_tensor(arg[0][:], arg[0][:], slope[0][:], ALU.add)
+        times_step(nc.vector, h_grouped[0], arg[0][:])
+        accs = first_slope(2, (2, 6))
+        group_f1(2)
+        quantize_batch("h0f2")
+        keep_a(2, accs)
+        cast_w3(0, nc.vector.tensor_copy)
+        quantize_w3(0)
         w3_grouped[1] = held([P, PACK * W3_PIECE], BF16, "f0_grouped")
         cast_w3(1, nc.vector.tensor_copy)
         quantize_w3(1)
-        accs = first_slope(2, (2, 0))
-        quantize_batch("h1f2")
-        unit((0,), (0, 1), on_vector=True, into=wide[:].rearrange("p (u j) -> p u j", j=P)[:, 0:9:8, :])
-        keep_a(2, accs)
-        cast_w3(2, nc.vector.tensor_copy)
-        quantize_w3(2)
-        accs = slope_product(2)
-        second_argument(2, 0, accs[0], wide)
-        late = product((0,), (2,), on_vector=True, into=wide[:, 2 * BANK : 2 * BANK + P].unsqueeze(1))
-        second_argument(2, 1, accs[1], wide)
-        scatter(*late)
-        unit((0,), (3, 4, 5), into=pieces(arg[2][:, 0:BANK], 3, P), acc=a_bank(1))
-        unit((1,), (0, 1), y=f1_grouped[3].bitcast(F32), into=pieces(y_tile()[:], 2, P))
-        unit((1,), (2, 3), y=h_grouped[2].bitcast(F32), into=pieces(y_tile()[:], 2, P))
-        second_slope(2, wide[:, 0 : 2 * BANK])
-        keep_a(3, first_slope(3, (2, 0)))
-        unit((1,), (4, 5), into=pieces(slope[2][:], 2, BANK)[:, :, 0:P], acc=a_bank(0))
+        target = held([P, 2 * BANK + 4 * P], F32, "target")
+        place_fused(*stage((1,), (0, 1), bank(5), target[:, 7 * P // 2 : 21 * P // 2].rearrange("p (u j) -> p u j", j=P)[:, 0:7:6, :]))
+        for b, acc in enumerate(slope_product(2)):
+            second_argument(2, b, acc, target)
+        first, width, tiles, staged = stage((1,), (2, 3, 4, 5), bank(7))
+        place(first, width, tiles[0:2], staged[:, 0:2, :], pieces(target[:, 19 * P // 2 : 23 * P // 2], 2, P))
+        place(first, width, tiles[2:4], staged[:, 2:4, :], pieces(arg[2][:], 2, P))
+        place(*stage((0,), (0, 1), bank(2), pieces(f1_grouped[3].bitcast(F32), 2, P)), pieces(arg[2][:, 3 * P : 5 * P], 2, P))
+        place(*stage((0,), (2, 3), bank(6), pieces(h_grouped[2].bitcast(F32), 2, P)), pieces(arg[2][:, 5 * P : 7 * P], 2, P))
+        accs = first_slope(3, (0, 1))
+        second_slope(2, target[:, 0 : 2 * BANK])
+        group_f1(3)
+        place_fused(*stage((0,), (4, 5), bank(5), pieces(slope[2][:], 2, P)))
+        keep_a(3, accs)
+        accs = first_slope(4, (2, 6))
         quantize_batch("h2f3")
-        unit((2,), (0,))
+        place(*stage((2,), (0,), bank(7)))
         for b, acc in enumerate(slope_product(3)):
-            second_argument(3, b, acc, slope[2])
-        unit((2,), (1,))
-        unit((2,), (2, 3))
-        second_slope(3, slope[2][:])
-        keep_a(4, first_slope(4, (1, 2)))
-        unit((2,), (4,), into=pieces(slope[3][:], 1, 2 * P), acc=a_bank(2))
+            second_argument(3, b, acc, arg[3])
+        place(*stage((2,), (1,), bank(5)))
+        place(*stage((2,), (2, 3), bank(0)))
+        second_slope(3, arg[3][:])
+        group_f1(4)
+        place_fused(*stage((2,), (4,), bank(1), pieces(slope[3][:], 1, 2 * P)))
+        arg[4] = held([P, 2 * BANK], F32, "arg2")
+        keep_a(4, accs)
         quantize_batch("h3f4")
-        unit((3,), (0,))
+        place(*stage((3,), (0,), bank(7)))
+        target = held([P, 2 * BANK], F32, "slope2")
         for b, acc in enumerate(slope_product(4)):
-            second_argument(4, b, acc, slope[3])
-        unit((3,), (1, 2))
-        second_slope(4, slope[3][:])
-        unit((2,), (5,), into=pieces(arg[4][:], 1, 2 * P))
-        unit((3,), (3,), into=pieces(slope[4][:], 1, 2 * P))
+            second_argument(4, b, acc, target)
+        place(*stage((3,), (1, 2), bank(5)))
+        second_slope(4, target[:])
+        place(*stage((2,), (5,), bank(0)), pieces(arg[4][:], 1, 2 * P))
+        place(*stage((3,), (3,), bank(6)), pieces(slope[4][:], 1, 2 * P))
         quantize_batch("h4")
-        unit((3,), (4,), into=pieces(held([P, BANK], F32, "h4_grouped")[:], 1, 2 * P))
-        unit((4,), (0, 1))
-        unit((4,), (2, 3))
-        unit((4,), (4,))
-        unit((3, 4), (5,))
-        for half in range(2):
-            add_on_tensor(0, half * BANK, 4, a_bank(half))
-        for n, acc in ((1, a_bank(2)), (2, y_bank()), (3, y_bank())):
-            add_on_gpsimd(n, slice(0, 5 * P), rows[n])
-            add_on_tensor(n, 5 * P, 3, acc)
-        add_on_gpsimd(4, slice(0, S), held([P, S], F32, "sum4")[:])
+        place(*stage((3,), (4,), bank(7)), pieces(held([P, BANK], F32, "h4_grouped")[:], 1, 2 * P))
+        place(*stage((4,), (0,), bank(5)))
+        place(*stage((4,), (1, 2), bank(6)))
+        place(*stage((4,), (3, 4), bank(7)))
+        place(*stage((3, 4), (5,), bank(5)))
+        add_on_tensor(0, 0, 4, bank(0), bank(3), rows[0])
+        add_on_tensor(0, BANK, 4, bank(1), bank(4), rows[0])
+        add_on_gpsimd(1, slice(0, 2 * P), rows[1])
+        add_on_tensor(1, 2 * P, 4, bank(2), bank(0), rows[1])
+        add_on_tensor(1, 6 * P, 2, bank(6), bank(1), rows[1])
+        add_on_gpsimd(2, slice(0, 4 * P), rows[2])
+        add_on_tensor(2, 4 * P, 4, bank(3), bank(2), rows[2])
+        add_on_gpsimd(3, slice(0, 5 * P), rows[3])
+        add_on_tensor(3, 5 * P, 3, bank(4), bank(6), rows[3])
+        add_on_gpsimd(4, slice(0, S), held([P, S], F32, "last_sum")[:])
         add_on_vector(5, rows[4])

@@ -104,11 +104,10 @@ def tile_list_core_age_slopes_kernel(tc, tab_words, tab_scales, offs, w1, w2_wor
         nc.sync.dma_start(w1_raw[1][:], w1_rows[1])
         for quadrant in range(4):
             move_scales(1, quadrant)
-        for i in range(2):
+        for i in w3_pieces:
             nc.sync.dma_start(w3_raw[i][:], w3_rows[:, :, i * W3_PIECE : (i + 1) * W3_PIECE])
         nc.sync.dma_start(places[:], offs2)
         nc.sync.dma_start(gains[:], wgo)
-        nc.sync.dma_start(w3_raw[2][:], w3_rows[:, :, 2 * W3_PIECE : 3 * W3_PIECE])
         make_identity(nc, ident[:])
 
         v_codes = [held([P, S], U32, f"v_codes{a}") for a in range(2)]
@@ -214,10 +213,10 @@ def tile_list_core_age_slopes_kernel(tc, tab_words, tab_scales, offs, w1, w2_wor
         def bank_span(b):
             return slice(b * BANK, (b + 1) * BANK)
 
-        def w1_product(acc, c, b, close):
+        def w1_product(acc, c, b, close, count=None):
             first, width = CHUNKS[c]
             samples = slice(first, first + width)
-            planes = bank_planes(c, b)
+            planes = bank_planes(c, b)[:count]
             for a in range(2):
                 for u, (t, cols) in enumerate(planes):
                     nc.tensor.matmul_mx(
@@ -287,11 +286,18 @@ def tile_list_core_age_slopes_kernel(tc, tab_words, tab_scales, offs, w1, w2_wor
         def second_argument(c, b, acc, target):
             nc.vector.tensor_tensor(target[:, bank_span(b)], acc[:], arg[c][:, bank_span(b)], ALU.add)
 
-        def second_slope(c, target):
+        def second_tanh(target, b):
+            nc.scalar.activation(target[:, bank_span(b)], target[:, bank_span(b)], ACT.Tanh)
+
+        def finish_h(c, target):
             for b in banks(c):
-                nc.scalar.activation(target[:, bank_span(b)], target[:, bank_span(b)], ACT.Tanh)
                 scale_planes(target, c, b)
             nc.gpsimd.tensor_tensor(woven(h_grouped[c]), by_fours(as_planes(target)), by_fours(as_planes(slope[c])), ALU.add)
+
+        def second_slope(c, target):
+            for b in banks(c):
+                second_tanh(target, b)
+            finish_h(c, target)
 
         def y_tile():
             return ring.tile([P, BANK], F32, name="y", tag="y", bufs=Y_TILES)
@@ -299,7 +305,7 @@ def tile_list_core_age_slopes_kernel(tc, tab_words, tab_scales, offs, w1, w2_wor
         def pieces(ap, count, width):
             return ap[:, 0 : count * width].rearrange("p (u j) -> p u j", j=width)
 
-        def stage(chunks, tiles, acc, into=None):
+        def project(chunks, tiles, acc):
             first = CHUNKS[chunks[0]][0]
             width = sum(CHUNKS[c][1] for c in chunks)
             for u, n in enumerate(tiles):
@@ -315,6 +321,10 @@ def tile_list_core_age_slopes_kernel(tc, tab_words, tab_scales, offs, w1, w2_wor
                         start=True,
                         stop=True,
                     )
+            return first, width, tiles
+
+        def stage(chunks, tiles, acc, into=None):
+            first, width, tiles = project(chunks, tiles, acc)
             staged = into if into is not None else pieces(y_tile()[:], len(tiles), width)
             nc.scalar.copy(staged, pieces(acc[:], len(tiles), width))
             return first, width, tiles, staged
@@ -326,16 +336,21 @@ def tile_list_core_age_slopes_kernel(tc, tab_words, tab_scales, offs, w1, w2_wor
             for u, n in enumerate(tiles):
                 nc.vector.tensor_tensor(window(n, first, width), staged[:, u, :], gains[:, first : first + width], ALU.mult)
 
-        def place(first, width, tiles, staged, into=None):
+        def times_gains(first, width, tiles, staged, into=None):
             factors = gains[:, first : first + width].unsqueeze(1).to_broadcast([P, len(tiles), width])
             into = into if into is not None else staged
             nc.gpsimd.tensor_tensor(into, staged, factors, ALU.mult)
+            return first, width, tiles, into
+
+        def scatter(first, width, tiles, staged):
             for u, n in enumerate(tiles):
-                nc.vector.tensor_copy(window(n, first, width), into[:, u, :])
+                nc.vector.tensor_copy(window(n, first, width), staged[:, u, :])
+
+        def place(first, width, tiles, staged, into=None):
+            scatter(*times_gains(first, width, tiles, staged, into))
 
         def add_on_gpsimd(n, cols, target):
             nc.gpsimd.tensor_tensor(target[:, cols], pages[n][:, cols], rows[n][:, cols], ALU.add)
-            nc.sync.dma_start(out[n * P : (n + 1) * P, cols], target[:, cols])
 
         def add_on_tensor(n, first, blocks, turned_acc, back_acc, target):
             span = slice(0, blocks * P)
@@ -355,11 +370,13 @@ def tile_list_core_age_slopes_kernel(tc, tab_words, tab_scales, offs, w1, w2_wor
             for u in range(blocks):
                 nc.tensor.transpose(back_acc[:, u * P : (u + 1) * P], turned[:, u * P : (u + 1) * P], ident[:])
             nc.scalar.copy(target[:, cols], back_acc[:, span])
-            nc.scalar.dma_start(out[n * P : (n + 1) * P, cols], target[:, cols])
 
-        def add_on_vector(n, target):
-            for half in range(S // BANK):
-                cols = bank_span(half)
+        def store(queue, n, source, cols=slice(0, S)):
+            queue.dma_start(out[n * P : (n + 1) * P, cols], source[:, cols])
+
+        def add_on_vector(n, target, cuts=(0, BANK, S)):
+            for low, high in zip(cuts, cuts[1:]):
+                cols = slice(low, high)
                 nc.vector.tensor_tensor(target[:, cols], pages[n][:, cols], rows[n][:, cols], ALU.add)
                 nc.sync.dma_start(out[n * P : (n + 1) * P, cols], target[:, cols])
 
@@ -374,8 +391,9 @@ def tile_list_core_age_slopes_kernel(tc, tab_words, tab_scales, offs, w1, w2_wor
         arg[1] = arg[2][:, BANK : 2 * BANK]
         kept = bank(0)
         w1_product(kept, 0, 0, close=True)
-        nc.scalar.activation(as_grouped(slope[0]), planes_by_sample(kept), ACT.Tanh)
-        times_step(nc.vector, f1_grouped[0], slope[0][:])
+        tanh_in_halves(slope[0], kept)
+        for cols in halves:
+            times_step(nc.vector, f1_grouped[0][:, cols], slope[0][:, cols])
         quantize_batch("f0")
         acc = bank(1)
         w1_product(acc, 1, 0, close=True)
@@ -401,7 +419,8 @@ def tile_list_core_age_slopes_kernel(tc, tab_words, tab_scales, offs, w1, w2_wor
         accs = first_slope(2, (2, 6))
         group_f1(2)
         quantize_batch("h0f2")
-        keep_a(2, accs)
+        nc.scalar.copy(arg[2][:, 2 * P : BANK], accs[0][:, 2 * P : BANK])
+        nc.scalar.copy(arg[2][:, bank_span(1)], accs[1][:])
         cast_w3(0, nc.vector.tensor_copy)
         quantize_w3(0)
         w3_grouped[1] = held([P, PACK * W3_PIECE], BF16, "f0_grouped")
@@ -409,21 +428,29 @@ def tile_list_core_age_slopes_kernel(tc, tab_words, tab_scales, offs, w1, w2_wor
         quantize_w3(1)
         target = held([P, 2 * BANK + 4 * P], F32, "target")
         place_fused(*stage((1,), (0, 1), bank(5), target[:, 7 * P // 2 : 21 * P // 2].rearrange("p (u j) -> p u j", j=P)[:, 0:7:6, :]))
-        for b, acc in enumerate(slope_product(2)):
-            second_argument(2, b, acc, target)
+        summed = bank(3)
+        w1_product(summed, 2, 0, close=False, count=1)
+        w2_product(summed, 2, 0, onto_a=True)
+        acc = bank(4)
+        w2_product(acc, 2, 1, onto_a=False)
+        nc.vector.tensor_tensor(target[:, 2 * P : BANK], summed[:, 2 * P : BANK], arg[2][:, 2 * P : BANK], ALU.add)
+        second_argument(2, 1, acc, target)
         first, width, tiles, staged = stage((1,), (2, 3, 4, 5), bank(7))
-        place(first, width, tiles[0:2], staged[:, 0:2, :], pieces(target[:, 19 * P // 2 : 23 * P // 2], 2, P))
-        place(first, width, tiles[2:4], staged[:, 2:4, :], pieces(arg[2][:], 2, P))
-        place(*stage((0,), (0, 1), bank(2), pieces(f1_grouped[3].bitcast(F32), 2, P)), pieces(arg[2][:, 3 * P : 5 * P], 2, P))
-        place(*stage((0,), (2, 3), bank(6), pieces(h_grouped[2].bitcast(F32), 2, P)), pieces(arg[2][:, 5 * P : 7 * P], 2, P))
+        place(first, width, tiles[0:1], staged[:, 0:1, :], pieces(target[:, 19 * P // 2 : 21 * P // 2], 1, P))
+        place(first, width, tiles[1:3], staged[:, 1:3, :], pieces(arg[2][:, 2 * P : BANK], 2, P))
+        place(first, width, tiles[3:4], staged[:, 3:4, :], pieces(target[:, 19 * P // 2 : 21 * P // 2], 1, P))
+        place(*stage((0,), (0, 1), bank(2), pieces(f1_grouped[3].bitcast(F32), 2, P)), pieces(arg[2][:, 4 * P : 6 * P], 2, P))
+        place(*stage((0,), (2, 3), bank(6), pieces(h_grouped[2].bitcast(F32), 2, P)), pieces(arg[2][:, 6 * P : 8 * P], 2, P))
         accs = first_slope(3, (0, 1))
-        second_slope(2, target[:, 0 : 2 * BANK])
+        nc.scalar.activation(target[:, 0 : 2 * P], summed[:, 0 : 2 * P], ACT.Tanh)
+        nc.scalar.activation(target[:, 2 * P : 2 * BANK], target[:, 2 * P : 2 * BANK], ACT.Tanh)
+        finish_h(2, target[:, 0 : 2 * BANK])
         group_f1(3)
         place_fused(*stage((0,), (4, 5), bank(5), pieces(slope[2][:], 2, P)))
         keep_a(3, accs)
-        accs = first_slope(4, (2, 6))
         quantize_batch("h2f3")
         place(*stage((2,), (0,), bank(7)))
+        accs = first_slope(4, (2, 6))
         for b, acc in enumerate(slope_product(3)):
             second_argument(3, b, acc, arg[3])
         place(*stage((2,), (1,), bank(5)))
@@ -439,9 +466,17 @@ def tile_list_core_age_slopes_kernel(tc, tab_words, tab_scales, offs, w1, w2_wor
         for b, acc in enumerate(slope_product(4)):
             second_argument(4, b, acc, target)
         place(*stage((3,), (1, 2), bank(5)))
-        second_slope(4, target[:])
         place(*stage((2,), (5,), bank(0)), pieces(arg[4][:], 1, 2 * P))
-        place(*stage((3,), (3,), bank(6)), pieces(slope[4][:], 1, 2 * P))
+        acc = bank(6)
+        first, width, tiles = project((3,), (3,), acc)
+        early = pieces(h_grouped[4].bitcast(F32), 1, P)
+        nc.scalar.copy(early, pieces(acc[:, P : 2 * P], 1, P))
+        kept = times_gains(first + P, P, tiles, early, pieces(y_tile()[:], 1, P))
+        second_slope(4, target[:])
+        late = pieces(slope[4][:], 1, P)
+        nc.scalar.copy(late, pieces(acc[:], 1, P))
+        place_fused(first, P, tiles, late)
+        scatter(*kept)
         quantize_batch("h4")
         place(*stage((3,), (4,), bank(7)), pieces(held([P, BANK], F32, "h4_grouped")[:], 1, 2 * P))
         place(*stage((4,), (0,), bank(5)))
@@ -450,12 +485,21 @@ def tile_list_core_age_slopes_kernel(tc, tab_words, tab_scales, offs, w1, w2_wor
         place(*stage((3, 4), (5,), bank(5)))
         add_on_tensor(0, 0, 4, bank(0), bank(3), rows[0])
         add_on_tensor(0, BANK, 4, bank(1), bank(4), rows[0])
+        store(nc.scalar, 0, rows[0])
         add_on_gpsimd(1, slice(0, 2 * P), rows[1])
         add_on_tensor(1, 2 * P, 4, bank(2), bank(0), rows[1])
         add_on_tensor(1, 6 * P, 2, bank(6), bank(1), rows[1])
+        store(nc.scalar, 1, rows[1])
         add_on_gpsimd(2, slice(0, 4 * P), rows[2])
+        store(nc.sync, 2, rows[2], slice(0, 4 * P))
         add_on_tensor(2, 4 * P, 4, bank(3), bank(2), rows[2])
+        store(nc.scalar, 2, rows[2], slice(4 * P, S))
         add_on_gpsimd(3, slice(0, 5 * P), rows[3])
+        store(nc.sync, 3, rows[3], slice(0, 5 * P))
         add_on_tensor(3, 5 * P, 3, bank(4), bank(6), rows[3])
-        add_on_gpsimd(4, slice(0, S), held([P, S], F32, "last_sum")[:])
+        store(nc.scalar, 3, rows[3], slice(5 * P, S))
+        last_sum = held([P, S], F32, "last_sum")[:]
+        for half in range(2):
+            add_on_gpsimd(4, bank_span(half), last_sum)
+            store(nc.sync, 4, last_sum, bank_span(half))
         add_on_vector(5, rows[4])

@@ -478,7 +478,11 @@ def tile_list_core_age_slopes_kernel(tc, tab_words, tab_scales, offs, w1, w2_wor
         place_fused(first, P, tiles, late)
         scatter(*kept)
         quantize_batch("h4")
-        place(*stage((3,), (4,), bank(7)), pieces(held([P, BANK], F32, "h4_grouped")[:], 1, 2 * P))
+        acc = bank(7)
+        first, width, tiles = project((3,), (4,), acc)
+        staged = pieces(held([P, BANK], F32, "h4_grouped")[:], 1, width)
+        nc.vector.tensor_tensor(staged[:, 0, :], acc[:, 0:width], gains[:, first : first + width], ALU.mult)
+        scatter(first, width, tiles, staged)
         place(*stage((4,), (0,), bank(5)))
         place(*stage((4,), (1, 2), bank(6)))
         place(*stage((4,), (3, 4), bank(7)))
@@ -486,10 +490,11 @@ def tile_list_core_age_slopes_kernel(tc, tab_words, tab_scales, offs, w1, w2_wor
         add_on_tensor(0, 0, 4, bank(0), bank(3), rows[0])
         add_on_tensor(0, BANK, 4, bank(1), bank(4), rows[0])
         store(nc.scalar, 0, rows[0])
-        add_on_gpsimd(1, slice(0, 2 * P), rows[1])
-        add_on_tensor(1, 2 * P, 4, bank(2), bank(0), rows[1])
-        add_on_tensor(1, 6 * P, 2, bank(6), bank(1), rows[1])
-        store(nc.scalar, 1, rows[1])
+        add_on_gpsimd(1, slice(0, 3 * P), rows[1])
+        store(nc.sync, 1, rows[1], slice(0, 3 * P))
+        add_on_tensor(1, 3 * P, 4, bank(2), bank(0), rows[1])
+        add_on_tensor(1, 7 * P, 1, bank(6), bank(1), rows[1])
+        store(nc.scalar, 1, rows[1], slice(3 * P, S))
         add_on_gpsimd(2, slice(0, 4 * P), rows[2])
         store(nc.sync, 2, rows[2], slice(0, 4 * P))
         add_on_tensor(2, 4 * P, 4, bank(3), bank(2), rows[2])

@@ -93,17 +93,16 @@ def tile_list_core_age_slopes_kernel(tc, tab_words, tab_scales, offs, w1, w2_wor
         nc.vector.tensor_copy(picked_scale[:], tab_scale[:].indirect(picks[:]))
         load_table(0)
         nc.sync.dma_start(steps[:], step.rearrange("(p t) -> p t", t=PACK))
-        nc.sync.dma_start(w2_raw[:].bitcast(I32), w2_words[0].bitcast(I32))
-        for quadrant in range(3):
+        for quadrant in range(4):
             load_w2_scales(quadrant)
         load_table(1)
-        load_w2_scales(3)
         nc.sync.dma_start(w1_raw[0][:], w1_rows[0])
         for quadrant in range(4):
             move_scales(0, quadrant)
         nc.sync.dma_start(w1_raw[1][:], w1_rows[1])
         for quadrant in range(4):
             move_scales(1, quadrant)
+        nc.sync.dma_start(w2_raw[:].bitcast(I32), w2_words[0].bitcast(I32))
         for i in w3_pieces:
             nc.sync.dma_start(w3_raw[i][:], w3_rows[:, :, i * W3_PIECE : (i + 1) * W3_PIECE])
         nc.sync.dma_start(places[:], offs2)
@@ -112,12 +111,7 @@ def tile_list_core_age_slopes_kernel(tc, tab_words, tab_scales, offs, w1, w2_wor
 
         v_codes = [held([P, S], U32, f"v_codes{a}") for a in range(2)]
         nc.vector.tensor_copy(v_codes[0][:], tab[0][:].bitcast(U32).indirect(picks[:]))
-        w2_codes = held([P, 2 * H], U8, "w2_codes")
         w2_scale = held([P, H], U8, "w2_scale")
-        nc.vector.tensor_copy(
-            w2_codes[:].rearrange("p (t m b) -> p t m b", t=PACK, b=2),
-            w2_raw[:].rearrange("p (m t b) -> p t m b", t=PACK, b=2),
-        )
         step_row = held([P, P, PACK], F32, "step_row")
         nc.vector.tensor_copy(step_row[:], steps[:].unsqueeze(1).to_broadcast([P, P, PACK]))
         nc.vector.tensor_copy(v_codes[1][:], tab[1][:].bitcast(U32).indirect(picks[:]))
@@ -146,6 +140,12 @@ def tile_list_core_age_slopes_kernel(tc, tab_words, tab_scales, offs, w1, w2_wor
             for pair in range(2):
                 cols = slice(pair * HALF, (pair + 1) * HALF)
                 quantize(w1_codes[a][:, cols], w1_scale[a][:, cols], w1_grouped[a][:, PACK * cols.start : PACK * cols.stop])
+
+        w2_codes = held([P, 2 * H], U8, "w1_grouped1")
+        nc.vector.tensor_copy(
+            w2_codes[:].rearrange("p (t m b) -> p t m b", t=PACK, b=2),
+            w2_raw[:].rearrange("p (m t b) -> p t m b", t=PACK, b=2),
+        )
 
         def woven(grouped):
             return grouped.rearrange("p (c i t) -> p c t i", i=4, t=PACK)
@@ -412,8 +412,6 @@ def tile_list_core_age_slopes_kernel(tc, tab_words, tab_scales, offs, w1, w2_wor
         nc.vector.tensor_tensor(arg[1][:], arg[1][:], slope[1][:], ALU.add)
         times_step(nc.vector, h_grouped[1], arg[1][:])
         quantize_batch("h1")
-        cast_w3(2, nc.vector.tensor_copy)
-        quantize_w3(2)
         nc.vector.tensor_tensor(arg[0][:], arg[0][:], slope[0][:], ALU.add)
         times_step(nc.vector, h_grouped[0], arg[0][:])
         accs = first_slope(2, (2, 6))
@@ -426,6 +424,8 @@ def tile_list_core_age_slopes_kernel(tc, tab_words, tab_scales, offs, w1, w2_wor
         w3_grouped[1] = held([P, PACK * W3_PIECE], BF16, "f0_grouped")
         cast_w3(1, nc.vector.tensor_copy)
         quantize_w3(1)
+        cast_w3(2, nc.vector.tensor_copy)
+        quantize_w3(2)
         target = held([P, 2 * BANK + 4 * P], F32, "target")
         place_fused(*stage((1,), (0, 1), bank(5), target[:, 7 * P // 2 : 21 * P // 2].rearrange("p (u j) -> p u j", j=P)[:, 0:7:6, :]))
         summed = bank(3)

@@ -26,10 +26,14 @@ LIST_COLUMN = 16
 ROW_TILES = N // P
 W3_PIECE = 256
 HALF = H // 2
+
 CHUNKS = [(0, 128), (128, 128), (256, 256), (512, 256), (768, 256)]
-A_BANKS, B_BANKS, Y_BANKS = 3, 2, 3
+NARROW, WIDE = 128, 256
 Y_TILES = 8
+TURNED_TILES = 3
 VECTOR_SHARE = 84
+GPSIMD_BLOCKS = {1: 4, 2: 4, 3: 5}
+BANK_BLOCKS = BANK // P
 
 
 def tile_list_core_age_slopes_kernel(tc, tab_words, tab_scales, offs, w1, w2_words, w2_scales, step, w3, offs2, wgo, x0, out):
@@ -54,23 +58,23 @@ def tile_list_core_age_slopes_kernel(tc, tab_words, tab_scales, offs, w1, w2_wor
         w2_raw = held([P, 2 * H], U8, "w2_raw")
         w2_scale_raw = held([P, H], U8, "w2_scale_raw")
         tab_scale = held([P, T], U8, "tab_scale")
-        tab = [held([P, T], I32, f"tab{a}") for a in range(2)]
-        w1_raw = [held([P, PACK, H], F32, f"w1_raw{a}") for a in range(2)]
+        tab = [held([P, T], I32, f"tab{g}") for g in range(2)]
+        w1_raw = [held([P, PACK, H], F32, f"w1_raw{g}") for g in range(2)]
         w3_pieces = range(N // W3_PIECE)
         w3_raw = [held([P, PACK, W3_PIECE], F32, f"w3_raw{i}") for i in w3_pieces]
         gains = held([P, S], F32, "gains")
         ident = held([P, P], F32, "ident")
-        v_scale = [held([P, S], U8, f"v_scale{a}") for a in range(2)]
+        v_scale = [held([P, S], U8, f"v_scale{g}") for g in range(2)]
         picked_scale = held([P, S], U8, "picked_scale")
 
         nc.vector.memset(tab_scale[QUADRANT : 2 * QUADRANT, :].bitcast(I32), 0)
         nc.vector.memset(tab_scale[2 * QUADRANT : P, :].bitcast(I32), 0)
-        for a in range(2):
-            nc.vector.memset(v_scale[a][:].bitcast(I32), 0)
+        for g in range(2):
+            nc.vector.memset(v_scale[g][:].bitcast(I32), 0)
         nc.gpsimd.memset(w2_scale_raw[:].bitcast(I32), 0)
 
-        def load_table(a):
-            nc.sync.dma_start(tab[a][:], tab_words[a].rearrange("p t i -> p (t i)").bitcast(I32))
+        def load_table(g):
+            nc.sync.dma_start(tab[g][:], tab_words[g].rearrange("p t i -> p (t i)").bitcast(I32))
 
         def load_w2_scales(quadrant):
             nc.sync.dma_start(
@@ -78,18 +82,18 @@ def tile_list_core_age_slopes_kernel(tc, tab_words, tab_scales, offs, w1, w2_wor
                 w2_scales[0, 4 * quadrant : 4 * quadrant + 4, :].bitcast(I32),
             )
 
-        def move_scales(a, quadrant):
+        def move_scales(g, quadrant):
             first = QUADRANT * quadrant
             nc.sync.dma_start(
-                v_scale[a][first : first + 4, :].bitcast(I32),
-                picked_scale[16 * a + 4 * quadrant : 16 * a + 4 * quadrant + 4, :].bitcast(I32),
+                v_scale[g][first : first + 4, :].bitcast(I32),
+                picked_scale[16 * g + 4 * quadrant : 16 * g + 4 * quadrant + 4, :].bitcast(I32),
             )
 
-        w1_rows = [w1[a * K_PASS : (a + 1) * K_PASS, :].rearrange("(p j) c -> p j c", j=PACK) for a in range(2)]
+        w1_rows = [w1[g * K_PASS : (g + 1) * K_PASS, :].rearrange("(p j) c -> p j c", j=PACK) for g in range(2)]
         w3_rows = w3.rearrange("(p j) c -> p j c", j=PACK)
 
         nc.sync.dma_start(picks[:], offs)
-        nc.sync.dma_start(tab_scale[0:QUADRANT, :].bitcast(I32), tab_scales.rearrange("a q t -> (a q) t").bitcast(I32))
+        nc.sync.dma_start(tab_scale[0:QUADRANT, :].bitcast(I32), tab_scales.rearrange("g q t -> (g q) t").bitcast(I32))
         nc.vector.tensor_copy(picked_scale[:], tab_scale[:].indirect(picks[:]))
         load_table(0)
         nc.sync.dma_start(steps[:], step.rearrange("(p t) -> p t", t=PACK))
@@ -109,11 +113,11 @@ def tile_list_core_age_slopes_kernel(tc, tab_words, tab_scales, offs, w1, w2_wor
         nc.sync.dma_start(gains[:], wgo)
         make_identity(nc, ident[:])
 
-        v_codes = [held([P, S], U32, f"v_codes{a}") for a in range(2)]
+        v_codes = [held([P, S], U32, f"v_codes{g}") for g in range(2)]
         nc.vector.tensor_copy(v_codes[0][:], tab[0][:].bitcast(U32).indirect(picks[:]))
         w2_scale = held([P, H], U8, "w2_scale")
-        step_row = held([P, P, PACK], F32, "step_row")
-        nc.vector.tensor_copy(step_row[:], steps[:].unsqueeze(1).to_broadcast([P, P, PACK]))
+        step_row = held([P, NARROW, PACK], F32, "step_row")
+        nc.vector.tensor_copy(step_row[:], steps[:].unsqueeze(1).to_broadcast([P, NARROW, PACK]))
         nc.vector.tensor_copy(v_codes[1][:], tab[1][:].bitcast(U32).indirect(picks[:]))
         nc.vector.tensor_copy(
             w2_scale[:].rearrange("p (t m) -> p t m", t=PACK),
@@ -126,25 +130,25 @@ def tile_list_core_age_slopes_kernel(tc, tab_words, tab_scales, offs, w1, w2_wor
         for n in range(ROW_TILES):
             nc.sync.dma_start(rows[n], x0[n * P : (n + 1) * P, :])
 
-        w1_codes = [held([P, H], U32, f"w1_codes{a}") for a in range(2)]
-        w1_scale = [held([P, H], U8, f"w1_scale{a}") for a in range(2)]
-        w1_grouped = [held([P, PACK * H], BF16, f"w1_grouped{a}") for a in range(2)]
+        w1_codes = [held([P, H], U32, f"w1_codes{g}") for g in range(2)]
+        w1_scale = [held([P, H], U8, f"w1_scale{g}") for g in range(2)]
+        w1_grouped = [held([P, PACK * H], BF16, f"w1_grouped{g}") for g in range(2)]
 
-        for a in range(2):
-            grouped = w1_grouped[a][:].rearrange("p (t m j) -> p m j t", t=PACK, j=PACK)
-            source = w1_raw[a][:].rearrange("p j (m t) -> p m j t", t=PACK)
+        for g in range(2):
+            grouped = w1_grouped[g][:].rearrange("p (t m j) -> p m j t", t=PACK, j=PACK)
+            source = w1_raw[g][:].rearrange("p j (m t) -> p m j t", t=PACK)
             for pair in range(2):
-                ts = slice(2 * pair, 2 * pair + 2)
-                nc.vector.tensor_copy(grouped[:, 0:VECTOR_SHARE, :, ts], source[:, 0:VECTOR_SHARE, :, ts])
-                nc.scalar.copy(grouped[:, VECTOR_SHARE:P, :, ts], source[:, VECTOR_SHARE:P, :, ts])
+                planes = slice(2 * pair, 2 * pair + 2)
+                nc.vector.tensor_copy(grouped[:, 0:VECTOR_SHARE, :, planes], source[:, 0:VECTOR_SHARE, :, planes])
+                nc.scalar.copy(grouped[:, VECTOR_SHARE:P, :, planes], source[:, VECTOR_SHARE:P, :, planes])
             for pair in range(2):
                 cols = slice(pair * HALF, (pair + 1) * HALF)
-                quantize(w1_codes[a][:, cols], w1_scale[a][:, cols], w1_grouped[a][:, PACK * cols.start : PACK * cols.stop])
+                quantize(w1_codes[g][:, cols], w1_scale[g][:, cols], w1_grouped[g][:, PACK * cols.start : PACK * cols.stop])
 
         w2_codes = held([P, 2 * H], U8, "w1_grouped1")
         nc.vector.tensor_copy(
-            w2_codes[:].rearrange("p (t m b) -> p t m b", t=PACK, b=2),
-            w2_raw[:].rearrange("p (m t b) -> p t m b", t=PACK, b=2),
+            w2_codes[:].rearrange("p (t m e) -> p t m e", t=PACK, e=2),
+            w2_raw[:].rearrange("p (m t e) -> p t m e", t=PACK, e=2),
         )
 
         def woven(grouped):
@@ -153,84 +157,85 @@ def tile_list_core_age_slopes_kernel(tc, tab_words, tab_scales, offs, w1, w2_wor
         def by_fours(planes):
             return planes.rearrange("p t (c i) -> p c t i", i=4)
 
-        def as_planes(tile):
-            return tile[:].rearrange("p (t j) -> p t j", t=PACK)
+        def as_planes(values):
+            return values.rearrange("p (t j) -> p t j", t=PACK)
 
-        def planes_by_sample(tile):
-            return tile[:].rearrange("p (t j) -> p j t", t=PACK)
+        def planes_by_sample(values):
+            return values.rearrange("p (t j) -> p j t", t=PACK)
 
-        def as_grouped(tile):
-            return tile[:].rearrange("p (j t) -> p j t", t=PACK)
+        def as_grouped(values):
+            return values.rearrange("p (j t) -> p j t", t=PACK)
+
+        def pieces(values, count, width):
+            return values[:, 0 : count * width].rearrange("p (u j) -> p u j", j=width)
+
+        def bank_span(side):
+            return slice(side * BANK, (side + 1) * BANK)
 
         w3_codes = [held([P, W3_PIECE], U32, f"w3_codes{i}") for i in w3_pieces]
         w3_scale = [held([P, W3_PIECE], U8, f"w3_scale{i}") for i in w3_pieces]
-        w3_grouped = [held([P, PACK * W3_PIECE], BF16, f"w3_grouped{i}") for i in w3_pieces]
 
-        def gpsimd_copy(dst, src):
-            nc.gpsimd.tensor_scalar(dst, src, 1.0, 0.0, ALU.mult, ALU.add)
+        def prepare_w3(i, name):
+            grouped = held([P, PACK * W3_PIECE], BF16, name)
+            nc.vector.tensor_copy(woven(grouped[:]), by_fours(w3_raw[i][:]))
+            quantize(w3_codes[i][:], w3_scale[i][:], grouped[:])
 
-        def cast_w3(i, engine_copy):
-            engine_copy(woven(w3_grouped[i][:]), by_fours(w3_raw[i][:]))
+        slope = [held([P, PACK * width], F32, f"slope{c}")[:] for c, (first, width) in enumerate(CHUNKS)]
+        kept = {c: held([P, PACK * WIDE], F32, f"kept{c}")[:] for c in (2, 3)}
+        kept[0], kept[1] = kept[2][:, bank_span(0)], kept[2][:, bank_span(1)]
 
-        def quantize_w3(i):
-            quantize(w3_codes[i][:], w3_scale[i][:], w3_grouped[i][:])
-
-        def chunk_tiles(dtype, pack, name):
-            return [held([P, pack * width], dtype, f"{name}{c}") for c, (first, width) in enumerate(CHUNKS)]
-
-        slope = chunk_tiles(F32, PACK, "slope")
-        arg = chunk_tiles(F32, PACK, "arg")
         f1_grouped, f1_codes, f1_scale, h_grouped, h_codes, h_scale = {}, {}, {}, {}, {}, {}
         batches = {}
 
-        def batch(name, members, tag=None, grouped=None):
-            width = sum(CHUNKS[c][1] for kind, c in members)
-            if grouped is None:
-                grouped = held([P, PACK * width], BF16, tag or f"{name}_grouped")[:]
+        def batch(name, h_chunk=None, f1_chunk=None):
+            members = [(h_chunk, h_grouped, h_codes, h_scale), (f1_chunk, f1_grouped, f1_codes, f1_scale)]
+            members = [member for member in members if member[0] is not None]
+            width = sum(CHUNKS[member[0]][1] for member in members)
+            grouped = held([P, PACK * width], BF16, f"{name}_grouped")
             codes = held([P, width], U32, f"{name}_codes")
             scale = held([P, width], U8, f"{name}_scale")
-            at = 0
-            for kind, c in members:
-                cols = slice(at, at + CHUNKS[c][1])
-                views = (f1_grouped, f1_codes, f1_scale) if kind == "f1" else (h_grouped, h_codes, h_scale)
-                views[0][c] = grouped[:, PACK * cols.start : PACK * cols.stop]
-                views[1][c] = codes[:, cols]
-                views[2][c] = scale[:, cols]
-                at = cols.stop
-            batches[name] = (codes, scale, grouped)
+            start = 0
+            for c, grouped_of, codes_of, scale_of in members:
+                stop = start + CHUNKS[c][1]
+                grouped_of[c] = grouped[:, PACK * start : PACK * stop]
+                codes_of[c] = codes[:, start:stop]
+                scale_of[c] = scale[:, start:stop]
+                start = stop
+            batches[name] = (codes[:], scale[:], grouped[:])
 
-        def quantize_batch(name):
-            codes, scale, grouped = batches[name]
-            quantize(codes[:], scale[:], grouped)
+        batch("f0", f1_chunk=0)
+        batch("f1", f1_chunk=1)
+        batch("h1", h_chunk=1)
+        batch("h0f2", h_chunk=0, f1_chunk=2)
+        batch("h2f3", h_chunk=2, f1_chunk=3)
+        batch("h3f4", h_chunk=3, f1_chunk=4)
+        batch("h4", h_chunk=4)
 
         pages = [held([P, S], F32, f"page{n}") for n in range(ROW_TILES)]
 
-        def bank_planes(c, b):
+        def bank_planes(c, side):
             width = CHUNKS[c][1]
             count = BANK // width
-            return [(b * count + u, slice(u * width, (u + 1) * width)) for u in range(count)]
+            return [(side * count + u, slice(u * width, (u + 1) * width)) for u in range(count)]
 
-        def bank_span(b):
-            return slice(b * BANK, (b + 1) * BANK)
-
-        def w1_product(acc, c, b, close, count=None):
+        def w1_product(acc, c, side, close, count=None):
             first, width = CHUNKS[c]
             samples = slice(first, first + width)
-            planes = bank_planes(c, b)[:count]
-            for a in range(2):
+            planes = bank_planes(c, side)[:count]
+            for g in range(2):
                 for u, (t, cols) in enumerate(planes):
                     nc.tensor.matmul_mx(
                         out=acc[:, cols],
-                        lhsT=w1_codes[a][:, t * P : (t + 1) * P].bitcast(FP8X4),
-                        lhsT_scale=w1_scale[a][:, t * P : (t + 1) * P],
-                        rhs=v_codes[a][:, samples].bitcast(FP8X4),
-                        rhs_scale=v_scale[a][:, samples],
-                        start=(a == 0 and u == 0),
-                        stop=(close and a == 1 and u == len(planes) - 1),
+                        lhsT=w1_codes[g][:, t * P : (t + 1) * P].bitcast(FP8X4),
+                        lhsT_scale=w1_scale[g][:, t * P : (t + 1) * P],
+                        rhs=v_codes[g][:, samples].bitcast(FP8X4),
+                        rhs_scale=v_scale[g][:, samples],
+                        start=(g == 0 and u == 0),
+                        stop=(close and g == 1 and u == len(planes) - 1),
                     )
 
-        def w2_product(acc, c, b, onto_a):
-            planes = bank_planes(c, b)
+        def w2_product(acc, c, side, onto_a):
+            planes = bank_planes(c, side)
             for u, (t, cols) in enumerate(planes):
                 nc.tensor.matmul_mx(
                     out=acc[:, cols],
@@ -242,68 +247,55 @@ def tile_list_core_age_slopes_kernel(tc, tab_words, tab_scales, offs, w1, w2_wor
                     stop=(not onto_a or u == len(planes) - 1),
                 )
 
-        def times_step(engine, grouped, values):
-            engine.tensor_tensor(grouped, values, step_row[:].rearrange("p j t -> p (j t)")[:, 0 : values.shape[1]], ALU.mult)
+        def times_step(grouped, values):
+            factors = step_row[:].rearrange("p j t -> p (j t)")[:, 0 : values.shape[1]]
+            nc.vector.tensor_tensor(grouped, values, factors, ALU.mult)
 
-        def tanh_in_halves(target, acc):
-            for half in range(2):
-                samples = slice(half * P // 2, (half + 1) * P // 2)
-                nc.scalar.activation(as_grouped(target)[:, samples], planes_by_sample(acc)[:, samples], ACT.Tanh)
+        def narrow_h(c):
+            nc.vector.tensor_tensor(kept[c], kept[c], slope[c], ALU.add)
+            times_step(h_grouped[c], kept[c])
 
-        halves = [slice(0, BANK // 2), slice(BANK // 2, BANK)]
-
-        def banks(c):
-            return range(PACK * CHUNKS[c][1] // BANK)
-
-        def scale_planes(tile, c, b):
-            for t, cols in bank_planes(c, b):
-                plane = as_planes(tile)[:, t, :]
+        def scale_planes(values, c, side):
+            for t, cols in bank_planes(c, side):
+                plane = as_planes(values)[:, t, :]
                 nc.scalar.activation(plane, plane, ACT.Copy, scale=steps[:, t : t + 1])
 
-        def first_slope(c, names):
-            accs = []
-            for b in banks(c):
-                acc = bank(names[b])
-                w1_product(acc, c, b, close=True)
-                nc.scalar.activation(slope[c][:, bank_span(b)], acc[:], ACT.Tanh)
-                scale_planes(slope[c], c, b)
-                accs.append(acc)
+        def wide_f1(c, bank_numbers):
+            accs = [bank(i) for i in bank_numbers]
+            for side, acc in enumerate(accs):
+                w1_product(acc, c, side, close=True)
+                nc.scalar.activation(slope[c][:, bank_span(side)], acc[:], ACT.Tanh)
+                scale_planes(slope[c], c, side)
             return accs
 
         def group_f1(c):
             nc.scalar.copy(woven(f1_grouped[c]), by_fours(as_planes(slope[c])))
 
         def keep_a(c, accs):
-            for b in banks(c):
-                nc.scalar.copy(arg[c][:, bank_span(b)], accs[b][:])
+            for side, acc in enumerate(accs):
+                nc.scalar.copy(kept[c][:, bank_span(side)], acc[:])
 
-        def slope_product(c):
-            accs = [bank(3 + b) for b in banks(c)]
-            for b, acc in enumerate(accs):
-                w2_product(acc, c, b, onto_a=False)
-            return accs
+        def add_a(c, cols, acc, target):
+            nc.vector.tensor_tensor(target[:, cols], acc, kept[c][:, cols], ALU.add)
 
-        def second_argument(c, b, acc, target):
-            nc.vector.tensor_tensor(target[:, bank_span(b)], acc[:], arg[c][:, bank_span(b)], ALU.add)
+        def wide_b(c, target):
+            accs = [bank(3), bank(4)]
+            for side, acc in enumerate(accs):
+                w2_product(acc, c, side, onto_a=False)
+            for side, acc in enumerate(accs):
+                add_a(c, bank_span(side), acc[:], target)
 
-        def second_tanh(target, b):
-            nc.scalar.activation(target[:, bank_span(b)], target[:, bank_span(b)], ACT.Tanh)
+        def wide_h(c, second_slope):
+            for side in range(2):
+                scale_planes(second_slope, c, side)
+            nc.gpsimd.tensor_tensor(woven(h_grouped[c]), by_fours(as_planes(second_slope)), by_fours(as_planes(slope[c])), ALU.add)
 
-        def finish_h(c, target):
-            for b in banks(c):
-                scale_planes(target, c, b)
-            nc.gpsimd.tensor_tensor(woven(h_grouped[c]), by_fours(as_planes(target)), by_fours(as_planes(slope[c])), ALU.add)
-
-        def second_slope(c, target):
-            for b in banks(c):
-                second_tanh(target, b)
-            finish_h(c, target)
+        def tanh_in_place(values):
+            for side in range(2):
+                nc.scalar.activation(values[:, bank_span(side)], values[:, bank_span(side)], ACT.Tanh)
 
         def y_tile():
-            return ring.tile([P, BANK], F32, name="y", tag="y", bufs=Y_TILES)
-
-        def pieces(ap, count, width):
-            return ap[:, 0 : count * width].rearrange("p (u j) -> p u j", j=width)
+            return ring.tile([P, BANK], F32, name="y", tag="y", bufs=Y_TILES)[:]
 
         def project(chunks, tiles, acc):
             first = CHUNKS[chunks[0]][0]
@@ -325,7 +317,7 @@ def tile_list_core_age_slopes_kernel(tc, tab_words, tab_scales, offs, w1, w2_wor
 
         def stage(chunks, tiles, acc, into=None):
             first, width, tiles = project(chunks, tiles, acc)
-            staged = into if into is not None else pieces(y_tile()[:], len(tiles), width)
+            staged = into if into is not None else pieces(y_tile(), len(tiles), width)
             nc.scalar.copy(staged, pieces(acc[:], len(tiles), width))
             return first, width, tiles, staged
 
@@ -352,10 +344,9 @@ def tile_list_core_age_slopes_kernel(tc, tab_words, tab_scales, offs, w1, w2_wor
         def add_on_gpsimd(n, cols, target):
             nc.gpsimd.tensor_tensor(target[:, cols], pages[n][:, cols], rows[n][:, cols], ALU.add)
 
-        def add_on_tensor(n, first, blocks, turned_acc, back_acc, target):
+        def add_on_tensor(n, first, blocks, turned_acc, back_acc):
             span = slice(0, blocks * P)
-            cols = slice(first, first + blocks * P)
-            turned = ring.tile([P, BANK], F32, name="turned", tag="turned", bufs=3)
+            turned = ring.tile([P, BANK], F32, name="turned", tag="turned", bufs=TURNED_TILES)
             for opens, source in ((True, rows[n]), (False, pages[n][:])):
                 for u in range(blocks):
                     nc.tensor.matmul(
@@ -369,142 +360,132 @@ def tile_list_core_age_slopes_kernel(tc, tab_words, tab_scales, offs, w1, w2_wor
             nc.scalar.copy(turned[:, span], turned_acc[:, span])
             for u in range(blocks):
                 nc.tensor.transpose(back_acc[:, u * P : (u + 1) * P], turned[:, u * P : (u + 1) * P], ident[:])
-            nc.scalar.copy(target[:, cols], back_acc[:, span])
+            nc.scalar.copy(rows[n][:, first : first + blocks * P], back_acc[:, span])
 
-        def store(queue, n, source, cols=slice(0, S)):
+        def store(queue, n, source, cols):
             queue.dma_start(out[n * P : (n + 1) * P, cols], source[:, cols])
 
-        def add_on_vector(n, target, cuts=(0, BANK, S)):
-            for low, high in zip(cuts, cuts[1:]):
-                cols = slice(low, high)
-                nc.vector.tensor_tensor(target[:, cols], pages[n][:, cols], rows[n][:, cols], ALU.add)
-                nc.sync.dma_start(out[n * P : (n + 1) * P, cols], target[:, cols])
-
-        batch("f0", [("f1", 0)])
-        batch("f1", [("f1", 1)])
-        batch("h1", [("h", 1)])
-        batch("h0f2", [("h", 0), ("f1", 2)])
-        batch("h2f3", [("h", 2), ("f1", 3)])
-        batch("h3f4", [("h", 3), ("f1", 4)])
-        batch("h4", [("h", 4)])
-        arg[0] = arg[2][:, 0:BANK]
-        arg[1] = arg[2][:, BANK : 2 * BANK]
-        kept = bank(0)
-        w1_product(kept, 0, 0, close=True)
-        tanh_in_halves(slope[0], kept)
-        for cols in halves:
-            times_step(nc.vector, f1_grouped[0][:, cols], slope[0][:, cols])
-        quantize_batch("f0")
+        a_of_first = bank(0)
+        w1_product(a_of_first, 0, 0, close=True)
+        for half in range(2):
+            samples = slice(half * NARROW // 2, (half + 1) * NARROW // 2)
+            nc.scalar.activation(as_grouped(slope[0])[:, samples], planes_by_sample(a_of_first[:])[:, samples], ACT.Tanh)
+        for half in range(2):
+            cols = slice(half * BANK // 2, (half + 1) * BANK // 2)
+            times_step(f1_grouped[0][:, cols], slope[0][:, cols])
+        quantize(*batches["f0"])
         acc = bank(1)
         w1_product(acc, 1, 0, close=True)
-        nc.scalar.activation(as_grouped(slope[1]), planes_by_sample(acc), ACT.Tanh)
-        nc.scalar.copy(as_grouped(arg[0]), planes_by_sample(kept))
+        nc.scalar.activation(as_grouped(slope[1]), planes_by_sample(acc[:]), ACT.Tanh)
+        nc.scalar.copy(as_grouped(kept[0]), planes_by_sample(a_of_first[:]))
         acc = bank(4)
         w2_product(acc, 0, 0, onto_a=False)
-        nc.vector.tensor_tensor(as_grouped(arg[0]), planes_by_sample(acc), as_grouped(arg[0]), ALU.add)
-        nc.scalar.activation(arg[0][:], arg[0][:], ACT.Tanh)
-        times_step(nc.vector, f1_grouped[1], slope[1][:])
-        quantize_batch("f1")
+        nc.vector.tensor_tensor(as_grouped(kept[0]), planes_by_sample(acc[:]), as_grouped(kept[0]), ALU.add)
+        nc.scalar.activation(kept[0], kept[0], ACT.Tanh)
+        times_step(f1_grouped[1], slope[1])
+        quantize(*batches["f1"])
         acc = bank(3)
         w1_product(acc, 1, 0, close=False)
         w2_product(acc, 1, 0, onto_a=True)
-        nc.scalar.activation(as_grouped(arg[1]), planes_by_sample(acc), ACT.Tanh)
-        nc.vector.tensor_tensor(arg[1][:], arg[1][:], slope[1][:], ALU.add)
-        times_step(nc.vector, h_grouped[1], arg[1][:])
-        quantize_batch("h1")
-        nc.vector.tensor_tensor(arg[0][:], arg[0][:], slope[0][:], ALU.add)
-        times_step(nc.vector, h_grouped[0], arg[0][:])
-        accs = first_slope(2, (2, 6))
+        nc.scalar.activation(as_grouped(kept[1]), planes_by_sample(acc[:]), ACT.Tanh)
+        narrow_h(1)
+        quantize(*batches["h1"])
+        narrow_h(0)
+        accs = wide_f1(2, (2, 6))
         group_f1(2)
-        quantize_batch("h0f2")
-        nc.scalar.copy(arg[2][:, 2 * P : BANK], accs[0][:, 2 * P : BANK])
-        nc.scalar.copy(arg[2][:, bank_span(1)], accs[1][:])
-        cast_w3(0, nc.vector.tensor_copy)
-        quantize_w3(0)
-        w3_grouped[1] = held([P, PACK * W3_PIECE], BF16, "f0_grouped")
-        cast_w3(1, nc.vector.tensor_copy)
-        quantize_w3(1)
-        cast_w3(2, nc.vector.tensor_copy)
-        quantize_w3(2)
-        target = held([P, 2 * BANK + 4 * P], F32, "target")
-        place_fused(*stage((1,), (0, 1), bank(5), target[:, 7 * P // 2 : 21 * P // 2].rearrange("p (u j) -> p u j", j=P)[:, 0:7:6, :]))
+        quantize(*batches["h0f2"])
+        plane_0, plane_1 = slice(0, WIDE), slice(WIDE, BANK)
+        nc.scalar.copy(kept[2][:, plane_1], accs[0][:, plane_1])
+        nc.scalar.copy(kept[2][:, bank_span(1)], accs[1][:])
+        for i, name in enumerate(("w3_grouped0", "f0_grouped", "w3_grouped2")):
+            prepare_w3(i, name)
+
+        b_tile = held([P, 2 * BANK + 4 * NARROW], F32, "b_tile")
+        b_planes = b_tile[:, 0 : 2 * BANK]
+        middle = BANK - NARROW // 2
+        spare = slice(middle + 6 * NARROW, middle + 7 * NARROW)
+        middle_and_spare = pieces(b_tile[:, middle : spare.stop], 7, NARROW)[:, 0:7:6, :]
+        place_fused(*stage((1,), (0, 1), bank(5), middle_and_spare))
         summed = bank(3)
         w1_product(summed, 2, 0, close=False, count=1)
         w2_product(summed, 2, 0, onto_a=True)
         acc = bank(4)
         w2_product(acc, 2, 1, onto_a=False)
-        nc.vector.tensor_tensor(target[:, 2 * P : BANK], summed[:, 2 * P : BANK], arg[2][:, 2 * P : BANK], ALU.add)
-        second_argument(2, 1, acc, target)
+        add_a(2, plane_1, summed[:, plane_1], b_planes)
+        add_a(2, bank_span(1), acc[:], b_planes)
         first, width, tiles, staged = stage((1,), (2, 3, 4, 5), bank(7))
-        place(first, width, tiles[0:1], staged[:, 0:1, :], pieces(target[:, 19 * P // 2 : 21 * P // 2], 1, P))
-        place(first, width, tiles[1:3], staged[:, 1:3, :], pieces(arg[2][:, 2 * P : BANK], 2, P))
-        place(first, width, tiles[3:4], staged[:, 3:4, :], pieces(target[:, 19 * P // 2 : 21 * P // 2], 1, P))
-        place(*stage((0,), (0, 1), bank(2), pieces(f1_grouped[3].bitcast(F32), 2, P)), pieces(arg[2][:, 4 * P : 6 * P], 2, P))
-        place(*stage((0,), (2, 3), bank(6), pieces(h_grouped[2].bitcast(F32), 2, P)), pieces(arg[2][:, 6 * P : 8 * P], 2, P))
-        accs = first_slope(3, (0, 1))
-        nc.scalar.activation(target[:, 0 : 2 * P], summed[:, 0 : 2 * P], ACT.Tanh)
-        nc.scalar.activation(target[:, 2 * P : 2 * BANK], target[:, 2 * P : 2 * BANK], ACT.Tanh)
-        finish_h(2, target[:, 0 : 2 * BANK])
+        place(first, width, tiles[0:1], staged[:, 0:1, :], pieces(b_tile[:, spare], 1, NARROW))
+        place(first, width, tiles[1:3], staged[:, 1:3, :], pieces(kept[2][:, plane_1], 2, NARROW))
+        place(first, width, tiles[3:4], staged[:, 3:4, :], pieces(b_tile[:, spare], 1, NARROW))
+        place(*stage((0,), (0, 1), bank(2), pieces(f1_grouped[3].bitcast(F32), 2, NARROW)), pieces(kept[2][:, 2 * WIDE : 3 * WIDE], 2, NARROW))
+        place(*stage((0,), (2, 3), bank(6), pieces(h_grouped[2].bitcast(F32), 2, NARROW)), pieces(kept[2][:, 3 * WIDE : 4 * WIDE], 2, NARROW))
+        accs = wide_f1(3, (0, 1))
+        nc.scalar.activation(b_planes[:, plane_0], summed[:, plane_0], ACT.Tanh)
+        nc.scalar.activation(b_planes[:, WIDE : 2 * BANK], b_planes[:, WIDE : 2 * BANK], ACT.Tanh)
+        wide_h(2, b_planes)
         group_f1(3)
-        place_fused(*stage((0,), (4, 5), bank(5), pieces(slope[2][:], 2, P)))
+        place_fused(*stage((0,), (4, 5), bank(5), pieces(slope[2], 2, NARROW)))
         keep_a(3, accs)
-        quantize_batch("h2f3")
+        quantize(*batches["h2f3"])
+
         place(*stage((2,), (0,), bank(7)))
-        accs = first_slope(4, (2, 6))
-        for b, acc in enumerate(slope_product(3)):
-            second_argument(3, b, acc, arg[3])
+        accs = wide_f1(4, (2, 6))
+        wide_b(3, kept[3])
         place(*stage((2,), (1,), bank(5)))
         place(*stage((2,), (2, 3), bank(0)))
-        second_slope(3, arg[3][:])
+        tanh_in_place(kept[3])
+        wide_h(3, kept[3])
         group_f1(4)
-        place_fused(*stage((2,), (4,), bank(1), pieces(slope[3][:], 1, 2 * P)))
-        arg[4] = held([P, 2 * BANK], F32, "arg2")
+        place_fused(*stage((2,), (4,), bank(1), pieces(slope[3], 1, WIDE)))
+        kept[4] = held([P, PACK * WIDE], F32, "kept2")[:]
         keep_a(4, accs)
-        quantize_batch("h3f4")
+        quantize(*batches["h3f4"])
+
         place(*stage((3,), (0,), bank(7)))
-        target = held([P, 2 * BANK], F32, "slope2")
-        for b, acc in enumerate(slope_product(4)):
-            second_argument(4, b, acc, target)
+        last_b = held([P, PACK * WIDE], F32, "slope2")[:]
+        wide_b(4, last_b)
         place(*stage((3,), (1, 2), bank(5)))
-        place(*stage((2,), (5,), bank(0)), pieces(arg[4][:], 1, 2 * P))
+        place(*stage((2,), (5,), bank(0)), pieces(kept[4], 1, WIDE))
         acc = bank(6)
         first, width, tiles = project((3,), (3,), acc)
-        early = pieces(h_grouped[4].bitcast(F32), 1, P)
-        nc.scalar.copy(early, pieces(acc[:, P : 2 * P], 1, P))
-        kept = times_gains(first + P, P, tiles, early, pieces(y_tile()[:], 1, P))
-        second_slope(4, target[:])
-        late = pieces(slope[4][:], 1, P)
-        nc.scalar.copy(late, pieces(acc[:], 1, P))
-        place_fused(first, P, tiles, late)
-        scatter(*kept)
-        quantize_batch("h4")
+        early = pieces(h_grouped[4].bitcast(F32), 1, NARROW)
+        nc.scalar.copy(early, pieces(acc[:, NARROW:WIDE], 1, NARROW))
+        second_half = times_gains(first + NARROW, NARROW, tiles, early, pieces(y_tile(), 1, NARROW))
+        tanh_in_place(last_b)
+        wide_h(4, last_b)
+        late = pieces(slope[4], 1, NARROW)
+        nc.scalar.copy(late, pieces(acc[:], 1, NARROW))
+        place_fused(first, NARROW, tiles, late)
+        scatter(*second_half)
+        quantize(*batches["h4"])
         acc = bank(7)
         first, width, tiles = project((3,), (4,), acc)
         staged = pieces(held([P, BANK], F32, "h4_grouped")[:], 1, width)
         nc.vector.tensor_tensor(staged[:, 0, :], acc[:, 0:width], gains[:, first : first + width], ALU.mult)
         scatter(first, width, tiles, staged)
+
         place(*stage((4,), (0,), bank(5)))
         place(*stage((4,), (1, 2), bank(6)))
         place(*stage((4,), (3, 4), bank(7)))
         place(*stage((3, 4), (5,), bank(5)))
-        add_on_tensor(0, 0, 4, bank(0), bank(3), rows[0])
-        add_on_tensor(0, BANK, 4, bank(1), bank(4), rows[0])
-        store(nc.scalar, 0, rows[0])
-        add_on_gpsimd(1, slice(0, 3 * P), rows[1])
-        store(nc.sync, 1, rows[1], slice(0, 3 * P))
-        add_on_tensor(1, 3 * P, 4, bank(2), bank(0), rows[1])
-        add_on_tensor(1, 7 * P, 1, bank(6), bank(1), rows[1])
-        store(nc.scalar, 1, rows[1], slice(3 * P, S))
-        add_on_gpsimd(2, slice(0, 4 * P), rows[2])
-        store(nc.sync, 2, rows[2], slice(0, 4 * P))
-        add_on_tensor(2, 4 * P, 4, bank(3), bank(2), rows[2])
-        store(nc.scalar, 2, rows[2], slice(4 * P, S))
-        add_on_gpsimd(3, slice(0, 5 * P), rows[3])
-        store(nc.sync, 3, rows[3], slice(0, 5 * P))
-        add_on_tensor(3, 5 * P, 3, bank(4), bank(6), rows[3])
-        store(nc.scalar, 3, rows[3], slice(5 * P, S))
-        last_sum = held([P, S], F32, "last_sum")[:]
-        for half in range(2):
-            add_on_gpsimd(4, bank_span(half), last_sum)
-            store(nc.sync, 4, last_sum, bank_span(half))
-        add_on_vector(5, rows[4])
+
+        bank_pairs = [(0, 3), (1, 4), (2, 0), (6, 1), (3, 2)]
+        part = 0
+        for n in range(4):
+            cut = GPSIMD_BLOCKS.get(n, 0)
+            if cut:
+                add_on_gpsimd(n, slice(0, cut * P), rows[n])
+                store(nc.sync, n, rows[n], slice(0, cut * P))
+            for block in range(cut, S // P, BANK_BLOCKS):
+                there, back = bank_pairs[part]
+                part += 1
+                add_on_tensor(n, block * P, min(BANK_BLOCKS, S // P - block), bank(there), bank(back))
+            store(nc.scalar, n, rows[n], slice(cut * P, S))
+        fifth_sum = held([P, S], F32, "fifth_sum")[:]
+        for side in range(2):
+            add_on_gpsimd(4, bank_span(side), fifth_sum)
+            store(nc.sync, 4, fifth_sum, bank_span(side))
+        for side in range(2):
+            cols = bank_span(side)
+            nc.vector.tensor_tensor(rows[4][:, cols], pages[5][:, cols], rows[5][:, cols], ALU.add)
+            store(nc.sync, 5, rows[4], cols)

@@ -424,11 +424,11 @@ def tile_list_core_age_slopes_kernel(tc, tab_words, tab_scales, offs, w1, w2_wor
         nc.scalar.activation(b_planes[:, WIDE : 2 * BANK], b_planes[:, WIDE : 2 * BANK], ACT.Tanh)
         wide_h(2, b_planes)
         group_f1(3)
-        place_fused(*stage((0,), (4, 5), bank(5), pieces(slope[2], 2, NARROW)))
+        place_fused(*stage((0,), (4, 5), bank(5), pieces(slope[2], 2, BANK)[:, :, 0:NARROW]))
         keep_a(3, accs)
         quantize(*batches["h2f3"])
 
-        place(*stage((2,), (0,), bank(7)))
+        place(*stage((2,), (0,), bank(7)), pieces(slope[2], 1, WIDE))
         accs = wide_f1(4, (2, 6))
         wide_b(3, kept[3])
         place(*stage((2,), (1,), bank(5)))

@@ -24,16 +24,15 @@ QUADRANT = 32
 BANK = 512
 LIST_COLUMN = 16
 ROW_TILES = N // P
-W3_PIECE = 256
+W3_PIECES = [(0, 128), (128, 128), (256, 256), (512, 256)]
 HALF = H // 2
 
 CHUNKS = [(0, 128), (128, 128), (256, 256), (512, 256), (768, 256)]
 NARROW, WIDE = 128, 256
 Y_TILES = 8
-TURNED_TILES = 3
+TURNED_TILES = 4
 VECTOR_SHARE = 84
-GPSIMD_BLOCKS = {1: 4, 2: 4, 3: 5}
-BANK_BLOCKS = BANK // P
+GPSIMD_COLUMNS = {2: 4 * P, 3: 5 * P}
 
 
 def tile_list_core_age_slopes_kernel(tc, tab_words, tab_scales, offs, w1, w2_words, w2_scales, step, w3, offs2, wgo, x0, out):
@@ -59,9 +58,9 @@ def tile_list_core_age_slopes_kernel(tc, tab_words, tab_scales, offs, w1, w2_wor
         w2_scale_raw = held([P, H], U8, "w2_scale_raw")
         tab_scale = held([P, T], U8, "tab_scale")
         tab = [held([P, T], I32, f"tab{g}") for g in range(2)]
-        w1_raw = [held([P, PACK, H], F32, f"w1_raw{g}") for g in range(2)]
-        w3_pieces = range(N // W3_PIECE)
-        w3_raw = [held([P, PACK, W3_PIECE], F32, f"w3_raw{i}") for i in w3_pieces]
+        w1_pieces = [(0, slice(0, PACK)), (1, slice(0, 2)), (1, slice(2, PACK))]
+        w1_raw = [held([P, js.stop - js.start, H], F32, f"w1_raw{i}") for i, (g, js) in enumerate(w1_pieces)]
+        w3_raw = [held([P, PACK, width], F32, f"w3_raw{i}") for i, (first, width) in enumerate(W3_PIECES)]
         gains = held([P, S], F32, "gains")
         ident = held([P, P], F32, "ident")
         v_scale = [held([P, S], U8, f"v_scale{g}") for g in range(2)]
@@ -103,12 +102,13 @@ def tile_list_core_age_slopes_kernel(tc, tab_words, tab_scales, offs, w1, w2_wor
         nc.sync.dma_start(w1_raw[0][:], w1_rows[0])
         for quadrant in range(4):
             move_scales(0, quadrant)
-        nc.sync.dma_start(w1_raw[1][:], w1_rows[1])
+        for i in (1, 2):
+            nc.sync.dma_start(w1_raw[i][:], w1_rows[1][:, w1_pieces[i][1], :])
+        nc.sync.dma_start(w2_raw[:].bitcast(I32), w2_words[0].bitcast(I32))
         for quadrant in range(4):
             move_scales(1, quadrant)
-        nc.sync.dma_start(w2_raw[:].bitcast(I32), w2_words[0].bitcast(I32))
-        for i in w3_pieces:
-            nc.sync.dma_start(w3_raw[i][:], w3_rows[:, :, i * W3_PIECE : (i + 1) * W3_PIECE])
+        for i, (first, width) in enumerate(W3_PIECES):
+            nc.sync.dma_start(w3_raw[i][:], w3_rows[:, :, first : first + width])
         nc.sync.dma_start(places[:], offs2)
         nc.sync.dma_start(gains[:], wgo)
         make_identity(nc, ident[:])
@@ -118,6 +118,9 @@ def tile_list_core_age_slopes_kernel(tc, tab_words, tab_scales, offs, w1, w2_wor
         w2_scale = held([P, H], U8, "w2_scale")
         step_row = held([P, NARROW, PACK], F32, "step_row")
         nc.vector.tensor_copy(step_row[:], steps[:].unsqueeze(1).to_broadcast([P, NARROW, PACK]))
+        own_steps = [held([P, NARROW, PACK], F32, f"w3_grouped{i}") for i in (2, 3)]
+        for tile in own_steps:
+            nc.vector.tensor_copy(tile[:], steps[:].unsqueeze(1).to_broadcast([P, NARROW, PACK]))
         nc.vector.tensor_copy(v_codes[1][:], tab[1][:].bitcast(U32).indirect(picks[:]))
         nc.vector.tensor_copy(
             w2_scale[:].rearrange("p (t m) -> p t m", t=PACK),
@@ -134,21 +137,21 @@ def tile_list_core_age_slopes_kernel(tc, tab_words, tab_scales, offs, w1, w2_wor
         w1_scale = [held([P, H], U8, f"w1_scale{g}") for g in range(2)]
         w1_grouped = [held([P, PACK * H], BF16, f"w1_grouped{g}") for g in range(2)]
 
-        for g in range(2):
-            grouped = w1_grouped[g][:].rearrange("p (t m j) -> p m j t", t=PACK, j=PACK)
-            source = w1_raw[g][:].rearrange("p j (m t) -> p m j t", t=PACK)
+        for (g, js), raw in zip(w1_pieces, w1_raw):
+            grouped = w1_grouped[g][:].rearrange("p (t m j) -> p m j t", t=PACK, j=PACK)[:, :, js, :]
+            source = raw[:].rearrange("p j (m t) -> p m j t", t=PACK)
             for pair in range(2):
                 planes = slice(2 * pair, 2 * pair + 2)
                 nc.vector.tensor_copy(grouped[:, 0:VECTOR_SHARE, :, planes], source[:, 0:VECTOR_SHARE, :, planes])
                 nc.scalar.copy(grouped[:, VECTOR_SHARE:P, :, planes], source[:, VECTOR_SHARE:P, :, planes])
-            for pair in range(2):
-                cols = slice(pair * HALF, (pair + 1) * HALF)
-                quantize(w1_codes[g][:, cols], w1_scale[g][:, cols], w1_grouped[g][:, PACK * cols.start : PACK * cols.stop])
+            if js.stop == PACK:
+                for cols in [slice(0, HALF), slice(HALF, H)] if g == 0 else [slice(0, H)]:
+                    quantize(w1_codes[g][:, cols], w1_scale[g][:, cols], w1_grouped[g][:, PACK * cols.start : PACK * cols.stop])
 
-        w2_codes = held([P, 2 * H], U8, "w1_grouped1")
-        nc.vector.tensor_copy(
-            w2_codes[:].rearrange("p (t m e) -> p t m e", t=PACK, e=2),
-            w2_raw[:].rearrange("p (m t e) -> p t m e", t=PACK, e=2),
+        w2_codes = held([P, 2 * H], U8, "w2_codes")
+        nc.scalar.copy(
+            w2_codes[:].bitcast(U16).rearrange("p (t m) -> p t m", t=PACK),
+            w2_raw[:].bitcast(U16).rearrange("p (m t) -> p t m", t=PACK),
         )
 
         def woven(grouped):
@@ -172,17 +175,17 @@ def tile_list_core_age_slopes_kernel(tc, tab_words, tab_scales, offs, w1, w2_wor
         def bank_span(side):
             return slice(side * BANK, (side + 1) * BANK)
 
-        w3_codes = [held([P, W3_PIECE], U32, f"w3_codes{i}") for i in w3_pieces]
-        w3_scale = [held([P, W3_PIECE], U8, f"w3_scale{i}") for i in w3_pieces]
+        w3_codes = [held([P, width], U32, f"w3_codes{i}") for i, (first, width) in enumerate(W3_PIECES)]
+        w3_scale = [held([P, width], U8, f"w3_scale{i}") for i, (first, width) in enumerate(W3_PIECES)]
 
         def prepare_w3(i, name):
-            grouped = held([P, PACK * W3_PIECE], BF16, name)
+            grouped = held([P, PACK * W3_PIECES[i][1]], BF16, name)
             nc.vector.tensor_copy(woven(grouped[:]), by_fours(w3_raw[i][:]))
             quantize(w3_codes[i][:], w3_scale[i][:], grouped[:])
 
         slope = [held([P, PACK * width], F32, f"slope{c}")[:] for c, (first, width) in enumerate(CHUNKS)]
         kept = {c: held([P, PACK * WIDE], F32, f"kept{c}")[:] for c in (2, 3)}
-        kept[0], kept[1] = kept[2][:, bank_span(0)], kept[2][:, bank_span(1)]
+        kept[0], kept[1] = (held([P, BANK], F32, f"kept{c}")[:] for c in range(2))
 
         f1_grouped, f1_codes, f1_scale, h_grouped, h_codes, h_scale = {}, {}, {}, {}, {}, {}
         batches = {}
@@ -205,8 +208,9 @@ def tile_list_core_age_slopes_kernel(tc, tab_words, tab_scales, offs, w1, w2_wor
 
         batch("f0", f1_chunk=0)
         batch("f1", f1_chunk=1)
+        batch("h0", h_chunk=0)
         batch("h1", h_chunk=1)
-        batch("h0f2", h_chunk=0, f1_chunk=2)
+        batch("f2", f1_chunk=2)
         batch("h2f3", h_chunk=2, f1_chunk=3)
         batch("h3f4", h_chunk=3, f1_chunk=4)
         batch("h4", h_chunk=4)
@@ -218,11 +222,11 @@ def tile_list_core_age_slopes_kernel(tc, tab_words, tab_scales, offs, w1, w2_wor
             count = BANK // width
             return [(side * count + u, slice(u * width, (u + 1) * width)) for u in range(count)]
 
-        def w1_product(acc, c, side, close, count=None):
+        def w1_product(acc, c, side, close, count=None, passes=(1, 0)):
             first, width = CHUNKS[c]
             samples = slice(first, first + width)
             planes = bank_planes(c, side)[:count]
-            for g in range(2):
+            for g in passes:
                 for u, (t, cols) in enumerate(planes):
                     nc.tensor.matmul_mx(
                         out=acc[:, cols],
@@ -230,8 +234,8 @@ def tile_list_core_age_slopes_kernel(tc, tab_words, tab_scales, offs, w1, w2_wor
                         lhsT_scale=w1_scale[g][:, t * P : (t + 1) * P],
                         rhs=v_codes[g][:, samples].bitcast(FP8X4),
                         rhs_scale=v_scale[g][:, samples],
-                        start=(g == 0 and u == 0),
-                        stop=(close and g == 1 and u == len(planes) - 1),
+                        start=(g == passes[0] and u == 0),
+                        stop=(close and g == passes[1] and u == len(planes) - 1),
                     )
 
         def w2_product(acc, c, side, onto_a):
@@ -247,8 +251,8 @@ def tile_list_core_age_slopes_kernel(tc, tab_words, tab_scales, offs, w1, w2_wor
                     stop=(not onto_a or u == len(planes) - 1),
                 )
 
-        def times_step(grouped, values):
-            factors = step_row[:].rearrange("p j t -> p (j t)")[:, 0 : values.shape[1]]
+        def times_step(grouped, values, row=step_row):
+            factors = row[:].rearrange("p j t -> p (j t)")[:, 0 : values.shape[1]]
             nc.vector.tensor_tensor(grouped, values, factors, ALU.mult)
 
         def narrow_h(c):
@@ -260,13 +264,16 @@ def tile_list_core_age_slopes_kernel(tc, tab_words, tab_scales, offs, w1, w2_wor
                 plane = as_planes(values)[:, t, :]
                 nc.scalar.activation(plane, plane, ACT.Copy, scale=steps[:, t : t + 1])
 
-        def wide_f1(c, bank_numbers):
+        def wide_a(c, bank_numbers, early_sides=()):
             accs = [bank(i) for i in bank_numbers]
             for side, acc in enumerate(accs):
-                w1_product(acc, c, side, close=True)
+                w1_product(acc, c, side, close=True, passes=(0, 1) if side in early_sides else (1, 0))
+            return accs
+
+        def wide_f1(c, accs):
+            for side, acc in enumerate(accs):
                 nc.scalar.activation(slope[c][:, bank_span(side)], acc[:], ACT.Tanh)
                 scale_planes(slope[c], c, side)
-            return accs
 
         def group_f1(c):
             nc.scalar.copy(woven(f1_grouped[c]), by_fours(as_planes(slope[c])))
@@ -301,7 +308,8 @@ def tile_list_core_age_slopes_kernel(tc, tab_words, tab_scales, offs, w1, w2_wor
             first = CHUNKS[chunks[0]][0]
             width = sum(CHUNKS[c][1] for c in chunks)
             for u, n in enumerate(tiles):
-                i, in_piece = divmod(n * P, W3_PIECE)
+                i = max(k for k, piece in enumerate(W3_PIECES) if piece[0] <= n * P)
+                in_piece = n * P - W3_PIECES[i][0]
                 for c in chunks:
                     column = u * width + CHUNKS[c][0] - first
                     nc.tensor.matmul_mx(
@@ -344,60 +352,80 @@ def tile_list_core_age_slopes_kernel(tc, tab_words, tab_scales, offs, w1, w2_wor
         def add_on_gpsimd(n, cols, target):
             nc.gpsimd.tensor_tensor(target[:, cols], pages[n][:, cols], rows[n][:, cols], ALU.add)
 
-        def add_on_tensor(n, first, blocks, turned_acc, back_acc):
-            span = slice(0, blocks * P)
-            turned = ring.tile([P, BANK], F32, name="turned", tag="turned", bufs=TURNED_TILES)
-            for opens, source in ((True, rows[n]), (False, pages[n][:])):
-                for u in range(blocks):
+        def blocks_of(values):
+            return [values[:, j : j + P] for j in range(0, values.shape[1], P)]
+
+        def add_turned(page, row, acc):
+            count = len(blocks_of(page))
+            turned = ring.tile([P, BANK], F32, name="turned", tag="turned", bufs=TURNED_TILES)[:, 0 : count * P]
+            for opens, source in ((True, row), (False, page)):
+                for u, block in enumerate(blocks_of(source)):
                     nc.tensor.matmul(
-                        turned_acc[:, u * P : (u + 1) * P],
-                        source[:, first + u * P : first + (u + 1) * P],
+                        acc[:, u * P : (u + 1) * P],
+                        block,
                         ident[:],
                         is_transpose=True,
                         start=(opens and u == 0),
-                        stop=(not opens and u == blocks - 1),
+                        stop=(not opens and u == count - 1),
                     )
-            nc.scalar.copy(turned[:, span], turned_acc[:, span])
-            for u in range(blocks):
-                nc.tensor.transpose(back_acc[:, u * P : (u + 1) * P], turned[:, u * P : (u + 1) * P], ident[:])
-            nc.scalar.copy(rows[n][:, first : first + blocks * P], back_acc[:, span])
+            nc.scalar.copy(turned, acc[:, 0 : count * P])
+            return turned
+
+        def turn_back(turned, acc, target):
+            for u, block in enumerate(blocks_of(turned)):
+                nc.tensor.transpose(acc[:, u * P : (u + 1) * P], block, ident[:])
+            nc.scalar.copy(target, acc[:, 0 : turned.shape[1]])
 
         def store(queue, n, source, cols):
             queue.dma_start(out[n * P : (n + 1) * P, cols], source[:, cols])
 
-        a_of_first = bank(0)
-        w1_product(a_of_first, 0, 0, close=True)
-        for half in range(2):
-            samples = slice(half * NARROW // 2, (half + 1) * NARROW // 2)
-            nc.scalar.activation(as_grouped(slope[0])[:, samples], planes_by_sample(a_of_first[:])[:, samples], ACT.Tanh)
-        for half in range(2):
-            cols = slice(half * BANK // 2, (half + 1) * BANK // 2)
-            times_step(f1_grouped[0][:, cols], slope[0][:, cols])
+        halves = [slice(half * BANK // 2, (half + 1) * BANK // 2) for half in range(2)]
+
+        def tanh_in_halves(grouped, acc):
+            for half in range(2):
+                samples = slice(half * NARROW // 2, (half + 1) * NARROW // 2)
+                nc.scalar.activation(as_grouped(grouped)[:, samples], planes_by_sample(acc[:])[:, samples], ACT.Tanh)
+
+        a_narrow = [bank(0), bank(1)]
+        for c in range(2):
+            w1_product(a_narrow[c], c, 0, close=True, passes=(0, 1))
+        accs = [bank(2), bank(6)]
+        w1_product(accs[0], 2, 0, close=True, passes=(0, 1))
+        b_first = bank(3)
+        w1_product(b_first, 0, 0, close=False)
+        w1_product(accs[1], 2, 1, close=True)
+        tanh_in_halves(slope[0], a_narrow[0])
+        times_step(f1_grouped[0][:, halves[0]], slope[0][:, halves[0]], own_steps[0])
+        times_step(f1_grouped[0][:, halves[1]], slope[0][:, halves[1]])
         quantize(*batches["f0"])
-        acc = bank(1)
-        w1_product(acc, 1, 0, close=True)
-        nc.scalar.activation(as_grouped(slope[1]), planes_by_sample(acc[:]), ACT.Tanh)
-        nc.scalar.copy(as_grouped(kept[0]), planes_by_sample(a_of_first[:]))
-        acc = bank(4)
-        w2_product(acc, 0, 0, onto_a=False)
-        nc.vector.tensor_tensor(as_grouped(kept[0]), planes_by_sample(acc[:]), as_grouped(kept[0]), ALU.add)
-        nc.scalar.activation(kept[0], kept[0], ACT.Tanh)
-        times_step(f1_grouped[1], slope[1])
+        nc.scalar.activation(as_grouped(slope[1]), planes_by_sample(a_narrow[1][:]), ACT.Tanh)
+        nc.scalar.copy(as_grouped(kept[1]), planes_by_sample(a_narrow[1][:]))
+        times_step(f1_grouped[1], slope[1], own_steps[1])
         quantize(*batches["f1"])
-        acc = bank(3)
-        w1_product(acc, 1, 0, close=False)
-        w2_product(acc, 1, 0, onto_a=True)
-        nc.scalar.activation(as_grouped(kept[1]), planes_by_sample(acc[:]), ACT.Tanh)
-        narrow_h(1)
-        quantize(*batches["h1"])
-        narrow_h(0)
-        accs = wide_f1(2, (2, 6))
-        group_f1(2)
-        quantize(*batches["h0f2"])
+        for side in range(2):
+            nc.scalar.activation(slope[2][:, bank_span(side)], accs[side][:], ACT.Tanh)
+        for t in range(PACK):
+            plane = as_planes(slope[2])[:, t, :]
+            nc.vector.tensor_scalar(plane, plane, steps[:, t : t + 1], None, ALU.mult)
+        w2_product(b_first, 0, 0, onto_a=True)
+        nc.scalar.activation(as_grouped(kept[0]), planes_by_sample(b_first[:]), ACT.Tanh)
+        acc = bank(0)
+        w2_product(acc, 1, 0, onto_a=False)
+        for cols in halves:
+            nc.vector.tensor_tensor(kept[0][:, cols], kept[0][:, cols], slope[0][:, cols], ALU.add)
+        nc.vector.tensor_tensor(as_grouped(kept[1]), planes_by_sample(acc[:]), as_grouped(kept[1]), ALU.add)
+        for cols in halves:
+            times_step(h_grouped[0][:, cols], kept[0][:, cols])
+        quantize(*batches["h0"])
         plane_0, plane_1 = slice(0, WIDE), slice(WIDE, BANK)
         nc.scalar.copy(kept[2][:, plane_1], accs[0][:, plane_1])
+        nc.scalar.activation(kept[1], kept[1], ACT.Tanh)
+        group_f1(2)
+        quantize(*batches["f2"])
+        narrow_h(1)
+        quantize(*batches["h1"])
         nc.scalar.copy(kept[2][:, bank_span(1)], accs[1][:])
-        for i, name in enumerate(("w3_grouped0", "f0_grouped", "w3_grouped2")):
+        for i, name in enumerate(("w1_grouped1", "w3_raw0", "w3_grouped2", "w3_grouped3")):
             prepare_w3(i, name)
 
         b_tile = held([P, 2 * BANK + 4 * NARROW], F32, "b_tile")
@@ -405,7 +433,7 @@ def tile_list_core_age_slopes_kernel(tc, tab_words, tab_scales, offs, w1, w2_wor
         middle = BANK - NARROW // 2
         spare = slice(middle + 6 * NARROW, middle + 7 * NARROW)
         middle_and_spare = pieces(b_tile[:, middle : spare.stop], 7, NARROW)[:, 0:7:6, :]
-        place_fused(*stage((1,), (0, 1), bank(5), middle_and_spare))
+        place_fused(*stage((0,), (0, 1), bank(5), middle_and_spare))
         summed = bank(3)
         w1_product(summed, 2, 0, close=False, count=1)
         w2_product(summed, 2, 0, onto_a=True)
@@ -413,30 +441,33 @@ def tile_list_core_age_slopes_kernel(tc, tab_words, tab_scales, offs, w1, w2_wor
         w2_product(acc, 2, 1, onto_a=False)
         add_a(2, plane_1, summed[:, plane_1], b_planes)
         add_a(2, bank_span(1), acc[:], b_planes)
-        first, width, tiles, staged = stage((1,), (2, 3, 4, 5), bank(7))
+        first, width, tiles, staged = stage((0,), (2, 3, 4, 5), bank(7))
         place(first, width, tiles[0:1], staged[:, 0:1, :], pieces(b_tile[:, spare], 1, NARROW))
         place(first, width, tiles[1:3], staged[:, 1:3, :], pieces(kept[2][:, plane_1], 2, NARROW))
         place(first, width, tiles[3:4], staged[:, 3:4, :], pieces(b_tile[:, spare], 1, NARROW))
-        place(*stage((0,), (0, 1), bank(2), pieces(f1_grouped[3].bitcast(F32), 2, NARROW)), pieces(kept[2][:, 2 * WIDE : 3 * WIDE], 2, NARROW))
-        place(*stage((0,), (2, 3), bank(6), pieces(h_grouped[2].bitcast(F32), 2, NARROW)), pieces(kept[2][:, 3 * WIDE : 4 * WIDE], 2, NARROW))
-        accs = wide_f1(3, (0, 1))
+        place(*stage((1,), (0, 1), bank(2), pieces(f1_grouped[3].bitcast(F32), 2, NARROW)), pieces(kept[2][:, 2 * WIDE : 3 * WIDE], 2, NARROW))
+        place(*stage((1,), (2, 3), bank(6), pieces(h_grouped[2].bitcast(F32), 2, NARROW)), pieces(kept[2][:, 3 * WIDE : 4 * WIDE], 2, NARROW))
         nc.scalar.activation(b_planes[:, plane_0], summed[:, plane_0], ACT.Tanh)
-        nc.scalar.activation(b_planes[:, WIDE : 2 * BANK], b_planes[:, WIDE : 2 * BANK], ACT.Tanh)
+        for cols in (plane_1, bank_span(1)):
+            nc.scalar.activation(b_planes[:, cols], b_planes[:, cols], ACT.Tanh)
         wide_h(2, b_planes)
+        accs = wide_a(3, (0, 5))
+        wide_f1(3, accs)
         group_f1(3)
-        place_fused(*stage((0,), (4, 5), bank(5), pieces(slope[2], 2, BANK)[:, :, 0:NARROW]))
         keep_a(3, accs)
+        place_fused(*stage((1,), (4, 5), bank(1), pieces(slope[2], 2, BANK)[:, :, 0:NARROW]))
         quantize(*batches["h2f3"])
 
         place(*stage((2,), (0,), bank(7)), pieces(slope[2], 1, WIDE))
-        accs = wide_f1(4, (2, 6))
+        accs = wide_a(4, (2, 6))
+        wide_f1(4, accs)
         wide_b(3, kept[3])
-        place(*stage((2,), (1,), bank(5)))
+        place(*stage((2,), (1,), bank(1)))
         place(*stage((2,), (2, 3), bank(0)))
         tanh_in_place(kept[3])
         wide_h(3, kept[3])
         group_f1(4)
-        place_fused(*stage((2,), (4,), bank(1), pieces(slope[3], 1, WIDE)))
+        place_fused(*stage((2,), (4,), bank(5), pieces(slope[3], 1, WIDE)))
         kept[4] = held([P, PACK * WIDE], F32, "kept2")[:]
         keep_a(4, accs)
         quantize(*batches["h3f4"])
@@ -444,9 +475,9 @@ def tile_list_core_age_slopes_kernel(tc, tab_words, tab_scales, offs, w1, w2_wor
         place(*stage((3,), (0,), bank(7)))
         last_b = held([P, PACK * WIDE], F32, "slope2")[:]
         wide_b(4, last_b)
-        place(*stage((3,), (1, 2), bank(5)))
+        place(*stage((3,), (1, 2), bank(6)))
         place(*stage((2,), (5,), bank(0)), pieces(kept[4], 1, WIDE))
-        acc = bank(6)
+        acc = bank(5)
         first, width, tiles = project((3,), (3,), acc)
         early = pieces(h_grouped[4].bitcast(F32), 1, NARROW)
         nc.scalar.copy(early, pieces(acc[:, NARROW:WIDE], 1, NARROW))
@@ -460,27 +491,33 @@ def tile_list_core_age_slopes_kernel(tc, tab_words, tab_scales, offs, w1, w2_wor
         quantize(*batches["h4"])
         acc = bank(7)
         first, width, tiles = project((3,), (4,), acc)
-        staged = pieces(held([P, BANK], F32, "h4_grouped")[:], 1, width)
-        nc.vector.tensor_tensor(staged[:, 0, :], acc[:, 0:width], gains[:, first : first + width], ALU.mult)
-        scatter(first, width, tiles, staged)
+        fifth_y = y_tile()[:, 0 : NARROW + WIDE]
+        nc.scalar.copy(fifth_y[:, 0:NARROW], acc[:, NARROW:WIDE])
+        staged = pieces(held([P, BANK], F32, "h4_grouped")[:], 1, NARROW)
+        nc.vector.tensor_tensor(staged[:, 0, :], acc[:, 0:NARROW], gains[:, first : first + NARROW], ALU.mult)
+        scatter(first, NARROW, tiles, staged)
 
-        place(*stage((4,), (0,), bank(5)))
-        place(*stage((4,), (1, 2), bank(6)))
-        place(*stage((4,), (3, 4), bank(7)))
-        place(*stage((3, 4), (5,), bank(5)))
+        place(*stage((4,), (0,), bank(3)))
+        place(*stage((4,), (1, 2), bank(4)))
+        place(*stage((4,), (3,), bank(5)))
+        stage((4,), (4,), bank(7), fifth_y[:, NARROW:].unsqueeze(1))
+        place(first + NARROW, NARROW + WIDE, tiles, fifth_y.unsqueeze(1))
+        place(*stage((3, 4), (5,), bank(3)))
 
-        bank_pairs = [(0, 3), (1, 4), (2, 0), (6, 1), (3, 2)]
-        part = 0
-        for n in range(4):
-            cut = GPSIMD_BLOCKS.get(n, 0)
-            if cut:
-                add_on_gpsimd(n, slice(0, cut * P), rows[n])
-                store(nc.sync, n, rows[n], slice(0, cut * P))
-            for block in range(cut, S // P, BANK_BLOCKS):
-                there, back = bank_pairs[part]
-                part += 1
-                add_on_tensor(n, block * P, min(BANK_BLOCKS, S // P - block), bank(there), bank(back))
-            store(nc.scalar, n, rows[n], slice(cut * P, S))
+        halves = [(n, bank_span(side)) for n in range(2) for side in range(2)]
+        turned = [add_turned(pages[n][:, cols], rows[n][:, cols], bank(i)) for (n, cols), i in zip(halves, (0, 1, 2, 6))]
+        for (n, cols), values, i in zip(halves, turned, (4, 3, 7, 5)):
+            turn_back(values, bank(i), rows[n][:, cols])
+            if cols.stop == S:
+                store(nc.scalar, n, rows[n], slice(0, S))
+        for n, cut in GPSIMD_COLUMNS.items():
+            add_on_gpsimd(n, slice(0, cut), rows[n])
+            store(nc.sync, n, rows[n], slice(0, cut))
+        rests = [(n, slice(cut, S)) for n, cut in GPSIMD_COLUMNS.items()]
+        turned = [add_turned(pages[n][:, cols], rows[n][:, cols], bank(i)) for (n, cols), i in zip(rests, (2, 6))]
+        for (n, cols), values, i in zip(rests, turned, (0, 1)):
+            turn_back(values, bank(i), rows[n][:, cols])
+            store(nc.scalar, n, rows[n], cols)
         fifth_sum = held([P, S], F32, "fifth_sum")[:]
         for side in range(2):
             add_on_gpsimd(4, bank_span(side), fifth_sum)

@@ -280,7 +280,8 @@ def tile_list_core_age_slopes_kernel(tc, tab_words, tab_scales, offs, w1, w2_wor
 
         def keep_a(c, accs):
             for side, acc in enumerate(accs):
-                nc.scalar.copy(kept[c][:, bank_span(side)], acc[:])
+                for t, cols in bank_planes(c, side):
+                    nc.scalar.copy(as_planes(kept[c])[:, t, :], acc[:, cols])
 
         def add_a(c, cols, acc, target):
             nc.vector.tensor_tensor(target[:, cols], acc, kept[c][:, cols], ALU.add)
@@ -459,24 +460,31 @@ def tile_list_core_age_slopes_kernel(tc, tab_words, tab_scales, offs, w1, w2_wor
         quantize(*batches["h2f3"])
 
         place(*stage((2,), (0,), bank(7)), pieces(slope[2], 1, WIDE))
-        accs = wide_a(4, (2, 6))
-        wide_f1(4, accs)
         wide_b(3, kept[3])
         place(*stage((2,), (1,), bank(1)))
         place(*stage((2,), (2, 3), bank(0)))
         tanh_in_place(kept[3])
         wide_h(3, kept[3])
+        accs = [bank(2), bank(6)]
+        for side, acc in enumerate(accs):
+            w1_product(acc, 4, side, close=True)
+            nc.scalar.activation(slope[4][:, bank_span(side)], acc[:], ACT.Tanh)
+        for t, cols in bank_planes(4, 0):
+            plane = as_planes(slope[4])[:, t, :]
+            nc.gpsimd.tensor_scalar(plane, plane, steps[:, t : t + 1], 0.0, ALU.mult, ALU.add)
+        scale_planes(slope[4], 4, 1)
         group_f1(4)
-        place_fused(*stage((2,), (4,), bank(5), pieces(slope[3], 1, WIDE)))
         kept[4] = held([P, PACK * WIDE], F32, "kept2")[:]
         keep_a(4, accs)
+        place_fused(*stage((2,), (4,), bank(5), pieces(slope[3], 1, WIDE)))
         quantize(*batches["h3f4"])
 
-        place(*stage((3,), (0,), bank(7)))
+        opening = stage((3,), (0,), bank(7))
         last_b = held([P, PACK * WIDE], F32, "slope2")[:]
         wide_b(4, last_b)
+        place(*stage((2,), (5,), bank(0)), pieces(slope[3], 1, WIDE))
+        place(*opening)
         place(*stage((3,), (1, 2), bank(6)))
-        place(*stage((2,), (5,), bank(0)), pieces(kept[4], 1, WIDE))
         acc = bank(5)
         first, width, tiles = project((3,), (3,), acc)
         early = pieces(h_grouped[4].bitcast(F32), 1, NARROW)

from contextlib import ExitStack

import concourse.mybir as mybir
from concourse.masks import make_identity

K, H, N, T, S = 1024, 512, 768, 4096, 1024
FLOPS = 2 * S * (K * H + H * H + H * N)

F32 = mybir.dt.float32
BF16 = mybir.dt.bfloat16
I32 = mybir.dt.int32
U32 = mybir.dt.uint32
U16 = mybir.dt.uint16
U8 = mybir.dt.uint8
FP8X4 = mybir.dt.float8_e4m3fn_x4
FP4X4 = mybir.dt.float4_e2m1fn_x4
ALU = mybir.AluOpType
ACT = mybir.ActivationFunctionType

P = 128
PACK = 4
K_PASS = P * PACK
QUADRANT = 32
BANK = 512
LIST_COLUMN = 16
ROW_TILES = N // P
W3_PIECES = [(0, 128), (128, 128), (256, 256), (512, 256)]
HALF = H // 2

CHUNKS = [(0, 128), (128, 128), (256, 256), (512, 256), (768, 256)]
NARROW, WIDE = 128, 256
Y_TILES = 8
TURNED_TILES = 4
VECTOR_SHARE = 84
GPSIMD_COLUMNS = {2: 4 * P, 3: 5 * P}


def tile_list_core_age_slopes_kernel(tc, tab_words, tab_scales, offs, w1, w2_words, w2_scales, step, w3, offs2, wgo, x0, out):
    nc = tc.nc
    with ExitStack() as ctx:
        keep = ctx.enter_context(tc.tile_pool(name="keep", bufs=1))
        ring = ctx.enter_context(tc.tile_pool(name="ring", bufs=1))
        psum = ctx.enter_context(tc.psum_pool(name="psum", bufs=1))

        def held(shape, dtype, name):
            return keep.tile(shape, dtype, name=name, tag=name, align_bytes=64)

        def bank(i):
            return psum.tile([P, BANK], F32, name=f"bank{i}", tag=f"bank{i}", bufs=1)

        def quantize(codes, scale, grouped):
            nc.vector.quantize_mx(out=codes.bitcast(FP8X4), scales=scale, in_=grouped)

        picks = held([P, S // LIST_COLUMN], U16, "picks")
        places = held([P, S // LIST_COLUMN], U16, "places")
        steps = held([P, PACK], F32, "steps")
        w2_raw = held([P, 2 * H], U8, "w2_raw")
        w2_scale_raw = held([P, H], U8, "w2_scale_raw")
        tab_scale = held([P, T], U8, "tab_scale")
        tab = [held([P, T], I32, f"tab{g}") for g in range(2)]
        w1_pieces = [(0, slice(0, PACK)), (1, slice(0, 2)), (1, slice(2, PACK))]
        w1_raw = [held([P, js.stop - js.start, H], F32, f"w1_raw{i}") for i, (g, js) in enumerate(w1_pieces)]
        w3_raw = [held([P, PACK, width], F32, f"w3_raw{i}") for i, (first, width) in enumerate(W3_PIECES)]
        gains = held([P, S], F32, "gains")
        ident = held([P, P], F32, "ident")
        v_scale = [held([P, S], U8, f"v_scale{g}") for g in range(2)]
        picked_scale = held([P, S], U8, "picked_scale")

        nc.vector.memset(tab_scale[QUADRANT : 2 * QUADRANT, :].bitcast(I32), 0)
        nc.vector.memset(tab_scale[2 * QUADRANT : P, :].bitcast(I32), 0)
        for g in range(2):
            nc.vector.memset(v_scale[g][:].bitcast(I32), 0)
        nc.gpsimd.memset(w2_scale_raw[:].bitcast(I32), 0)

        def load_table(g):
            nc.sync.dma_start(tab[g][:], tab_words[g].rearrange("p t i -> p (t i)").bitcast(I32))

        def load_w2_scales(quadrant):
            nc.sync.dma_start(
                w2_scale_raw[QUADRANT * quadrant : QUADRANT * quadrant + 4, :].bitcast(I32),
                w2_scales[0, 4 * quadrant : 4 * quadrant + 4, :].bitcast(I32),
            )

        def move_scales(g, quadrant):
            first = QUADRANT * quadrant
            nc.sync.dma_start(
                v_scale[g][first : first + 4, :].bitcast(I32),
                picked_scale[16 * g + 4 * quadrant : 16 * g + 4 * quadrant + 4, :].bitcast(I32),
            )

        w1_rows = [w1[g * K_PASS : (g + 1) * K_PASS, :].rearrange("(p j) c -> p j c", j=PACK) for g in range(2)]
        w3_rows = w3.rearrange("(p j) c -> p j c", j=PACK)

        nc.sync.dma_start(picks[:], offs)
        nc.sync.dma_start(tab_scale[0:QUADRANT, :].bitcast(I32), tab_scales.rearrange("g q t -> (g q) t").bitcast(I32))
        nc.vector.tensor_copy(picked_scale[:], tab_scale[:].indirect(picks[:]))
        load_table(0)
        nc.sync.dma_start(steps[:], step.rearrange("(p t) -> p t", t=PACK))
        for quadrant in range(4):
            load_w2_scales(quadrant)
        load_table(1)
        nc.sync.dma_start(w1_raw[0][:], w1_rows[0])
        for quadrant in range(4):
            move_scales(0, quadrant)
        for i in (1, 2):
            nc.sync.dma_start(w1_raw[i][:], w1_rows[1][:, w1_pieces[i][1], :])
        nc.sync.dma_start(w2_raw[:].bitcast(I32), w2_words[0].bitcast(I32))
        for quadrant in range(4):
            move_scales(1, quadrant)
        for i, (first, width) in enumerate(W3_PIECES):
            nc.sync.dma_start(w3_raw[i][:], w3_rows[:, :, first : first + width])
        nc.sync.dma_start(places[:], offs2)
        nc.sync.dma_start(gains[:], wgo)
        make_identity(nc, ident[:])

        v_codes = [held([P, S], U32, f"v_codes{g}") for g in range(2)]
        nc.vector.tensor_copy(v_codes[0][:], tab[0][:].bitcast(U32).indirect(picks[:]))
        w2_scale = held([P, H], U8, "w2_scale")
        step_row = held([P, NARROW, PACK], F32, "step_row")
        nc.vector.tensor_copy(step_row[:], steps[:].unsqueeze(1).to_broadcast([P, NARROW, PACK]))
        own_steps = [held([P, NARROW, PACK], F32, f"w3_grouped{i}") for i in (2, 3)]
        for tile in own_steps:
            nc.vector.tensor_copy(tile[:], steps[:].unsqueeze(1).to_broadcast([P, NARROW, PACK]))
        nc.vector.tensor_copy(v_codes[1][:], tab[1][:].bitcast(U32).indirect(picks[:]))
        nc.vector.tensor_copy(
            w2_scale[:].rearrange("p (t m) -> p t m", t=PACK),
            w2_scale_raw[:].rearrange("p (m t) -> p t m", t=PACK),
        )

        rows_low = held([P, 4, S], F32, "tab0")
        rows_high = held([P, 2, S], F32, "tab1")
        rows = [rows_low[:, n, :] for n in range(4)] + [rows_high[:, n, :] for n in range(2)]
        for n in range(ROW_TILES):
            nc.sync.dma_start(rows[n], x0[n * P : (n + 1) * P, :])

        w1_codes = [held([P, H], U32, f"w1_codes{g}") for g in range(2)]
        w1_scale = [held([P, H], U8, f"w1_scale{g}") for g in range(2)]
        w1_grouped = [held([P, PACK * H], BF16, f"w1_grouped{g}") for g in range(2)]

        for (g, js), raw in zip(w1_pieces, w1_raw):
            grouped = w1_grouped[g][:].rearrange("p (t m j) -> p m j t", t=PACK, j=PACK)[:, :, js, :]
            source = raw[:].rearrange("p j (m t) -> p m j t", t=PACK)
            for pair in range(2):
                planes = slice(2 * pair, 2 * pair + 2)
                nc.vector.tensor_copy(grouped[:, 0:VECTOR_SHARE, :, planes], source[:, 0:VECTOR_SHARE, :, planes])
                nc.scalar.copy(grouped[:, VECTOR_SHARE:P, :, planes], source[:, VECTOR_SHARE:P, :, planes])
            if js.stop == PACK:
                for cols in [slice(0, HALF), slice(HALF, H)] if g == 0 else [slice(0, H)]:
                    quantize(w1_codes[g][:, cols], w1_scale[g][:, cols], w1_grouped[g][:, PACK * cols.start : PACK * cols.stop])

        w2_codes = held([P, 2 * H], U8, "w2_codes")
        nc.scalar.copy(
            w2_codes[:].bitcast(U16).rearrange("p (t m) -> p t m", t=PACK),
            w2_raw[:].bitcast(U16).rearrange("p (m t) -> p t m", t=PACK),
        )

        def woven(grouped):
            return grouped.rearrange("p (c i t) -> p c t i", i=4, t=PACK)

        def by_fours(planes):
            return planes.rearrange("p t (c i) -> p c t i", i=4)

        def as_planes(values):
            return values.rearrange("p (t j) -> p t j", t=PACK)

        def planes_by_sample(values):
            return values.rearrange("p (t j) -> p j t", t=PACK)

        def as_grouped(values):
            return values.rearrange("p (j t) -> p j t", t=PACK)

        def pieces(values, count, width):
            return values[:, 0 : count * width].rearrange("p (u j) -> p u j", j=width)

        def bank_span(side):
            return slice(side * BANK, (side + 1) * BANK)

        w3_codes = [held([P, width], U32, f"w3_codes{i}") for i, (first, width) in enumerate(W3_PIECES)]
        w3_scale = [held([P, width], U8, f"w3_scale{i}") for i, (first, width) in enumerate(W3_PIECES)]

        def prepare_w3(i, name):
            grouped = held([P, PACK * W3_PIECES[i][1]], BF16, name)
            nc.vector.tensor_copy(woven(grouped[:]), by_fours(w3_raw[i][:]))
            quantize(w3_codes[i][:], w3_scale[i][:], grouped[:])

        slope = [held([P, PACK * width], F32, f"slope{c}")[:] for c, (first, width) in enumerate(CHUNKS)]
        kept = {c: held([P, PACK * WIDE], F32, f"kept{c}")[:] for c in (2, 3)}
        kept[0], kept[1] = (held([P, BANK], F32, f"kept{c}")[:] for c in range(2))

        f1_grouped, f1_codes, f1_scale, h_grouped, h_codes, h_scale = {}, {}, {}, {}, {}, {}
        batches = {}

        def batch(name, h_chunk=None, f1_chunk=None):
            members = [(h_chunk, h_grouped, h_codes, h_scale), (f1_chunk, f1_grouped, f1_codes, f1_scale)]
            members = [member for member in members if member[0] is not None]
            width = sum(CHUNKS[member[0]][1] for member in members)
            grouped = held([P, PACK * width], BF16, f"{name}_grouped")
            codes = held([P, width], U32, f"{name}_codes")
            scale = held([P, width], U8, f"{name}_scale")
            start = 0
            for c, grouped_of, codes_of, scale_of in members:
                stop = start + CHUNKS[c][1]
                grouped_of[c] = grouped[:, PACK * start : PACK * stop]
                codes_of[c] = codes[:, start:stop]
                scale_of[c] = scale[:, start:stop]
                start = stop
            batches[name] = (codes[:], scale[:], grouped[:])

        batch("f0", f1_chunk=0)
        batch("f1", f1_chunk=1)
        batch("h0", h_chunk=0)
        batch("h1", h_chunk=1)
        batch("f2", f1_chunk=2)
        batch("h2f3", h_chunk=2, f1_chunk=3)
        batch("h3f4", h_chunk=3, f1_chunk=4)
        batch("h4", h_chunk=4)

        pages = [held([P, S], F32, f"page{n}") for n in range(ROW_TILES)]

        def bank_planes(c, side):
            width = CHUNKS[c][1]
            count = BANK // width
            return [(side * count + u, slice(u * width, (u + 1) * width)) for u in range(count)]

        def w1_product(acc, c, side, close, count=None, passes=(1, 0)):
            first, width = CHUNKS[c]
            samples = slice(first, first + width)
            planes = bank_planes(c, side)[:count]
            for g in passes:
                for u, (t, cols) in enumerate(planes):
                    nc.tensor.matmul_mx(
                        out=acc[:, cols],
                        lhsT=w1_codes[g][:, t * P : (t + 1) * P].bitcast(FP8X4),
                        lhsT_scale=w1_scale[g][:, t * P : (t + 1) * P],
                        rhs=v_codes[g][:, samples].bitcast(FP8X4),
                        rhs_scale=v_scale[g][:, samples],
                        start=(g == passes[0] and u == 0),
                        stop=(close and g == passes[1] and u == len(planes) - 1),
                    )

        def w2_product(acc, c, side, onto_a):
            planes = bank_planes(c, side)
            for u, (t, cols) in enumerate(planes):
                nc.tensor.matmul_mx(
                    out=acc[:, cols],
                    lhsT=w2_codes[:, 2 * t * P : 2 * (t + 1) * P].bitcast(FP4X4),
                    lhsT_scale=w2_scale[:, t * P : (t + 1) * P],
                    rhs=f1_codes[c].bitcast(FP8X4),
                    rhs_scale=f1_scale[c],
                    start=not onto_a,
                    stop=(not onto_a or u == len(planes) - 1),
                )

        def times_step(grouped, values, row=step_row):
            factors = row[:].rearrange("p j t -> p (j t)")[:, 0 : values.shape[1]]
            nc.vector.tensor_tensor(grouped, values, factors, ALU.mult)

        def narrow_h(c):
            nc.vector.tensor_tensor(kept[c], kept[c], slope[c], ALU.add)
            times_step(h_grouped[c], kept[c])

        def scale_planes(values, c, side):
            for t, cols in bank_planes(c, side):
                plane = as_planes(values)[:, t, :]
                nc.scalar.activation(plane, plane, ACT.Copy, scale=steps[:, t : t + 1])

        def wide_a(c, bank_numbers, early_sides=()):
            accs = [bank(i) for i in bank_numbers]
            for side, acc in enumerate(accs):
                w1_product(acc, c, side, close=True, passes=(0, 1) if side in early_sides else (1, 0))
            return accs

        def wide_f1(c, accs):
            for side, acc in enumerate(accs):
                nc.scalar.activation(slope[c][:, bank_span(side)], acc[:], ACT.Tanh)
                scale_planes(slope[c], c, side)

        def group_f1(c):
            nc.scalar.copy(woven(f1_grouped[c]), by_fours(as_planes(slope[c])))

        def keep_a(c, accs):
            for side, acc in enumerate(accs):
                for t, cols in bank_planes(c, side):
                    nc.scalar.copy(as_planes(kept[c])[:, t, :], acc[:, cols])

        def add_a(c, cols, acc, target):
            nc.vector.tensor_tensor(target[:, cols], acc, kept[c][:, cols], ALU.add)

        def wide_b(c, target):
            accs = [bank(3), bank(4)]
            for side, acc in enumerate(accs):
                w2_product(acc, c, side, onto_a=False)
            for side, acc in enumerate(accs):
                add_a(c, bank_span(side), acc[:], target)

        def wide_h(c, second_slope):
            for side in range(2):
                scale_planes(second_slope, c, side)
            nc.gpsimd.tensor_tensor(woven(h_grouped[c]), by_fours(as_planes(second_slope)), by_fours(as_planes(slope[c])), ALU.add)

        def tanh_in_place(values):
            for side in range(2):
                nc.scalar.activation(values[:, bank_span(side)], values[:, bank_span(side)], ACT.Tanh)

        def y_tile():
            return ring.tile([P, BANK], F32, name="y", tag="y", bufs=Y_TILES)[:]

        def project(chunks, tiles, acc):
            first = CHUNKS[chunks[0]][0]
            width = sum(CHUNKS[c][1] for c in chunks)
            for u, n in enumerate(tiles):
                i = max(k for k, piece in enumerate(W3_PIECES) if piece[0] <= n * P)
                in_piece = n * P - W3_PIECES[i][0]
                for c in chunks:
                    column = u * width + CHUNKS[c][0] - first
                    nc.tensor.matmul_mx(
                        out=acc[:, column : column + CHUNKS[c][1]],
                        lhsT=w3_codes[i][:, in_piece : in_piece + P].bitcast(FP8X4),
                        lhsT_scale=w3_scale[i][:, in_piece : in_piece + P],
                        rhs=h_codes[c].bitcast(FP8X4),
                        rhs_scale=h_scale[c],
                        start=True,
                        stop=True,
                    )
            return first, width, tiles

        def stage(chunks, tiles, acc, into=None):
            first, width, tiles = project(chunks, tiles, acc)
            staged = into if into is not None else pieces(y_tile(), len(tiles), width)
            nc.scalar.copy(staged, pieces(acc[:], len(tiles), width))
            return first, width, tiles, staged

        def window(n, first, width):
            return pages[n][:].indirect(places[:, first // LIST_COLUMN : (first + width) // LIST_COLUMN])

        def place_fused(first, width, tiles, staged):
            for u, n in enumerate(tiles):
                nc.vector.tensor_tensor(window(n, first, width), staged[:, u, :], gains[:, first : first + width], ALU.mult)

        def times_gains(first, width, tiles, staged, into=None):
            factors = gains[:, first : first + width].unsqueeze(1).to_broadcast([P, len(tiles), width])
            into = into if into is not None else staged
            nc.gpsimd.tensor_tensor(into, staged, factors, ALU.mult)
            return first, width, tiles, into

        def scatter(first, width, tiles, staged):
            for u, n in enumerate(tiles):
                nc.vector.tensor_copy(window(n, first, width), staged[:, u, :])

        def place(first, width, tiles, staged, into=None):
            scatter(*times_gains(first, width, tiles, staged, into))

        def add_on_gpsimd(n, cols, target):
            nc.gpsimd.tensor_tensor(target[:, cols], pages[n][:, cols], rows[n][:, cols], ALU.add)

        def blocks_of(values):
            return [values[:, j : j + P] for j in range(0, values.shape[1], P)]

        def add_turned(page, row, acc):
            count = len(blocks_of(page))
            turned = ring.tile([P, BANK], F32, name="turned", tag="turned", bufs=TURNED_TILES)[:, 0 : count * P]
            for opens, source in ((True, row), (False, page)):
                for u, block in enumerate(blocks_of(source)):
                    nc.tensor.matmul(
                        acc[:, u * P : (u + 1) * P],
                        block,
                        ident[:],
                        is_transpose=True,
                        start=(opens and u == 0),
                        stop=(not opens and u == count - 1),
                    )
            nc.scalar.copy(turned, acc[:, 0 : count * P])
            return turned

        def turn_back(turned, acc, target):
            for u, block in enumerate(blocks_of(turned)):
                nc.tensor.transpose(acc[:, u * P : (u + 1) * P], block, ident[:])
            nc.scalar.copy(target, acc[:, 0 : turned.shape[1]])

        def store(queue, n, source, cols):
            queue.dma_start(out[n * P : (n + 1) * P, cols], source[:, cols])

        halves = [slice(half * BANK // 2, (half + 1) * BANK // 2) for half in range(2)]

        def tanh_in_halves(grouped, acc):
            for half in range(2):
                samples = slice(half * NARROW // 2, (half + 1) * NARROW // 2)
                nc.scalar.activation(as_grouped(grouped)[:, samples], planes_by_sample(acc[:])[:, samples], ACT.Tanh)

        a_narrow = [bank(0), bank(1)]
        for c in range(2):
            w1_product(a_narrow[c], c, 0, close=True, passes=(0, 1))
        accs = [bank(2), bank(6)]
        w1_product(accs[0], 2, 0, close=True, passes=(0, 1))
        b_first = bank(3)
        w1_product(b_first, 0, 0, close=False)
        w1_product(accs[1], 2, 1, close=True)
        tanh_in_halves(slope[0], a_narrow[0])
        times_step(f1_grouped[0][:, halves[0]], slope[0][:, halves[0]], own_steps[0])
        times_step(f1_grouped[0][:, halves[1]], slope[0][:, halves[1]])
        quantize(*batches["f0"])
        nc.scalar.activation(as_grouped(slope[1]), planes_by_sample(a_narrow[1][:]), ACT.Tanh)
        nc.scalar.copy(as_grouped(kept[1]), planes_by_sample(a_narrow[1][:]))
        times_step(f1_grouped[1], slope[1], own_steps[1])
        quantize(*batches["f1"])
        for side in range(2):
            nc.scalar.activation(slope[2][:, bank_span(side)], accs[side][:], ACT.Tanh)
        for t in range(PACK):
            plane = as_planes(slope[2])[:, t, :]
            nc.vector.tensor_scalar(plane, plane, steps[:, t : t + 1], None, ALU.mult)
        w2_product(b_first, 0, 0, onto_a=True)
        nc.scalar.activation(as_grouped(kept[0]), planes_by_sample(b_first[:]), ACT.Tanh)
        acc = bank(0)
        w2_product(acc, 1, 0, onto_a=False)
        for cols in halves:
            nc.vector.tensor_tensor(kept[0][:, cols], kept[0][:, cols], slope[0][:, cols], ALU.add)
        nc.vector.tensor_tensor(as_grouped(kept[1]), planes_by_sample(acc[:]), as_grouped(kept[1]), ALU.add)
        for cols in halves:
            times_step(h_grouped[0][:, cols], kept[0][:, cols])
        quantize(*batches["h0"])
        plane_0, plane_1 = slice(0, WIDE), slice(WIDE, BANK)
        nc.scalar.copy(kept[2][:, plane_1], accs[0][:, plane_1])
        nc.scalar.activation(kept[1], kept[1], ACT.Tanh)
        group_f1(2)
        quantize(*batches["f2"])
        narrow_h(1)
        quantize(*batches["h1"])
        nc.scalar.copy(kept[2][:, bank_span(1)], accs[1][:])
        for i, name in enumerate(("w1_grouped1", "w3_raw0", "w3_grouped2", "w3_grouped3")):
            prepare_w3(i, name)

        b_tile = held([P, 2 * BANK + 4 * NARROW], F32, "b_tile")
        b_planes = b_tile[:, 0 : 2 * BANK]
        middle = BANK - NARROW // 2
        spare = slice(middle + 6 * NARROW, middle + 7 * NARROW)
        middle_and_spare = pieces(b_tile[:, middle : spare.stop], 7, NARROW)[:, 0:7:6, :]
        place_fused(*stage((0,), (0, 1), bank(5), middle_and_spare))
        summed = bank(3)
        w1_product(summed, 2, 0, close=False, count=1)
        w2_product(summed, 2, 0, onto_a=True)
        acc = bank(4)
        w2_product(acc, 2, 1, onto_a=False)
        add_a(2, plane_1, summed[:, plane_1], b_planes)
        add_a(2, bank_span(1), acc[:], b_planes)
        first, width, tiles, staged = stage((0,), (2, 3, 4, 5), bank(7))
        place(first, width, tiles[0:1], staged[:, 0:1, :], pieces(b_tile[:, spare], 1, NARROW))
        place(first, width, tiles[1:3], staged[:, 1:3, :], pieces(kept[2][:, plane_1], 2, NARROW))
        place(first, width, tiles[3:4], staged[:, 3:4, :], pieces(b_tile[:, spare], 1, NARROW))
        place(*stage((1,), (0, 1), bank(2), pieces(f1_grouped[3].bitcast(F32), 2, NARROW)), pieces(kept[2][:, 2 * WIDE : 3 * WIDE], 2, NARROW))
        place(*stage((1,), (2, 3), bank(6), pieces(h_grouped[2].bitcast(F32), 2, NARROW)), pieces(kept[2][:, 3 * WIDE : 4 * WIDE], 2, NARROW))
        nc.scalar.activation(b_planes[:, plane_0], summed[:, plane_0], ACT.Tanh)
        for cols in (plane_1, bank_span(1)):
            nc.scalar.activation(b_planes[:, cols], b_planes[:, cols], ACT.Tanh)
        wide_h(2, b_planes)
        accs = wide_a(3, (0, 5))
        wide_f1(3, accs)
        group_f1(3)
        keep_a(3, accs)
        place_fused(*stage((1,), (4, 5), bank(1), pieces(slope[2], 2, BANK)[:, :, 0:NARROW]))
        quantize(*batches["h2f3"])

        place(*stage((2,), (0,), bank(7)), pieces(slope[2], 1, WIDE))
        wide_b(3, kept[3])
        place(*stage((2,), (1,), bank(1)))
        place(*stage((2,), (2, 3), bank(0)))
        tanh_in_place(kept[3])
        wide_h(3, kept[3])
        accs = [bank(2), bank(6)]
        for side, acc in enumerate(accs):
            w1_product(acc, 4, side, close=True)
            nc.scalar.activation(slope[4][:, bank_span(side)], acc[:], ACT.Tanh)
        for t, cols in bank_planes(4, 0):
            plane = as_planes(slope[4])[:, t, :]
            nc.gpsimd.tensor_scalar(plane, plane, steps[:, t : t + 1], 0.0, ALU.mult, ALU.add)
        scale_planes(slope[4], 4, 1)
        group_f1(4)
        kept[4] = held([P, PACK * WIDE], F32, "kept2")[:]
        keep_a(4, accs)
        place_fused(*stage((2,), (4,), bank(5), pieces(slope[3], 1, WIDE)))
        quantize(*batches["h3f4"])

        opening = stage((3,), (0,), bank(7))
        last_b = held([P, PACK * WIDE], F32, "slope2")[:]
        wide_b(4, last_b)
        place(*stage((2,), (5,), bank(0)), pieces(slope[3], 1, WIDE))
        place(*opening)
        place(*stage((3,), (1, 2), bank(6)))
        acc = bank(5)
        first, width, tiles = project((3,), (3,), acc)
        early = pieces(h_grouped[4].bitcast(F32), 1, NARROW)
        nc.scalar.copy(early, pieces(acc[:, NARROW:WIDE], 1, NARROW))
        second_half = times_gains(first + NARROW, NARROW, tiles, early, pieces(y_tile(), 1, NARROW))
        tanh_in_place(last_b)
        wide_h(4, last_b)
        late = pieces(slope[4], 1, NARROW)
        nc.scalar.copy(late, pieces(acc[:], 1, NARROW))
        place_fused(first, NARROW, tiles, late)
        scatter(*second_half)
        quantize(*batches["h4"])
        acc = bank(7)
        first, width, tiles = project((3,), (4,), acc)
        fifth_y = y_tile()[:, 0 : NARROW + WIDE]
        nc.scalar.copy(fifth_y[:, 0:NARROW], acc[:, NARROW:WIDE])
        staged = pieces(held([P, BANK], F32, "h4_grouped")[:], 1, NARROW)
        nc.vector.tensor_tensor(staged[:, 0, :], acc[:, 0:NARROW], gains[:, first : first + NARROW], ALU.mult)
        scatter(first, NARROW, tiles, staged)

        place(*stage((4,), (0,), bank(3)))
        place(*stage((4,), (1, 2), bank(4)))
        place(*stage((4,), (3,), bank(5)))
        stage((4,), (4,), bank(7), fifth_y[:, NARROW:].unsqueeze(1))
        place(first + NARROW, NARROW + WIDE, tiles, fifth_y.unsqueeze(1))
        place(*stage((3, 4), (5,), bank(3)))

        halves = [(n, bank_span(side)) for n in range(2) for side in range(2)]
        turned = [add_turned(pages[n][:, cols], rows[n][:, cols], bank(i)) for (n, cols), i in zip(halves, (0, 1, 2, 6))]
        for (n, cols), values, i in zip(halves, turned, (4, 3, 7, 5)):
            turn_back(values, bank(i), rows[n][:, cols])
            if cols.stop == S:
                store(nc.scalar, n, rows[n], slice(0, S))
        for n, cut in GPSIMD_COLUMNS.items():
            add_on_gpsimd(n, slice(0, cut), rows[n])
            store(nc.sync, n, rows[n], slice(0, cut))
        rests = [(n, slice(cut, S)) for n, cut in GPSIMD_COLUMNS.items()]
        turned = [add_turned(pages[n][:, cols], rows[n][:, cols], bank(i)) for (n, cols), i in zip(rests, (2, 6))]
        for (n, cols), values, i in zip(rests, turned, (0, 1)):
            turn_back(values, bank(i), rows[n][:, cols])
            store(nc.scalar, n, rows[n], cols)
        fifth_sum = held([P, S], F32, "fifth_sum")[:]
        for side in range(2):
            add_on_gpsimd(4, bank_span(side), fifth_sum)
            store(nc.sync, 4, fifth_sum, bank_span(side))
        for side in range(2):
            cols = bank_span(side)
            nc.vector.tensor_tensor(rows[4][:, cols], pages[5][:, cols], rows[5][:, cols], ALU.add)
            store(nc.sync, 5, rows[4], cols)
